import numpy as np, ml_dtypes
CORES = [30,158,46,174,86,214]
N = 6
BF = ml_dtypes.bfloat16
def gentries(a):
    return np.ascontiguousarray(a.reshape(8, 16, -1).transpose(0, 2, 1)).reshape(8, -1)
def gtable(e):
    e = np.asarray(e); return np.ascontiguousarray(e.reshape(8, -1, 16).transpose(0, 2, 1)).reshape(128, -1).astype(np.int32)
F, M, T, H = 640, 4, 5, 9
W = N * F
def pack(x, m, nm):
    return {"x": np.ascontiguousarray(x.reshape(128, N, F).transpose(1, 0, 2)).astype(BF), "mix": np.ascontiguousarray(m.reshape(16, N, F).transpose(1, 0, 2)).astype(BF),
            "nb": np.stack([gtable(np.ascontiguousarray(nm[:, q * F:(q + 1) * F].transpose(0, 2, 1)).reshape(8, -1)) for q in range(N)])}
def spaced(nm):
    nm = nm.astype(np.int64) % W; own = np.arange(W)[None, :]
    for j in range(M):
        for i in range(M + 1):
            clash = nm[:, :, j] == own
            for h in range(j): clash = clash | (nm[:, :, j] == nm[:, :, h])
            nm[:, :, j] = (nm[:, :, j] + clash) % W
    return nm
def links(rng):
    far = rng.integers(0, W, (8, W, M)); by = np.arange(W)[None, :, None] + rng.integers(-24, 25, (8, W, M))
    return spaced(np.where(rng.random((8, W, M)) < 0.5, far, by))
def among(rng, pool, own):
    keys = np.where(pool[None, :] == own[:, None], 2.0, rng.random((len(own), len(pool))))
    return pool[np.argsort(keys, axis=1)[:, :M]]
def setup_inputs(rng):
    form = rng.integers(0, 16, (8, 16, 24)); kind = rng.integers(0, 24, (8, W))
    x = np.clip(np.stack([form[g][:, kind[g]] for g in range(8)]) + rng.integers(-3, 4, (8, 16, W)), 0, 15)
    m = np.clip(np.add.reduce(x, axis=0) + rng.integers(-40, 41, (16, W)), 0, 120)
    return pack(x, m, links(rng))
def setup_inputs_spread(rng):
    s = 0.5 + 0.5 * rng.random((1, 1, W))
    x = np.floor(16 * s * rng.random((8, 16, W))).astype(np.int64) * (rng.random((1, 1, W)) > 0.0625)
    m = np.floor(121 * (0.6 + 0.4 * rng.random((1, W))) * rng.random((16, W))).astype(np.int64)
    c = np.floor(W * rng.random((8, W, M)) ** 3).astype(np.int64); c[1::2] = W - 1 - c[1::2]
    return pack(x, m, spaced(c))
def setup_inputs_ends(rng):
    one = np.concatenate([np.repeat(np.arange(8), F // 64), np.full(F // 8, 8), np.full(F // 32, 9), np.full(F // 8, 10)])
    one = np.concatenate([one, np.full(F - len(one), 11)])
    kind = np.concatenate([rng.permutation(one) for q in range(N)])
    kind[:60] = np.tile(np.arange(10), 6); kind[W - 60:] = np.tile(np.arange(10), 6)
    edge = np.concatenate([np.arange(60), np.arange(W - 60, W)])
    x = 15 * rng.integers(0, 2, (8, 16, W)); m = 120 * rng.integers(0, 2, (16, W))
    x[:, :, kind < 9] = 0; i = np.flatnonzero(kind < 8); x[kind[i], :, i] = 15
    m[:, kind < 8] = 120; m[:, kind == 8] = 0
    x[:, :, kind == 10] = 15; m[:, kind == 10] = 120 * rng.integers(0, 2, (1, int(np.sum(kind == 10))))
    c = np.where(rng.random((8, W, M)) < 0.5, edge[rng.integers(0, 120, (8, W, M))], rng.integers(0, W, (8, W, M)))
    c[:, :, 0] = 0; c[:, :, M - 1] = W - 1
    nm = spaced(np.take_along_axis(c, np.argsort(rng.random(c.shape), axis=-1), -1))
    full = np.flatnonzero(kind == 10); quiet = edge[kind[edge] == 8]
    for g in range(8):
        loud = edge[kind[edge] == g]
        for who, pool in ((kind == g, loud), ((kind < 9) & (kind != g), quiet), (kind == 9, loud), (kind == 10, full)):
            nm[g, who] = among(rng, pool, np.flatnonzero(who))
    return pack(x, m, nm)
def setup_inputs_corners(rng):
    own = np.arange(W)[:, None]; j = np.arange(M)[None, :]; b = own // (M + 1) * (M + 1)
    ways = [own + 1 + j, own - 1 - j, b + (own - b + 1 + j) % (M + 1), 0 * own + j, 0 * own + W - 1 - j, 0 * own + np.where(j % 2 == 0, j // 2, W - 1 - j // 2),
            np.where(j == 0, own ^ 1, own + W // 2 + 2 * j), own + F * (j + 1)]
    p = rng.permutation(8)
    c = np.stack([np.concatenate([ways[(int(p[g]) + q) % 8][q * F:(q + 1) * F] for q in range(N)]) for g in range(8)])
    z = rng.integers(4, 12, (8, 16, 1)); kind = rng.integers(0, 4, (8, 1, W)); o = np.argsort(rng.random((8, 16, W)), axis=1)
    size = np.where(kind == 0, 0, np.where(kind == 1, 2, np.where(o < np.where(kind == 2, H, H - 1), 1, 3)))
    x = z + size * (2 * rng.integers(0, 2, (8, 16, W)) - 1)
    m = np.clip(np.add.reduce(x, axis=0) + rng.choice(np.array([-24, 0, 24]), (1, W)), 0, 120)
    return pack(x, m, spaced(c))
def setup_inputs_calm(rng):
    x = rng.integers(4, 12, (8, 16, 1)) + rng.integers(0, 2, (8, 16, W))
    m = np.clip(np.add.reduce(x, axis=0) + rng.integers(-3, 4, (16, W)), 0, 120)
    return pack(x, m, links(rng))
def steps(rng, x, m, nm, kind, quiet):
    left = rng.permutation(np.flatnonzero(kind == 33)); h, h2 = [int(g) for g in rng.permutation(8)[:2]]; others = [g for g in range(8) if g != h]
    cut = np.add.accumulate(np.array([M, M, M, M, M + 1, M + 1, 7, 7, 8, 8])); who = left[:int(cut[-1]) + 8 * N]
    p1a, p1b, p2a, p2b, p3a, p3b, da, db, sa, sb, ask = np.split(who, cut)
    x[:, :, who] = 0; m[:, who] = 0
    for g in range(8): nm[g, who] = among(rng, quiet, who)
    m1 = rng.integers(20, 60, 16); m2 = rng.integers(40, 80, (16, 1)); m3 = rng.integers(40, 70, (16, 1))
    up = np.where(rng.permutation(16) < H, 1, rng.integers(-1, 1, 16))
    m[:, p1a] = m1[:, None]; m[:, p1b] = (m1 + up)[:, None]
    md = rng.integers(80, 99, (16, 7)); ms = rng.integers(104, 121, (16, 8))
    for p1, p2, p3, d, s in ((p1a, p2a, p3a, da, sa), (p1b, p2b, p3b, db, sb)):
        m[:, p2] = m2; m[:, p3] = m3; m[:, d] = md; m[:, s] = ms
        nm[h, p2] = among(rng, p1, p2); nm[h2, p3] = among(rng, p2, p3); nm[h, p3] = among(rng, p3, p3)
        nm[h, d] = among(rng, p3, d); nm[h, s] = among(rng, p3, s)
    j = int(rng.integers(0, M)); k = (j + T - 1) % M
    for i, g in enumerate(others):
        two = np.array([da[i], db[i]]); nm[g, two] = among(rng, np.flatnonzero(kind == g + 16), two); nm[g, da[i], k] = db[i]
        for n in range(8):
            two = np.array([sa[n], sb[n]]); nm[g, two] = among(rng, np.flatnonzero(kind == g + 16 * int(rng.integers(0, 2))), two); nm[g, sa[n], k] = sb[n]
        nm[g, ask[::2], j] = da[i]; nm[g, ask[1::2], j] = sa[(np.arange(len(ask[1::2])) + i) % 8]
def setup_inputs_loud(rng):
    one = np.concatenate([np.repeat(np.arange(24), F // 64), np.repeat(np.arange(24, 32), F // 20), np.full(F // 16, 32)])
    one = np.concatenate([one, np.full(F - len(one), 33)])
    kind = np.concatenate([rng.permutation(one) for q in range(N)])
    x = rng.integers(0, 16, (8, 16, W)); x[:, :, kind < 33] = 0
    i = np.flatnonzero(kind < 32); x[kind[i] % 8, :, i] = 15
    m = np.clip(np.add.reduce(x, axis=0) + rng.integers(-40, 41, (16, W)), 0, 120); m[:, kind == 32] = 0
    nm = spaced(rng.integers(0, W, (8, W, M)))
    quiet = rng.permutation(np.flatnonzero(kind == 32))[:64]
    width = rng.permutation(np.array([3, 4, 6, 8, 12, 16, 25, 25]))
    for g in range(8):
        low, mid, high, free = [np.flatnonzero(kind == g + 8 * h) for h in range(4)]
        still = np.flatnonzero((kind == 32) | ((kind < 32) & (kind % 8 != g)))
        nm[g, still] = among(rng, quiet, still)
        nm[g, free] = among(rng, free, free); nm[g, high] = among(rng, high, high); nm[g, low] = among(rng, low, low)
        nm[g, low, np.arange(len(low)) % M] = rng.choice(high, len(low))
        nm[g, mid] = among(rng, high, mid)
        half = np.argsort(rng.random((len(mid), M)), axis=1) < M // 2
        for j in range(M):
            s = mid[half[:, j]]; nm[g, s, j] = rng.choice(low[(j + T - 1) % M::M], len(s))
        c = rng.integers(98, 120, 16); step = 1 + (rng.permutation(16) < H - 1)
        m[:, low] = (c - step)[:, None]; m[:, mid] = c[:, None]; m[:, high] = (c + 1)[:, None]
        w = int(width[g]); m[:, free] = rng.integers(96, 122 - w, (16, 1)) + rng.integers(0, w, (16, len(free)))
    steps(rng, x, m, nm, kind, quiet)
    return pack(x, m, nm)
def check_ranges(d):
    bad = []
    for k, hi in (("x", 15), ("mix", 120), ("nb", W - 1)):
        v = np.asarray(d[k]).astype(np.float64)
        if not np.all((v >= 0) & (v <= hi)): bad.append("range of " + k)
        elif np.any(v != np.floor(v)): bad.append("whole numbers of " + k)
    nm = np.stack([gentries(a) for a in d["nb"]]).astype(np.int64).reshape(N, 8, M, F)
    if np.any(nm == np.arange(W).reshape(N, 1, 1, F)): bad.append("a frame names itself in nb")
    s = np.sort(nm, axis=2)
    if np.any(s[:, :, 1:] == s[:, :, :-1]): bad.append("a frame's names in nb repeat")
    return bad
def reference(x, mix, nb):
    a = np.ascontiguousarray(x.astype(np.float64).reshape(N, 8, 16, F).transpose(1, 2, 0, 3)).reshape(8, 16, W)
    m = np.ascontiguousarray(mix.astype(np.float64).transpose(1, 0, 2)).reshape(16, W)
    nm = np.stack([gentries(b) for b in nb]).astype(np.int64).reshape(N, 8, M, F)
    nm = np.ascontiguousarray(nm.transpose(1, 2, 0, 3)).reshape(8, M, W)
    own = np.arange(W)
    for t in range(T):
        v = np.stack([a[g][:, nm[g]] for g in range(8)])
        e = np.sort(np.concatenate([a[:, :, None], v], axis=2), axis=2)[:, :, M // 2]
        c = np.take_along_axis(np.roll(nm, -(t % M), axis=1), nm, 2)
        void = c == own
        for i in range(M): void = void | (c == nm[:, i:i + 1])
        for j in range(1, M): void[:, j] = void[:, j] | np.any(c[:, :j] == c[:, j:j + 1], axis=1)
        u = np.stack([a[g][:, c[g]] for g in range(8)])
        near = np.abs(u - a[:, :, None]) < np.abs(v - a[:, :, None])
        n = np.add.reduce(near.astype(np.int64), axis=1)
        nm = np.where((n >= H) & ~void, c, nm)
        if t < T - 1: a = np.maximum(e + 0.125 * (m - np.add.reduce(e, axis=0)), 0.0)
    e2 = e * e
    return {"ye": np.ascontiguousarray(e2.reshape(128, N, F).transpose(1, 0, 2)).astype(np.float32),
            "yd": np.ascontiguousarray(np.add.reduce(e2, axis=0).reshape(16, N, F).transpose(1, 0, 2)).astype(np.float32),
            "yn": np.stack([gtable(np.ascontiguousarray(nm[:, :, q * F:(q + 1) * F]).reshape(8, -1)) for q in range(N)]).astype(np.float32)}

def check_inputs(d):
    bad = list(check_ranges(d))
    if not bad:
        for name, y in reference(**d).items():
            for q in range(N):
                v = np.abs(np.asarray(y[q], np.float64)); s = np.sqrt(np.mean(v * v))
                if v.max() > 12 * s or s < 2.0 ** 4: bad.append('%s of rank %d is uneven or too small' % (name, q))
    return bad

@@ -1,0 +1,675 @@
+from concourse.bass import DstId, RemoteDMATransfer
+from concourse.mybir import AluOpType as ALU, ActivationFunctionType as AF
+
+N, F, M, R = 6, 640, 4, 5
+W = N * F
+HF, HL = F // 2, F // 32
+TILES = ((0, 128), (128, 128), (256, 64))
+XD = ["bfloat16", "bfloat16", "float32", "float32", "float32"]
+
+SCRATCH = {
+    "nbi": ("sbuf", [128, 4, 40], "int32"), "pti": ("sbuf", [128, 8, 40], "int32"), "ptb": ("sbuf", [128, 320], "bfloat16"),
+    "mixs": ("sbuf", [128, F], "bfloat16"), "wide": ("sbuf", [128, 5120], "bfloat16"),
+    "dv": ("sbuf", [128, 2560], "float32"), "adv": ("sbuf", [128, 2560], "float32"), "du": ("sbuf", [128, 1280], "float32"),
+    "tmp": ("sbuf", [128, 4 * HF], "float32"), "na": ("sbuf", [128, HF], "float32"), "pos": ("sbuf", [128, F], "float32"),
+    "xb0": ("sbuf", [128, F], "bfloat16"), "xb1": ("sbuf", [128, F], "bfloat16"), "xo": ("sbuf", [128, 2 * F], "float32"),
+    "ef": ("sbuf", [128, F], "float32"), "eb": ("sbuf", [128, F], "bfloat16"),
+    "yes": ("sbuf", [128, F], "float32"), "yds": ("sbuf", [128, F], "float32"), "yns": ("sbuf", [128, 4, 40], "float32"),
+    "nd": ("sbuf", [128, 320], "float32"), "own": ("sbuf", [128, 160], "float32"), "cs": ("sbuf", [128, 160], "float32"),
+    "cn": ("sbuf", [128, 160], "float32"), "un": ("sbuf", [128, 160], "uint16"), "uc": ("sbuf", [128, 160], "uint16"),
+    "eq": ("sbuf", [128, 1120], "bfloat16"), "nv": ("sbuf", [128, 160], "float32"), "wl": ("sbuf", [128, 160], "bfloat16"),
+    "wf": ("sbuf", [128, 192], "bfloat16"), "tf": ("sbuf", [128, 24, 16], "bfloat16"),
+    "ci": ("sbuf", [128, 128], "float32"), "cm": ("sbuf", [128, 128], "float32"), "ch": ("sbuf", [128, 72], "float32"),
+    "pi": ("sbuf", [128, 8], "int32"), "cf": ("sbuf", [128, 16], "float32"), "km": ("sbuf", [128, 16], "float32"),
+    "dm": ("sbuf", [128, 2048], "bfloat16"), "idb": ("sbuf", [128, 128], "bfloat16"), "b8": ("sbuf", [128, 128], "bfloat16"),
+    "neg": ("sbuf", [128, 128], "bfloat16"), "raw": ("sbuf", [128, 3 * HF], "bfloat16"),
+    "am": ("sbuf", [128, 128], "float32"), "ab": ("sbuf", [128, 128], "bfloat16"),
+    "gcf": ("sbuf", [128, 72], "bfloat16"), "gdf": ("sbuf", [128, 72], "bfloat16"), "gn": ("sbuf", [128, 64], "bfloat16"),
+    "ps": ("psum", [128, 4096], "float32"),
+}
+for _t in range(R):
+    SCRATCH["xt%d" % _t] = ("sbuf", [128, W], XD[_t])
+    SCRATCH["nt%d" % _t] = ("sbuf", [128, W], "bfloat16")
+
+EVENTS = [("xt0", 0, F), ("nt0", 0, F)]
+for _t in range(1, R):
+    EVENTS += [("xt%d" % _t, 0, HF), ("xt%d" % _t, HF, HF), ("nt%d" % _t, 0, HF), ("nt%d" % _t, HF, HF)]
+WAYS = ["late", "late"] + ["early", "late", "early", "late"] * (R - 1)
+GATHER, HAND, FLY = 560, 120, (3500, 3.0, 4000)
+LOOK = {"v": 60, "a": 150, "p": 150, "g": 0, "s": 0}
+SIDE_V, SIDE_U = (), (3,)
+TURNS, TRIES, ORDER = 4, 2000, []
+SEMAPHORES = ["sv", "sa", "sp", "sg", "ldx", "ldo", "ldn", "ldm", "sto", "sent"] + ["e%s_%d" % (e[0], e[1]) for e in EVENTS]
+
+
+def ones(m):
+    return bin(m).count("1")
+
+
+def routes(T, topo):
+    cores = list(T.cores)
+    best = None
+    for a in range(1, N):
+        for b in range(a + 1, N):
+            worst = 0
+            for s in range(N):
+                for part in ((a, b), [d for d in range(1, N) if d not in (a, b)]):
+                    worst = max(worst, sum(1 for d in part if not topo.same_plane(cores[s], cores[(s + d) % N])))
+            if best is None or worst < best[0]:
+                best = (worst, (a, b))
+    out = []
+    for s in range(N):
+        two = [(s + d) % N for d in best[1]]
+        three = [(s + d) % N for d in range(1, N) if d not in best[1]]
+        helper = [c for c in topo.cores_of(cores[s])
+                  if topo.die(c) != topo.die(cores[s]) and all(topo.may_write(c, cores[d]) for d in two + three)][0]
+        out.append((three, two, helper))
+    return out
+
+
+def split(route, ev):
+    three, two = route[0], route[1]
+    way = WAYS[EVENTS.index(ev)]
+    return {"own": (three + two, []), "late": (three, two), "early": (two, three)}[way]
+
+
+def transfer(T, topo, src, dsts, ev, rank, mask):
+    ap = T[ev[0]][:, rank * F + ev[1]: rank * F + ev[1] + ev[2]]
+    ids = [DstId(rid=topo.addr(d, src)[0], pnc=topo.addr(d, src)[1]) for d in dsts]
+    return RemoteDMATransfer(dst_ids=ids, dma_engine_mask=mask, remote_sem=T.sem["e%s_%d" % ev[:2]],
+                             srcs=[ap], dsts=[ap for d in dsts])
+
+
+def helper_program(g, core, T, topo, rank, route):
+    cores = list(T.cores)
+    far = topo.mask(core, cores[route[0][0]])
+    near = topo.mask(cores[rank], core) & ~topo.mask(cores[rank], cores[route[0][0]])
+    sent = 0
+    for ev in EVENTS:
+        dsts = [cores[d] for d in split(route, ev)[1]]
+        if dsts:
+            g.wait_ge(T.sem["e%s_%d" % ev[:2]], ones(near))
+            g.remote_dma_fused([transfer(T, topo, core, dsts, ev, rank, far)], local_sem=T.sem.sent)
+            sent += ones(far)
+    g.wait_ge(T.sem.sent, sent)
+
+
+def make_emitter(g, T):
+    q = {"v": g.vector, "a": g.scalar, "p": g.tensor, "g": g, "s": g.sync}
+    sem = {"v": "sv", "a": "sa", "p": "sp", "g": "sg"}
+    count = {k: 0 for k in sem}
+    known = {k: {} for k in q}
+    clock, writer, readers = {}, {}, {}
+
+    def apart(e, k):
+        return e in "pgs" or k[0] == "B" or k in ("wf", "wg", "mask") or (e == "v" and k[:2] in ("pa", "pc", "pt"))
+
+    def need(e, s, n):
+        if known[e].get(s, 0) >= n:
+            return
+        q[e].wait_ge(T.sem[s], n)
+        known[e][s] = n
+        for s2, n2 in clock.get((s, n), {}).items():
+            known[e][s2] = max(known[e].get(s2, 0), n2)
+
+    def op(e, call, r=(), w=(), dma=None, group=False):
+        deps = {}
+        mine = sem.get(e)
+        for k in r:
+            if k in writer:
+                deps[writer[k]] = 1
+        for k in w:
+            for d in readers.get(k, []) + ([writer[k]] if k in writer else []):
+                if d[0] != mine or dma or not apart(e, k):
+                    deps[d] = 1
+        if group:
+            deps = {d: 1 for d in deps if d[0] != mine}
+        top = {}
+        for s, n in deps:
+            top[s] = max(top.get(s, 0), n)
+        for s in sorted(top, key=lambda s: s == mine):
+            need(e, s, top[s])
+        ins = call(q[e])
+        if dma == "remote":
+            return
+        if dma:
+            ins.then_inc(T.sem[dma[0]], 16)
+            me = dma
+        else:
+            count[e] += 1
+            ins.then_inc(T.sem[mine], 1)
+            me = (mine, count[e])
+        clock[me] = dict(known[e])
+        for k in r:
+            readers.setdefault(k, []).append(me)
+        for k in w:
+            writer[k] = me
+            readers[k] = []
+
+    def outside(key, s, n):
+        writer[key] = (s, n)
+
+    calls = []
+
+    def note(e, call, r=(), w=(), dma=None, c=100, far=None):
+        calls.append((e, call, list(r), list(w), dma, c, far))
+
+    def arrange():
+        pre = [dict() for c in calls]
+        wr, rd, sends = {}, {}, {}
+        for i, (e, call, r, w, dma, c, far) in enumerate(calls):
+            for k in r:
+                if k in wr:
+                    pre[i][wr[k]] = max(pre[i].get(wr[k], 0), HAND)
+                if k in sends:
+                    pre[i][sends[k][0]] = sends[k][1]
+            for k in w:
+                for d in rd.get(k, []) + ([wr[k]] if k in wr else []):
+                    if d != i:
+                        pre[i][d] = max(pre[i].get(d, 0), HAND if calls[d][0] != e or not apart(e, k) else 0)
+            for k in r:
+                rd.setdefault(k, []).append(i)
+            for k in w:
+                wr[k] = i
+                rd[k] = []
+            if far:
+                sends[far[0]] = (i, far[1])
+        rest = [c[5] for c in calls]
+        post = [[] for c in calls]
+        for i in range(len(calls) - 1, -1, -1):
+            for d, lag in pre[i].items():
+                rest[d] = max(rest[d], calls[d][5] + lag + rest[i])
+                post[d].append(i)
+        back = [{i: pre[i][d] for i in post[d]} for d in range(len(calls))]
+
+        def run(before, after, rank_):
+            left = [len(p) for p in before]
+            ready = [i for i in range(len(calls)) if not left[i]]
+            at, done, free, order = [0] * len(calls), [0] * len(calls), {k: 0 for k in q}, []
+            while ready:
+                start = {i: max(at[i], free[calls[i][0]]) for i in ready}
+                first = min(ready, key=lambda i: (start[i], -rank_[i]))
+                e = calls[first][0]
+                i = max((j for j in ready if calls[j][0] == e and start[j] <= start[first] + LOOK[e]), key=lambda j: (rank_[j], -j))
+                ready.remove(i)
+                order.append(i)
+                done[i] = start[i] + calls[i][5]
+                free[e] = start[i] + (100 if calls[i][4] else calls[i][5])
+                for j in after[i]:
+                    at[j] = max(at[j], done[i] + before[j][i])
+                    left[j] -= 1
+                    if not left[j]:
+                        ready.append(j)
+            return max(done), order, done
+
+        if not ORDER:
+            best = None
+            for turn in range(TURNS):
+                span, order, done = run(pre, post, rest)
+                if best is None or span < best[0]:
+                    best = (span, order, rest)
+                rest = run(back, pre, done)[2]
+            kind = [c[0] + (c[3][-1] if c[3] else "") for c in calls]
+            kinds = sorted(set(kind))
+            seed = [12345]
+
+            def draw():
+                seed[0] = (seed[0] * 1103515245 + 12345) % 2147483648
+                return (seed[0] >> 8) / 8388608.0
+            for turn in range(TRIES):
+                shift = {k: (draw() + draw() - 1.0) * 3000 for k in kinds if draw() < 0.06}
+                rest = [x + shift.get(k, 0.0) for x, k in zip(best[2], kind)]
+                span, order, done = run(pre, post, rest)
+                if span <= best[0]:
+                    best = (span, order, rest)
+            ORDER.append(best)
+        for i in ORDER[0][1]:
+            op(*calls[i][:5])
+
+    def finish(extra):
+        arrange()
+        for e in sem:
+            need("g", sem[e], count[e])
+        for s, n in extra:
+            need("g", s, n)
+    return note, outside, finish
+
+
+def rank_program(g, core, T, topo):
+    rts = routes(T, topo)
+    rank = T.rank_of(core)
+    if rank is None:
+        for s in range(N):
+            if rts[s][2] == core:
+                helper_program(g, core, T, topo, s, rts[s])
+        return
+    cores = list(T.cores)
+    own_d, via_d, helper = rts[rank]
+    far = topo.mask(core, cores[own_d[0]])
+    near = topo.mask(core, helper) & ~far
+    op, outside, finish = make_emitter(g, T)
+    for ev in EVENTS:
+        n = 0
+        for s in range(N):
+            if rank in split(rts[s], ev)[0]:
+                n += ones(topo.mask(cores[s], core))
+            if rank in split(rts[s], ev)[1]:
+                n += ones(topo.mask(rts[s][2], core))
+        outside("far%s_%d" % ev[:2], "e%s_%d" % ev[:2], n)
+    base = rank * F
+    ps = T.ps
+    sent = [0]
+
+    def send(tab, c0):
+        ev = [e for e in EVENTS if e[0] == tab and e[1] == c0][0]
+        keys = [tab + "h%d" % h for h in range(c0 // HF, (c0 + ev[2]) // HF)]
+        mine, handed = split(rts[rank], ev)
+        tr = [transfer(T, topo, core, [cores[d] for d in mine], ev, rank, far)]
+        if handed:
+            tr.append(transfer(T, topo, core, [helper], ev, rank, near))
+        op("g", lambda e: e.remote_dma_fused(tr, local_sem=T.sem.sent), r=keys, w=["sends"], dma="remote",
+           far=("far%s_%d" % ev[:2], FLY[0] + FLY[1] * ev[2] * (4 if tab in ("xt2", "xt3", "xt4") else 2) + FLY[2] * (tab == "xt0")))
+        sent[0] += ones(far) + (ones(near) if handed else 0)
+
+    def whole(tab):
+        return [tab + "h0", tab + "h1"] + ["far%s_%d" % e[:2] for e in EVENTS if e[0] == tab]
+
+    def cyc(w):
+        k = w[-1].rstrip("0123456789_")
+        if k in ("dv", "du", "cg"):
+            return GATHER
+        if k in ("s", "pa", "pc", "e", "nr", "na", "pos", "adv", "au", "yes", "yds", "ptb", "rows") or k[:2] in ("xt", "xo", "nt"):
+            return 340
+        return {"tf": 210, "wf": 210, "z": 250, "pti": 180, "cl": 80, "b": 80, "df": 64, "cf": 64, "am": 270, "ab": 270}.get(k, 100)
+
+    def tt(out, a, b, alu, r, w):
+        op("v", lambda e: e.tensor_tensor(out, a, b, alu), r, w, c=cyc(w))
+
+    def ts(out, a, s1, s2, o0, o1, r, w):
+        if o1 is None:
+            op("v", lambda e: e.tensor_scalar(out, a, s1, None, o0), r, w, c=cyc(w))
+        else:
+            op("v", lambda e: e.tensor_scalar(out, a, s1, s2, o0, o1), r, w, c=cyc(w))
+
+    def cp(out, a, r, w):
+        op("v", lambda e: e.tensor_copy(out, a), r, w, c=cyc(w))
+
+    def act(out, a, fn, r, w, bias=0.0, scale=1.0, c=0):
+        op("a", lambda e: e.activation(out, a, fn, bias=bias, scale=scale), r, w, c=c or cyc(w))
+
+    def mm(out, l, rh, start, stop, r, w, c=0):
+        op("p", lambda e: e.matmul(out, l, rh, start, stop), r, w, c=c or cyc(w))
+
+    op("s", lambda e: e.dma_start(T.xt0[:, base:base + F], T.x[:]), w=["xt0h0", "xt0h1", "sq"], dma=("ldx", 16), c=2200)
+    op("a", lambda e: e.dma_start(T.nbi[:], T.nb[:]), w=["nbi"], dma=("ldn", 16), c=2200)
+    op("s", lambda e: e.dma_start(T.xb0[:], T.x[:]), w=["xo0h0", "xo0h1"], dma=("ldo", 16), c=2200)
+    op("s", lambda e: e.dma_start(T.mixs[0:16, :], T.mix[:]), w=["mix"], dma=("ldm", 16), c=2200)
+    fl = dict(allow_small_or_imprecise_dtypes=True)
+    op("g", lambda e: e.iota(T.pi[:, 0:1], [[0, 1]], 0, 1), w=["pi0"])
+    op("g", lambda e: e.iota(T.ci[:], [[1, 128]], 0, 0, **fl), w=["ci"])
+    op("g", lambda e: e.iota(T.own[:], [[HF, 2], [0, 4], [16, HL]], base, 1, **fl), w=["own"])
+    op("g", lambda e: e.iota(T.cm[:], [[0, 8], [1, 16]], 0, 0, **fl), w=["cm"])
+    op("g", lambda e: e.iota(T.ch[:], [[1, 36], [0, 2]], 0, 0, **fl), w=["ch"])
+    send("xt0", 0)
+    op("v", lambda e: e.memset(T.eq[:], 0.0), w=["eqz", "eq0_0"])
+    op("v", lambda e: e.memset(T.dm[:], 0.0), w=["dmz"])
+    op("v", lambda e: e.memset(T.tf[:], 0.0), w=["tf"])
+    for c, m in ((1, 112), (2, 15), (3, 1)):
+        ts(T.pi[:, c:c + 1], T.pi[:, 0:1], m, None, ALU.bitwise_and, None, ["pi0"], ["pi%d" % c])
+    cp(T.cf[:, 0:4], T.pi[:, 0:4], ["pi0", "pi1", "pi2", "pi3"], ["cf"])
+    P_, G16, K_, H_ = [T.cf[:, c:c + 1] for c in range(4)]
+    ts(T.km[:], T.ci[:, 0:16], K_, None, ALU.is_equal, None, ["ci", "cf"], ["km"])
+    ts(T.cf[:, 4:5], G16, 0.25, 3.0, ALU.mult, ALU.add, ["cf"], ["cf4"])
+    ts(T.cf[:, 5:6], G16, 0.5, H_, ALU.mult, ALU.add, ["cf"], ["cf5"])
+    ts(T.cf[:, 6:7], G16, 0.5, K_, ALU.mult, ALU.add, ["cf"], ["cf6"])
+    ts(T.cf[:, 7:8], K_, 8.0, -1.0, ALU.is_lt, ALU.mult, ["cf"], ["cf7"])
+    for r_ in range(4):
+        ts(T.cf[:, 8 + r_:9 + r_], K_, H_, 2.0 * r_, ALU.subtract, ALU.is_equal, ["cf"], ["mask"])
+    dmk = ["dm%d" % k for k in range(8)]
+    for k in range(8):
+        ts(T.dm[:, 16 * k::129], T.eq[:, 0:16], G16, 16.0 * k, ALU.add, ALU.is_equal, ["eq0_0", "cf", "dmz"], [dmk[k]])
+    ts(T.pti[:, 0::2, :], T.nbi[:], 4032, None, ALU.bitwise_and, None, ["nbi"], ["pti0"])
+    ts(T.pti[:, 1::2, :], T.nbi[:], 63, None, ALU.bitwise_and, None, ["nbi"], ["pti1"])
+    cp(T.ptb[:], T.pti[:], ["pti0", "pti1"], ["ptb"])
+    zk = []
+    for k in range(16):
+        zk.append("z%d" % k)
+        if k % 8 < 3:
+            act(T.wide[:, k::16], T.ptb[:], AF.Copy, ["ptb", "km"], [zk[-1]], scale=T.km[:, k:k + 1])
+        else:
+            ts(T.wide[:, k::16], T.ptb[:], T.km[:, k:k + 1], None, ALU.mult, None, ["ptb", "km"], [zk[-1]])
+    wide_keys = ["cg%d_%d" % (h, j) for h in range(2) for j in range(M)] + ["nr%d_%d" % (h, j) for h in range(2) for j in range(M)]
+    for h, b in ((0, 2), (1, 4)):
+        for r_ in range(8):
+            mm(ps[:, b * 512:b * 512 + HF], T.dm[:, r_ * 128:(r_ + 1) * 128], T.wide[:, r_ * F + h * HF:r_ * F + (h + 1) * HF],
+               r_ == 0, r_ == 7, zk + wide_keys + dmk, ["B%d" % b, "rows%d" % h])
+        act(T.nt0[:, base + h * HF:base + (h + 1) * HF], ps[:, b * 512:b * 512 + HF], AF.Copy, ["rows%d" % h], ["B%d" % b, "nt0h%d" % h])
+    send("nt0", 0)
+    for h in range(2):
+        cp(T.nd[:, h * 160:h * 160 + 80], T.nbi[:, :, h * HL:(h + 1) * HL], ["nbi"], ["nd%d" % h])
+        cp(T.un[:, h * 80:(h + 1) * 80], T.nbi[:, :, h * HL:(h + 1) * HL], ["nbi"], ["un%d" % h])
+    ts(T.own[:], T.own[:], G16, None, ALU.subtract, None, ["own", "cf"], ["own"])
+    ts(T.idb[:], T.ci[:], P_, None, ALU.is_equal, None, ["ci", "cf"], ["idb"])
+    ts(T.neg[:], T.ci[:], P_, -1.0, ALU.is_equal, ALU.mult, ["ci", "cf"], ["neg"])
+    ts(T.b8[:], T.cm[:], K_, 0.125, ALU.is_equal, ALU.mult, ["cm", "cf"], ["b8"])
+    ts(T.gcf[:], T.ch[:], T.cf[:, 4:5], None, ALU.is_equal, None, ["ch", "cf4"], ["gcf"])
+    ts(T.gdf[:], T.ci[:, 0:72], T.cf[:, 5:6], 6.0, ALU.subtract, ALU.is_equal, ["ci", "cf5"], ["gdf"])
+    ts(T.gn[:], T.ci[:, 0:64], T.cf[:, 6:7], T.cf[:, 7:8], ALU.is_equal, ALU.mult, ["ci", "cf6", "cf7"], ["gn"])
+    tt(T.am[:], T.idb[:], T.b8[:], ALU.subtract, ["idb", "b8"], ["am"])
+    tt(T.ab[:], T.idb[:], T.b8[:], ALU.subtract, ["idb", "b8"], ["ab"])
+
+    def xown(t, h):
+        return T["xt%d" % t][:, base + h * HF:base + (h + 1) * HF]
+
+    def xmine(t, h):
+        if t < 2:
+            return (T.xb0, T.xb1)[t][:, h * HF:(h + 1) * HF]
+        return T.xo[:, (t % 2) * F + h * HF:(t % 2) * F + (h + 1) * HF]
+
+    def blk(buf, h, j):
+        return buf[:, h * 1280 + j * HF:h * 1280 + (j + 1) * HF]
+
+    def lst(buf, h, j):
+        return buf[:, h * 80 + j * HL:h * 80 + (j + 1) * HL]
+
+    def dup(h):
+        act(T.nd[:, h * 160 + 80:h * 160 + 140], T.nd[:, h * 160:h * 160 + 60], AF.Copy, ["nd%d" % h], ["ndd%d" % h])
+
+    def side(t, off, key, h, slot, out, bk, made):
+        tab, raw = "xt%d" % t, T.raw[:, slot * HF:(slot + 1) * HF]
+        act(raw, T[tab][:].indirect(off), AF.Copy, whole(tab) + [key], ["raw%d" % slot], c=GATHER)
+        mm(out, T.neg[:], xmine(t, h), True, False, ["neg", "xo%dh%d" % (t % 2, h)], [bk, made], c=HF)
+        mm(out, T.idb[:], raw, False, True, ["idb", "raw%d" % slot], [bk, made], c=HF)
+
+    def gv(t, h, j):
+        tab = "xt%d" % t
+        if t < 2 and j in SIDE_V:
+            pa, pc, ba, bc = pslots(h)
+            out, bk, made = (pc, bc, "pc%d" % h) if j == 0 else (pa, ba, "pa%d" % h)
+            side(t, lst(T.un, h, j), "un%d" % h, h, j, out, bk, made)
+            act(blk(T.adv, h, j), out, AF.Abs, [made], [bk, "adv%d_%d" % (h, j)])
+            return
+        tt(blk(T.dv, h, j), T[tab][:].indirect(lst(T.un, h, j)), xmine(t, h), ALU.subtract,
+           whole(tab) + ["un%d" % h, "xo%dh%d" % (t % 2, h)], ["dv%d_%d" % (h, j)])
+
+    def pslots(h):
+        b = (0, 5)[h]
+        return ps[:, b * 512:b * 512 + HF], ps[:, (b + 1) * 512:(b + 1) * 512 + HF], "B%d" % b, "B%d" % (b + 1)
+
+    def prep(t, h, i):
+        pa, pc, ba, bc = pslots(h)
+        d1, src, bk = "dv%d_1" % h, blk(T.dv, h, 1), []
+        if t < 2 and 1 in SIDE_V:
+            d1, src, bk = "pa%d" % h, pa, [ba]
+        if i == 0:
+            if not (t < 2 and 0 in SIDE_V):
+                act(pc, blk(T.dv, h, 0), AF.Copy, ["dv%d_0" % h], [bc, "pc%d" % h])
+        elif i == 1:
+            act(T.na[:], src, AF.Relu, [d1], bk + ["na"], scale=-1.0)
+        elif i == 2:
+            act(T.pos[:, h * HF:(h + 1) * HF], src, AF.Relu, [d1], bk + ["pos%d" % h])
+        else:
+            act(pa, T.na[:], AF.Copy, ["na"], [ba, "pa%d" % h], scale=-1.0)
+
+    def med(t, h, i):
+        pa, pc, ba, bc = pslots(h)
+        a, c = "pa%d" % h, "pc%d" % h
+        s = [T.tmp[:, k * HF:(k + 1) * HF] for k in range(3)]
+        d2, d3 = blk(T.dv, h, 2), blk(T.dv, h, 3)
+        e_ = (T.eb if t < 2 else T.ef)[:, h * HF:(h + 1) * HF]
+        if i == 0:
+            tt(s[0], pc, d2, ALU.min, [c, "dv%d_2" % h], [bc, "s0"])
+        elif i == 1:
+            tt(pc, pc, d2, ALU.max, [c, "dv%d_2" % h], [bc, c])
+        elif i == 2:
+            tt(pa, pa, s[0], ALU.max, [a, "s0"], [ba, a])
+        elif i == 3:
+            tt(s[1], pc, T.pos[:, h * HF:(h + 1) * HF], ALU.min, [c, "pos%d" % h], [bc, "s1"])
+        elif i == 4:
+            tt(pc, pa, s[1], ALU.max, [a, "s1"], [ba, bc, c])
+        elif i == 5:
+            tt(pa, pa, s[1], ALU.min, [a, "s1"], [ba, a])
+        elif i == 6:
+            tt(s[2], pc, d3, ALU.min, [c, "dv%d_3" % h], [bc, "s2"])
+        elif i == 7 and t < R - 1:
+            tt(e_, pa, s[2], ALU.max, [a, "s2"], [ba, "e%d" % h])
+        elif i == 7:
+            tt(pa, pa, s[2], ALU.max, [a, "s2"], [ba, a])
+        elif t == R - 1:
+            tt(e_, pa, xmine(t, h), ALU.add, [a, "xo%dh%d" % (t % 2, h)], [ba, "e%d" % h])
+
+    b2 = ps[:, 2 * 512:2 * 512 + HF]
+
+    def mixin(t, h):
+        o, bk, nx = xbank(h)
+        if t < R - 1:
+            mm(ps[:, o:o + HF], T.b8[0:16, :], T.mixs[0:16, h * HF:(h + 1) * HF], True, False, ["b8", "mix"], [bk, nx], c=HF)
+            mm(ps[:, o:o + HF], (T.ab if t < 2 else T.am)[:], xmine(t, h), False, False, ["ab", "am", "xo%dh%d" % (t % 2, h)], [bk, nx],
+               c=HF * (1 if t < 2 else 4))
+
+    def xbank(h):
+        return (2 * 512, 7 * 512 + 160)[h], ("B2", "B7")[h], "nx%d" % h
+
+    def newx_p(t, h):
+        cols = slice(h * HF, (h + 1) * HF)
+        o, bk, nx = xbank(h)
+        if t < R - 1:
+            mm(ps[:, o:o + HF], (T.ab if t < 2 else T.am)[:], (T.eb if t < 2 else T.ef)[:, cols], False, True, ["ab", "am", "e%d" % h],
+               [bk, nx], c=HF * (1 if t < 2 else 4))
+        else:
+            act(T.yes[:, cols], T.ef[:, cols], AF.Square, ["e%d" % h], ["yes%d" % h])
+            mm(ps[0:16, o:o + HF], T.km[:], T.yes[:, cols], True, True, ["km", "yes%d" % h], [bk, nx], c=4 * HF)
+
+    def newx_a(t, h):
+        cols = slice(h * HF, (h + 1) * HF)
+        o, bk, nx = xbank(h)
+        if t < R - 1:
+            act(xown(t + 1, h), ps[:, o:o + HF], AF.Relu, [nx], [bk, "xt%dh%d" % (t + 1, h)])
+            send("xt%d" % (t + 1), h * HF)
+            act(xmine(t + 1, h), ps[:, o:o + HF], AF.Relu, [nx], [bk, "xo%dh%d" % ((t + 1) % 2, h)])
+        else:
+            act(T.yds[0:16, cols], ps[0:16, o:o + HF], AF.Copy, [nx], [bk, "yds%d" % h])
+            if h == 1:
+                op("s", lambda e: e.dma_start(T.ye[:], T.yes[:]), r=["yes0", "yes1"], dma=("sto", 16))
+                op("s", lambda e: e.dma_start(T.yd[:], T.yds[0:16, :]), r=["yds0", "yds1"], dma=("sto", 32))
+
+    def absv(t, h, j):
+        if t < 2 and j in SIDE_V:
+            return
+        act(blk(T.adv, h, j), blk(T.dv, h, j), AF.Abs, ["dv%d_%d" % (h, j)], ["adv%d_%d" % (h, j)])
+
+    def cg(h, j):
+        return T.wide[:, h * 1280 + j * HF:h * 1280 + (j + 1) * HF]
+
+    def nr(h, j):
+        return T.wide[:, 2560 + h * 1280 + j * HF:2560 + h * 1280 + (j + 1) * HF]
+
+    def gcn(t, h, j):
+        tab, r_ = "nt%d" % t, (j + t) % M
+        act(cg(h, j), T[tab][:].indirect(lst(T.un, h, j)), AF.Copy, whole(tab) + ["un%d" % h, "mask"], ["cg%d_%d" % (h, j)],
+            scale=T.cf[:, 8 + r_:9 + r_])
+
+    def tolist(out, o, keys, w):
+        for k in range(16):
+            mm(out, T.dm[:, k * 128:(k + 1) * 128], T.wide[:, o + k:o + 1280:16], k == 0, k == 15, keys + dmk, w)
+
+    def cbank(h):
+        o = (3, 7)[h] * 512
+        return ps[:, o:o + 80], ps[:, o + 80:o + 160], "B%d" % (o // 512), o
+
+    def clist(h):
+        pc_, pt_, bk, o = cbank(h)
+        tolist(pc_, h * 1280, ["cg%d_%d" % (h, j) for j in range(M)], [bk, "cl%d" % h])
+
+    def eqs(h):
+        pc_, pt_, bk, o = cbank(h)
+        cl, n0, e0 = "cl%d" % h, h * 160, h * 560
+        cp(T.cs[:, h * 80:(h + 1) * 80], pc_, [cl], [bk, "cs%d" % h])
+        tt(T.eq[:, e0:e0 + 80], pc_, T.own[:, h * 80:(h + 1) * 80], ALU.is_equal, [cl, "own", "eqz"], [bk, "eq%d_0" % h])
+        for i in range(1, M):
+            tt(T.eq[:, e0 + i * 80:e0 + (i + 1) * 80], pc_, T.nd[:, n0 + i * HL:n0 + i * HL + 80], ALU.is_equal,
+               [cl, "nd%d" % h, "ndd%d" % h], [bk, "eq%d_%d" % (h, i)])
+        for i in range(1, M):
+            c0 = e0 + (3 + i) * 80
+            tt(T.eq[:, c0 + i * HL:c0 + 80], ps[:, o + i * HL:o + 80], T.cs[:, h * 80:(h + 1) * 80 - i * HL], ALU.is_equal,
+               [cl, "cs%d" % h], [bk, "eq%d_%d" % (h, 3 + i)])
+        tt(pt_, pc_, T.nd[:, n0:n0 + 80], ALU.subtract, [cl, "nd%d" % h], [bk, "pt%d" % h])
+
+    b4 = ps[:, 4 * 512:4 * 512 + 80]
+
+    def voids(h):
+        for i in range(7):
+            mm(b4, T.idb[:], T.eq[:, h * 560 + i * 80:h * 560 + (i + 1) * 80], i == 0, i == 6, ["idb", "eqz", "eq%d_%d" % (h, i)], ["B4", "b4"])
+        act(T.nv[:, h * 80:(h + 1) * 80], b4, AF.Relu, ["b4"], ["B4", "nv%d" % h], bias=1.0, scale=-1.0)
+
+    def chal(h, i):
+        pc_, pt_, bk, o = cbank(h)
+        cols = slice(h * 80, (h + 1) * 80)
+        if i == 0:
+            tt(pt_, pt_, T.nv[:, cols], ALU.mult, ["pt%d" % h, "nv%d" % h], [bk, "pt%d" % h])
+        elif i == 1:
+            tt(T.cn[:, cols], pt_, T.nd[:, h * 160:h * 160 + 80], ALU.add, ["pt%d" % h, "nd%d" % h], [bk, "cn%d" % h])
+        else:
+            cp(T.uc[:, cols], T.cn[:, cols], ["cn%d" % h], ["uc%d" % h])
+
+    def gu(t, h, j):
+        tab = "xt%d" % t
+        if t < 2 and j in SIDE_U:
+            return
+        tt(blk(T.du, 0, j), T[tab][:].indirect(lst(T.uc, h, j)), xmine(t, h), ALU.subtract,
+           whole(tab) + ["uc%d" % h, "xo%dh%d" % (t % 2, h)], ["du%d" % j])
+
+    def absu(t, h, j):
+        if t < 2 and j in SIDE_U:
+            out, bk = ps[:, (j % 2) * 512:(j % 2) * 512 + HF], "B%d" % (j % 2)
+            side(t, lst(T.uc, h, j), "uc%d" % h, h, 2, out, bk, "au%d" % j)
+            act(out, out, AF.Abs, ["au%d" % j], [bk, "au%d" % j])
+            return
+        act(ps[:, (j % 2) * 512:(j % 2) * 512 + HF], blk(T.du, 0, j), AF.Abs, ["du%d" % j], ["B%d" % (j % 2), "au%d" % j])
+
+    def cmpr(h, j):
+        tt(nr(h, j), ps[:, (j % 2) * 512:(j % 2) * 512 + HF], blk(T.adv, h, j), ALU.is_lt, ["au%d" % j, "adv%d_%d" % (h, j)],
+           ["B%d" % (j % 2), "nr%d_%d" % (h, j)])
+
+    def difff(t, h):
+        if t == R - 1:
+            return
+        for i, (o, n) in enumerate(TILES):
+            out = ps[0:n, 6 * 512 + i * 64:6 * 512 + (i + 1) * 64]
+            c0 = base + h * HF + o
+            mm(out, T["nt%d" % t][:, c0:c0 + n], T.gn[:], True, False, ["nt%dh%d" % (t, h), "gn"], ["B6", "df"])
+            for j in range(M):
+                c1 = h * 1280 + j * HF + o
+                mm(out, T.wide[:, c1:c1 + n], T.gdf[:, 6 - 2 * j:70 - 2 * j], False, j == M - 1, ["cg%d_%d" % (h, j), "gdf"], ["B6", "df"])
+
+    def fbank(h, i):
+        b = (5, 4, 3)[i] if h else 5
+        return b, b * 512 + 256 * (b != 5) + i * 64
+
+    def countf(t, h, js):
+        if t == R - 1:
+            return
+        for i, (o, n) in enumerate(TILES):
+            b, c0 = fbank(h, i)
+            for j in js:
+                c1 = 2560 + h * 1280 + j * HF + o
+                mm(ps[0:n, c0:c0 + 64], T.wide[:, c1:c1 + n], T.gcf[:, 6 - 2 * j:70 - 2 * j], j == 0, j == M - 1,
+                   ["nr%d_%d" % (h, j), "gcf"], ["B%d" % b, "cf_%d" % i])
+
+    def wins(out, src, r, w):
+        act(out, src, AF.Sigmoid, r, w, bias=-2176.0, scale=256.0)
+
+    def winf(t, h):
+        if t < R - 1 and h == 0:
+            wins(T.wf[:], ps[:, 5 * 512:5 * 512 + 192], ["cf_2"], ["B5", "wf"])
+        elif t < R - 1:
+            for i, (o, n) in enumerate(TILES):
+                b, c0 = fbank(h, i)
+                wins(T.wf[0:n, i * 64:(i + 1) * 64], ps[0:n, c0:c0 + 64], ["cf_%d" % i], ["B%d" % b, "wf", "wg"])
+
+    def pickf(t):
+        if t < R - 1:
+            tt(T.tf[:, :, 0:8], ps[:, 6 * 512:6 * 512 + 192], T.wf[:], ALU.mult, ["df", "wf"], ["B6", "tf"])
+
+    def rows_p(t, h, first):
+        if t == R - 1:
+            return
+        if first:
+            c0 = base + h * HF
+            mm(b2, T.idb[:], T["nt%d" % t][:, c0:c0 + HF], True, False, ["idb", "nt%dh%d" % (t, h)], ["B2", "b2"], c=HF)
+            return
+        for i, (o, n) in enumerate(TILES):
+            mm(ps[:, 2 * 512 + o:2 * 512 + o + n], T.tf[0:n, 8 * i:8 * i + 8, :], T.idb[0:n, 0:n], False, i == 2, ["tf", "idb"], ["B2", "b2"], c=n)
+
+    def rows_a(t, h):
+        if t < R - 1:
+            c0 = base + h * HF
+            act(T["nt%d" % (t + 1)][:, c0:c0 + HF], b2, AF.Copy, ["b2"], ["B2", "nt%dh%d" % (t + 1, h)])
+            send("nt%d" % (t + 1), h * HF)
+
+    def countl(h):
+        tolist(b4, 2560 + h * 1280, ["nr%d_%d" % (h, j) for j in range(M)], ["B4", "b4"])
+
+    def winl(h):
+        wins(T.wl[:, h * 80:(h + 1) * 80], b4, ["b4"], ["B4", "wl%d" % h])
+
+    def pickl(t, h, i):
+        pc_, pt_, bk, o = cbank(h)
+        n_ = T.nd[:, h * 160:h * 160 + 80]
+        if i == 0:
+            tt(pt_, pt_, T.wl[:, h * 80:(h + 1) * 80], ALU.mult, ["pt%d" % h, "wl%d" % h], [bk, "pt%d" % h])
+        elif i == 1 and t == R - 1:
+            tt(T.yns[:, :, h * HL:(h + 1) * HL], pt_, n_, ALU.add, ["pt%d" % h, "nd%d" % h], [bk, "yns%d" % h])
+        elif i == 1:
+            tt(n_, pt_, n_, ALU.add, ["pt%d" % h, "nd%d" % h], [bk, "nd%d" % h])
+        elif t < R - 1:
+            cp(T.un[:, h * 80:(h + 1) * 80], n_, ["nd%d" % h], ["un%d" % h])
+            dup(h)
+
+    dup(0)
+    dup(1)
+    for t in range(R):
+        u = t - 1
+        if t:
+            winf(u, 1)
+        gv(t, 0, 0); prep(t, 0, 0)
+        if t:
+            pickf(u); rows_p(u, 1, False); countl(1); rows_a(u, 1)
+        gv(t, 0, 1); prep(t, 0, 1)
+        gv(t, 0, 2); prep(t, 0, 2); prep(t, 0, 3); gv(t, 0, 3)
+        if t:
+            winl(1)
+        mixin(t, 0)
+        for j in range(M):
+            absv(t, 0, j)
+        med(t, 0, 0); med(t, 0, 1); med(t, 0, 2)
+        if t:
+            pickl(u, 1, 0)
+        med(t, 0, 3)
+        if t:
+            pickl(u, 1, 1)
+        med(t, 0, 4)
+        if t:
+            pickl(u, 1, 2)
+        med(t, 0, 5); gv(t, 1, 0); prep(t, 1, 0); med(t, 0, 6); gv(t, 1, 1); med(t, 0, 7)
+        prep(t, 1, 1); prep(t, 1, 2); prep(t, 1, 3)
+        gv(t, 1, 2); med(t, 0, 8); newx_p(t, 0); gv(t, 1, 3)
+        for j in range(M):
+            absv(t, 1, j)
+        newx_a(t, 0); mixin(t, 1)
+        for i in range(9):
+            med(t, 1, i)
+        for j in range(M):
+            gcn(t, 0, j)
+        newx_p(t, 1); clist(0); newx_a(t, 1); gcn(t, 1, 0)
+        eqs(0); voids(0); chal(0, 0); gcn(t, 1, 1); chal(0, 1); chal(0, 2); difff(t, 0); rows_p(t, 0, True)
+        gu(t, 0, 0); absu(t, 0, 0); gcn(t, 1, 2); gu(t, 0, 1); absu(t, 0, 1); gcn(t, 1, 3); clist(1); cmpr(0, 0)
+        gu(t, 0, 2); absu(t, 0, 2); cmpr(0, 1); gu(t, 0, 3); absu(t, 0, 3); eqs(1); voids(1); cmpr(0, 2)
+        cmpr(0, 3); chal(1, 0); countf(t, 0, range(M)); countl(0); chal(1, 1); chal(1, 2)
+        gu(t, 1, 0); absu(t, 1, 0); winf(t, 0); gu(t, 1, 1); absu(t, 1, 1); winl(0); pickf(t); rows_p(t, 0, False); difff(t, 1); cmpr(1, 0)
+        gu(t, 1, 2); absu(t, 1, 2); rows_a(t, 0); pickl(t, 0, 0); cmpr(1, 1); pickl(t, 0, 1)
+        gu(t, 1, 3); absu(t, 1, 3); rows_p(t, 1, True); countf(t, 1, [0, 1]); pickl(t, 0, 2)
+        cmpr(1, 2); countf(t, 1, [2]); cmpr(1, 3); countf(t, 1, [3])
+    countl(1); winl(1); pickl(R - 1, 1, 0); pickl(R - 1, 1, 1)
+    op("s", lambda e: e.dma_start(T.yn[:], T.yns[:]), r=["yns0", "yns1"], dma=("sto", 48))
+    finish([("sto", 48), ("sent", sent[0]), ("ldx", 16), ("ldo", 16), ("ldn", 16), ("ldm", 16)])

@@ -1,45 +1,54 @@
 from concourse.bass import DstId, RemoteDMATransfer
 from concourse.mybir import AluOpType as ALU, ActivationFunctionType as AF
 
-N, F, M, R = 6, 640, 4, 5
+N, F, M, R, WORLD = 6, 640, 4, 5, 256
 W = N * F
 HF, HL = F // 2, F // 32
-TILES = ((0, 128), (128, 128), (256, 64))
 XD = ["bfloat16", "bfloat16", "float32", "float32", "float32"]
+
+UNITS_A = [(0, 0, 320), (1, 0, 192), (1, 192, 128)]
+UNITS_B = [(0, 0, 320), (1, 0, 320)]
+SIDE_V = [{0: "p"}, {0: "p"}, {0: "s", 3: "s"}, {0: "s", 3: "s"}, {0: "s", 3: "s"}]
+SIDE_U = [{3: "p"}, {3: "p"}, {3: "s"}, {3: "s"}, {3: "s"}]
+SHARED = (0,)
 
 SCRATCH = {
     "nbi": ("sbuf", [128, 4, 40], "int32"), "pti": ("sbuf", [128, 8, 40], "int32"), "ptb": ("sbuf", [128, 320], "bfloat16"),
     "mixs": ("sbuf", [128, F], "bfloat16"), "wide": ("sbuf", [128, 5120], "bfloat16"),
-    "dv": ("sbuf", [128, 2560], "float32"), "adv": ("sbuf", [128, 2560], "float32"), "du": ("sbuf", [128, 1280], "float32"),
-    "tmp": ("sbuf", [128, 4 * HF], "float32"), "na": ("sbuf", [128, HF], "float32"), "pos": ("sbuf", [128, F], "float32"),
-    "xb0": ("sbuf", [128, F], "bfloat16"), "xb1": ("sbuf", [128, F], "bfloat16"), "xo": ("sbuf", [128, 2 * F], "float32"),
-    "ef": ("sbuf", [128, F], "float32"), "eb": ("sbuf", [128, F], "bfloat16"),
+    "dv": ("sbuf", [128, 2, 4, HF], "float32"), "adv": ("sbuf", [128, 2, 4, HF], "float32"), "du": ("sbuf", [128, 4, HF], "float32"),
+    "tmp": ("sbuf", [128, 2, 5, HF], "float32"), "rawf": ("sbuf", [128, 4, HF], "float32"), "rawb": ("sbuf", [128, 4, HF], "bfloat16"),
+    "mob": ("sbuf", [128, F], "bfloat16"), "mof": ("sbuf", [128, F], "float32"),
     "yes": ("sbuf", [128, F], "float32"), "yds": ("sbuf", [128, F], "float32"), "yns": ("sbuf", [128, 4, 40], "float32"),
-    "nd": ("sbuf", [128, 320], "float32"), "own": ("sbuf", [128, 160], "float32"), "cs": ("sbuf", [128, 160], "float32"),
-    "cn": ("sbuf", [128, 160], "float32"), "un": ("sbuf", [128, 160], "uint16"), "uc": ("sbuf", [128, 160], "uint16"),
-    "eq": ("sbuf", [128, 1120], "bfloat16"), "nv": ("sbuf", [128, 160], "float32"), "wl": ("sbuf", [128, 160], "bfloat16"),
-    "wf": ("sbuf", [128, 192], "bfloat16"), "tf": ("sbuf", [128, 24, 16], "bfloat16"),
+    "nd": ("sbuf", [128, 2, 7, HL], "float32"), "own": ("sbuf", [128, 2, 4, HL], "float32"),
+    "un": ("sbuf", [128, 2, 4, HL], "uint16"), "cs": ("sbuf", [128, 160], "float32"), "uc": ("sbuf", [128, 160], "uint16"),
+    "eq": ("sbuf", [128, 2, 7, 80], "bfloat16"), "wl": ("sbuf", [128, 160], "bfloat16"),
+    "wf": ("sbuf", [128, 192], "bfloat16"), "tf": ("sbuf", [128, 24, 16], "bfloat16"), "zb": ("sbuf", [128, 192], "bfloat16"),
     "ci": ("sbuf", [128, 128], "float32"), "cm": ("sbuf", [128, 128], "float32"), "ch": ("sbuf", [128, 72], "float32"),
     "pi": ("sbuf", [128, 8], "int32"), "cf": ("sbuf", [128, 16], "float32"), "km": ("sbuf", [128, 16], "float32"),
-    "dm": ("sbuf", [128, 2048], "bfloat16"), "idb": ("sbuf", [128, 128], "bfloat16"), "b8": ("sbuf", [128, 128], "bfloat16"),
-    "neg": ("sbuf", [128, 128], "bfloat16"), "raw": ("sbuf", [128, 3 * HF], "bfloat16"),
-    "am": ("sbuf", [128, 128], "float32"), "ab": ("sbuf", [128, 128], "bfloat16"),
+    "dm": ("sbuf", [128, 2048], "bfloat16"),
+    "idb": ("sbuf", [128, 128], "bfloat16"), "idf": ("sbuf", [128, 128], "float32"), "neg": ("sbuf", [128, 128], "bfloat16"),
+    "far": ("sbuf", [128, 128], "bfloat16"), "b8": ("sbuf", [128, 128], "bfloat16"),
+    "amb": ("sbuf", [128, 128], "bfloat16"), "amf": ("sbuf", [128, 128], "float32"),
     "gcf": ("sbuf", [128, 72], "bfloat16"), "gdf": ("sbuf", [128, 72], "bfloat16"), "gn": ("sbuf", [128, 64], "bfloat16"),
     "ps": ("psum", [128, 4096], "float32"),
 }
 for _t in range(R):
-    SCRATCH["xt%d" % _t] = ("sbuf", [128, W], XD[_t])
+    SCRATCH["xt%d" % _t] = ("sbuf", [128, W + 16], XD[_t])
     SCRATCH["nt%d" % _t] = ("sbuf", [128, W], "bfloat16")
+    SCRATCH["xo%d" % _t] = ("sbuf", [128, F], XD[_t])
 
-EVENTS = [("xt0", 0, F), ("nt0", 0, F)]
+EVENTS = [("xt0", 0, F, "late"), ("nt0", 0, F, "early")]
 for _t in range(1, R):
-    EVENTS += [("xt%d" % _t, 0, HF), ("xt%d" % _t, HF, HF), ("nt%d" % _t, 0, HF), ("nt%d" % _t, HF, HF)]
-WAYS = ["late", "late"] + ["early", "late", "early", "late"] * (R - 1)
-GATHER, HAND, FLY = 560, 120, (3500, 3.0, 4000)
-LOOK = {"v": 60, "a": 150, "p": 150, "g": 0, "s": 0}
-SIDE_V, SIDE_U = (), (3,)
-TURNS, TRIES, ORDER = 4, 2000, []
-SEMAPHORES = ["sv", "sa", "sp", "sg", "ldx", "ldo", "ldn", "ldm", "sto", "sent"] + ["e%s_%d" % (e[0], e[1]) for e in EVENTS]
+    EVENTS += [("xt%d" % _t, u[0] * HF + u[1], u[2], "late" if u == UNITS_A[-1] else "early") for u in UNITS_A]
+    EVENTS += [("nt%d" % _t, u[0] * HF + u[1], u[2], "late" if u == UNITS_B[-1] else "mate") for u in UNITS_B]
+
+GATHER, HAND, FLY, LOCAL = (65, 1.6), 140, (4200, 3.5, 4000), 2300
+SPEEDS = [(1.2, 1.2), (1.6, 1.0), (2.0, 0.75)]
+SHIFT, SLACK = 1500, 500
+SAME = {"au0": ["pa0"], "au1": ["pc0"], "rows0": ["pa0"], "rows1": ["pc0"], "cf_": ["pa1"], "df": ["pc1"], "b2": ["nx0"]}
+TURNS, TRIES, ORDER = 4, 2500, []
+SEMAPHORES = (["sv", "sa", "sp", "sg", "ldx", "ldn", "ldm", "sto", "sent"] + ["xo%d" % t for t in range(R)]
+              + ["e%s_%d" % e[:2] for e in EVENTS])
 
 
 def ones(m):
@@ -48,50 +57,58 @@ def ones(m):
 
 def routes(T, topo):
     cores = list(T.cores)
-    best = None
-    for a in range(1, N):
-        for b in range(a + 1, N):
-            worst = 0
-            for s in range(N):
-                for part in ((a, b), [d for d in range(1, N) if d not in (a, b)]):
-                    worst = max(worst, sum(1 for d in part if not topo.same_plane(cores[s], cores[(s + d) % N])))
-            if best is None or worst < best[0]:
-                best = (worst, (a, b))
+    cross = lambda s, ds: sum(1 for d in ds if not topo.same_plane(cores[s], cores[(s + d) % N]))
+    pairs = [(a, b) for a in range(1, N) for b in range(a + 1, N)]
+    two = min(pairs, key=lambda p: max(max(cross(s, p), cross(s, [d for d in range(1, N) if d not in p])) for s in range(N)))
+    three = [d for d in range(1, N) if d not in two]
     out = []
-    for s in range(N):
-        two = [(s + d) % N for d in best[1]]
-        three = [(s + d) % N for d in range(1, N) if d not in best[1]]
-        helper = [c for c in topo.cores_of(cores[s])
-                  if topo.die(c) != topo.die(cores[s]) and all(topo.may_write(c, cores[d]) for d in two + three)][0]
-        out.append((three, two, helper))
+    for s, c in enumerate(cores):
+        mates_ = [h for h in topo.cores_of(c) if h != c]
+        ways = {}
+        for last in (False, True):
+            straight, helped = (three[:2], list(two) + three[2:]) if last else (list(two), three)
+            way, used = [((s + d) % N, None) for d in straight], []
+            dies = [True, True, not last]
+            order = sorted(range(3), key=lambda i: topo.same_plane(c, cores[(s + helped[i]) % N]))
+            for i in order:
+                to = cores[(s + helped[i]) % N]
+                able = [h for h in mates_ if (topo.die(h) != topo.die(c)) == dies[i] and topo.may_write(h, to)]
+                able.sort(key=lambda h: (used.count(h), all(topo.may_write(h, x) for x in cores if x != c) and topo.same_plane(c, to)))
+                used.append(able[0])
+                way.append(((s + helped[i]) % N, able[0]))
+            ways["late" if last else "early"] = way
+        way = [((s + two[0]) % N, None)]
+        for i, d in enumerate(d for d in range(1, N) if d != two[0]):
+            to = cores[(s + d) % N]
+            way.append(((s + d) % N, [h for h in range(WORLD) if topo.mates(h, to) and topo.may_write(h, to)][i]))
+        ways["mate"] = way
+        out.append(ways)
     return out
 
 
-def split(route, ev):
-    three, two = route[0], route[1]
-    way = WAYS[EVENTS.index(ev)]
-    return {"own": (three + two, []), "late": (three, two), "early": (two, three)}[way]
+def piece(T, ev, rank):
+    return T[ev[0]][:, rank * F + ev[1]:rank * F + ev[1] + ev[2]]
 
 
 def transfer(T, topo, src, dsts, ev, rank, mask):
-    ap = T[ev[0]][:, rank * F + ev[1]: rank * F + ev[1] + ev[2]]
     ids = [DstId(rid=topo.addr(d, src)[0], pnc=topo.addr(d, src)[1]) for d in dsts]
     return RemoteDMATransfer(dst_ids=ids, dma_engine_mask=mask, remote_sem=T.sem["e%s_%d" % ev[:2]],
-                             srcs=[ap], dsts=[ap for d in dsts])
+                             srcs=[piece(T, ev, rank)], dsts=[piece(T, ev, rank) for d in dsts])
 
 
-def helper_program(g, core, T, topo, rank, route):
+def helper_program(g, core, T, topo, rts):
     cores = list(T.cores)
-    far = topo.mask(core, cores[route[0][0]])
-    near = topo.mask(cores[rank], core) & ~topo.mask(cores[rank], cores[route[0][0]])
     sent = 0
     for ev in EVENTS:
-        dsts = [cores[d] for d in split(route, ev)[1]]
-        if dsts:
-            g.wait_ge(T.sem["e%s_%d" % ev[:2]], ones(near))
-            g.remote_dma_fused([transfer(T, topo, core, dsts, ev, rank, far)], local_sem=T.sem.sent)
-            sent += ones(far)
-    g.wait_ge(T.sem.sent, sent)
+        for rank in range(N):
+            dsts = [cores[d] for d, h in rts[rank][ev[3]] if h == core]
+            if dsts:
+                far = topo.mask(core, dsts[0])
+                g.wait_ge(T.sem["e%s_%d" % ev[:2]], ones(far if ev[3] == "mate" else topo.mask(cores[rank], core) & ~far))
+                g.remote_dma_fused([transfer(T, topo, core, dsts, ev, rank, far)], local_sem=T.sem.sent)
+                sent += ones(far)
+    if sent:
+        g.wait_ge(T.sem.sent, sent)
 
 
 def make_emitter(g, T):
@@ -101,8 +118,8 @@ def make_emitter(g, T):
     known = {k: {} for k in q}
     clock, writer, readers = {}, {}, {}
 
-    def apart(e, k):
-        return e in "pgs" or k[0] == "B" or k in ("wf", "wg", "mask") or (e == "v" and k[:2] in ("pa", "pc", "pt"))
+    def apart(e, k, r):
+        return e in "pgsl" or k[0] == "B" or k == "mask" or (e == "v" and k[:2] in ("pa", "pc", "pt") and k in r)
 
     def need(e, s, n):
         if known[e].get(s, 0) >= n:
@@ -112,7 +129,7 @@ def make_emitter(g, T):
         for s2, n2 in clock.get((s, n), {}).items():
             known[e][s2] = max(known[e].get(s2, 0), n2)
 
-    def op(e, call, r=(), w=(), dma=None, group=False):
+    def op(e, call, r, w, dma):
         deps = {}
         mine = sem.get(e)
         for k in r:
@@ -120,10 +137,8 @@ def make_emitter(g, T):
                 deps[writer[k]] = 1
         for k in w:
             for d in readers.get(k, []) + ([writer[k]] if k in writer else []):
-                if d[0] != mine or dma or not apart(e, k):
+                if d[0] != mine or dma or not apart(e, k, r):
                     deps[d] = 1
-        if group:
-            deps = {d: 1 for d in deps if d[0] != mine}
         top = {}
         for s, n in deps:
             top[s] = max(top.get(s, 0), n)
@@ -133,8 +148,8 @@ def make_emitter(g, T):
         if dma == "remote":
             return
         if dma:
-            ins.then_inc(T.sem[dma[0]], 16)
-            me = dma
+            ins.then_inc(T.sem[dma], 16)
+            me = (dma, total[dma])
         else:
             count[e] += 1
             ins.then_inc(T.sem[mine], 1)
@@ -149,88 +164,152 @@ def make_emitter(g, T):
     def outside(key, s, n):
         writer[key] = (s, n)
 
-    calls = []
+    calls, total = [], {}
 
-    def note(e, call, r=(), w=(), dma=None, c=100, far=None):
-        calls.append((e, call, list(r), list(w), dma, c, far))
+    def note(e, call, r=(), w=(), dma=None, c=100, far=(), kind=""):
+        r, w = [[x for k in keys for x in SAME.get(k, [k])] for keys in (r, w)]
+        calls.append((e, call, r, w, dma, c, far, e + kind))
+        if dma and dma != "remote":
+            total[dma] = total.get(dma, 0) + 16
 
     def arrange():
+        n_ = len(calls)
         pre = [dict() for c in calls]
         wr, rd, sends = {}, {}, {}
-        for i, (e, call, r, w, dma, c, far) in enumerate(calls):
+        for i, (e, call, r, w, dma, c, far, kind) in enumerate(calls):
+            if e != "p":
+                r = r + [k for k in w if k[0] == "B"]
             for k in r:
                 if k in wr:
                     pre[i][wr[k]] = max(pre[i].get(wr[k], 0), HAND)
                 if k in sends:
-                    pre[i][sends[k][0]] = sends[k][1]
+                    pre[i][sends[k][0]] = max(pre[i].get(sends[k][0], 0), sends[k][1])
             for k in w:
+                if k[0] == "B" and e != "p":
+                    continue
                 for d in rd.get(k, []) + ([wr[k]] if k in wr else []):
-                    if d != i:
-                        pre[i][d] = max(pre[i].get(d, 0), HAND if calls[d][0] != e or not apart(e, k) else 0)
+                    if d != i and (calls[d][0] != "l" or e == "l"):
+                        pre[i][d] = max(pre[i].get(d, 0), HAND if calls[d][0] != e or not apart(e, k, r) else 0)
             for k in r:
                 rd.setdefault(k, []).append(i)
             for k in w:
-                wr[k] = i
-                rd[k] = []
-            if far:
-                sends[far[0]] = (i, far[1])
-        rest = [c[5] for c in calls]
-        post = [[] for c in calls]
-        for i in range(len(calls) - 1, -1, -1):
+                if k[0] != "B" or e == "p":
+                    wr[k] = i
+                    rd[k] = []
+            for k, lag in far:
+                sends[k] = (i, lag)
+        length = [c[5] for c in calls]
+        rest, back = list(length), [dict() for c in calls]
+        for i in range(n_ - 1, -1, -1):
             for d, lag in pre[i].items():
-                rest[d] = max(rest[d], calls[d][5] + lag + rest[i])
-                post[d].append(i)
-        back = [{i: pre[i][d] for i in post[d]} for d in range(len(calls))]
+                rest[d] = max(rest[d], length[d] + lag + rest[i])
+                back[d][i] = lag
+        eng = [c[0] for c in calls]
+        busy = [(100 if c[4] == "remote" else 150) if c[4] else c[5] for c in calls]
+        uses = [[c[0]] + sorted(set(k for k in c[3] if k[0] == "B")) for c in calls]
+        spots_ = list(q) + ["l"] + ["B%d" % b for b in range(8)]
 
-        def run(before, after, rank_):
-            left = [len(p) for p in before]
-            ready = [i for i in range(len(calls)) if not left[i]]
-            at, done, free, order = [0] * len(calls), [0] * len(calls), {k: 0 for k in q}, []
-            while ready:
-                start = {i: max(at[i], free[calls[i][0]]) for i in ready}
-                first = min(ready, key=lambda i: (start[i], -rank_[i]))
-                e = calls[first][0]
-                i = max((j for j in ready if calls[j][0] == e and start[j] <= start[first] + LOOK[e]), key=lambda j: (rank_[j], -j))
-                ready.remove(i)
-                order.append(i)
-                done[i] = start[i] + calls[i][5]
-                free[e] = start[i] + (100 if calls[i][4] else calls[i][5])
-                for j in after[i]:
-                    at[j] = max(at[j], done[i] + before[j][i])
-                    left[j] -= 1
-                    if not left[j]:
-                        ready.append(j)
-            return max(done), order, done
+        def run(before, key, turned):
+            seq = range(n_ - 1, -1, -1) if turned else range(n_)
+            key = list(key)
+            for i in seq:
+                for d in before[i]:
+                    if key[d] >= key[i]:
+                        key[i] = key[d] + 0.01
+            done, starts, ends, whose = [0] * n_, {k: [] for k in spots_}, {k: [] for k in spots_}, {k: [] for k in spots_}
+            for i in sorted(seq, key=lambda i: key[i]):
+                at = 0
+                for d, lag in before[i].items():
+                    if done[d] + lag > at:
+                        at = done[d] + lag
+                lead = length[i] - busy[i] if turned else 0
+                at += lead
+                moved = True
+                while moved:
+                    moved, spots = False, []
+                    for k in uses[i]:
+                        st, en, by = starts[k], ends[k], whose[k]
+                        lo, hi = 0, len(en)
+                        while lo < hi:
+                            mid = (lo + hi) // 2
+                            if en[mid] + HAND <= at:
+                                lo = mid + 1
+                            else:
+                                hi = mid
+                        while lo < len(st):
+                            gap = 0 if by[lo] == eng[i] else HAND
+                            if en[lo] + gap <= at:
+                                lo += 1
+                            elif st[lo] < at + busy[i] + gap:
+                                at, moved = en[lo] + gap, len(uses[i]) > 1
+                                lo += 1
+                            else:
+                                break
+                        spots.append(lo)
+                for k, lo in zip(uses[i], spots):
+                    starts[k].insert(lo, at)
+                    ends[k].insert(lo, at + busy[i])
+                    whose[k].insert(lo, eng[i])
+                done[i] = at - lead + length[i]
+            return done
+
+        def improve(key):
+            done = run(pre, key, False)
+            late = run(back, [-x for x in done], True)
+            key = [-x for x in late]
+            done = run(pre, key, False)
+            order = sorted(range(n_), key=lambda i: (done[i] - length[i], i))
+            return sum(replay(order, *s) for s in speeds) / len(speeds), key, done
+
+        def replay(order, long_, slow):
+            done, free, who = [0] * n_, {k: 0 for k in spots_}, {}
+            for i in order:
+                at = 0
+                for d, lag in pre[i].items():
+                    x = done[d] + (lag * slow if lag > 1000 else lag)
+                    if x > at:
+                        at = x
+                e = eng[i]
+                for k in uses[i]:
+                    x = free[k] if who.get(k, e) == e else free[k] + HAND
+                    if x > at:
+                        at = x
+                done[i] = at + long_[i]
+                for k in uses[i]:
+                    free[k], who[k] = at + (long_[i] if busy[i] == length[i] else busy[i]), e
+            return max(done)
+
+        speeds = [([x * slow if c[0] == "l" or c[4] else (x - GATHER[0]) * quick / GATHER[1] + GATHER[0] if isinstance(x, float) else x
+                    for x, c in zip(length, calls)], slow) for quick, slow in SPEEDS]
 
         if not ORDER:
-            best = None
+            best = improve([-x for x in rest])
             for turn in range(TURNS):
-                span, order, done = run(pre, post, rest)
-                if best is None or span < best[0]:
-                    best = (span, order, rest)
-                rest = run(back, pre, done)[2]
-            kind = [c[0] + (c[3][-1] if c[3] else "") for c in calls]
+                best = min(best, improve(best[1]))
+            kind = [c[7] for c in calls]
             kinds = sorted(set(kind))
-            seed = [12345]
+            seed, last = [12345], best
 
             def draw():
                 seed[0] = (seed[0] * 1103515245 + 12345) % 2147483648
                 return (seed[0] >> 8) / 8388608.0
             for turn in range(TRIES):
-                shift = {k: (draw() + draw() - 1.0) * 3000 for k in kinds if draw() < 0.06}
-                rest = [x + shift.get(k, 0.0) for x, k in zip(best[2], kind)]
-                span, order, done = run(pre, post, rest)
-                if span <= best[0]:
-                    best = (span, order, rest)
-            ORDER.append(best)
+                shift = {k: (draw() + draw() - 1.0) * SHIFT for k in kinds if draw() < 0.1}
+                trial = improve([x + shift.get(k, 0.0) for x, k in zip(last[1], kind)])
+                if trial[0] <= last[0] + SLACK * (1.0 - turn / TRIES):
+                    last = trial
+                best = min(best, last)
+            order = sorted(range(n_), key=lambda i: (best[2][i] - length[i], i))
+            ORDER.append((best[0], order, best[1], best[2], kind, max(rest), pre, length))
         for i in ORDER[0][1]:
-            op(*calls[i][:5])
+            if eng[i] != "l":
+                op(*calls[i][:5])
 
     def finish(extra):
         arrange()
         for e in sem:
             need("g", sem[e], count[e])
-        for s, n in extra:
+        for s, n in list(total.items()) + extra:
             need("g", s, n)
     return note, outside, finish
 
@@ -238,438 +317,327 @@ def make_emitter(g, T):
 def rank_program(g, core, T, topo):
     rts = routes(T, topo)
     rank = T.rank_of(core)
-    if rank is None:
-        for s in range(N):
-            if rts[s][2] == core:
-                helper_program(g, core, T, topo, s, rts[s])
-        return
     cores = list(T.cores)
-    own_d, via_d, helper = rts[rank]
-    far = topo.mask(core, cores[own_d[0]])
-    near = topo.mask(core, helper) & ~far
+    if rank is None:
+        helper_program(g, core, T, topo, rts)
+        return
     op, outside, finish = make_emitter(g, T)
-    for ev in EVENTS:
-        n = 0
-        for s in range(N):
-            if rank in split(rts[s], ev)[0]:
-                n += ones(topo.mask(cores[s], core))
-            if rank in split(rts[s], ev)[1]:
-                n += ones(topo.mask(rts[s][2], core))
-        outside("far%s_%d" % ev[:2], "e%s_%d" % ev[:2], n)
-    base = rank * F
     ps = T.ps
-    sent = [0]
+    base = rank * F
+    sent, turn = [0], [0]
+    for ev in EVENTS:
+        n = sum(ones(topo.mask(cores[s] if h is None else h, core)) for s in range(N) for d, h in rts[s][ev[3]] if d == rank)
+        outside("far%s_%d" % ev[:2], "e%s_%d" % ev[:2], n)
 
-    def send(tab, c0):
-        ev = [e for e in EVENTS if e[0] == tab and e[1] == c0][0]
-        keys = [tab + "h%d" % h for h in range(c0 // HF, (c0 + ev[2]) // HF)]
-        mine, handed = split(rts[rank], ev)
-        tr = [transfer(T, topo, core, [cores[d] for d in mine], ev, rank, far)]
-        if handed:
-            tr.append(transfer(T, topo, core, [helper], ev, rank, near))
-        op("g", lambda e: e.remote_dma_fused(tr, local_sem=T.sem.sent), r=keys, w=["sends"], dma="remote",
-           far=("far%s_%d" % ev[:2], FLY[0] + FLY[1] * ev[2] * (4 if tab in ("xt2", "xt3", "xt4") else 2) + FLY[2] * (tab == "xt0")))
-        sent[0] += ones(far) + (ones(near) if handed else 0)
+    def span(name, c0, n):
+        return ["%s:%d" % (name, c) for c in range(c0 // 32, (c0 + n) // 32)]
+
+    def send():
+        ev = EVENTS[turn[0]]
+        turn[0] += 1
+        mine = [cores[d] for d, h in rts[rank][ev[3]] if h is None]
+        handed = sorted(set(h for d, h in rts[rank][ev[3]] if h is not None), key=lambda h: topo.die(h) == topo.die(core))
+        far = topo.mask(core, mine[0])
+        near = topo.mask(core, handed[0]) & ~far
+        time, lag = FLY[1] * ev[2] * (4 if ev[0] in ("xt2", "xt3", "xt4") else 2), FLY[0] + FLY[2] * (turn[0] == 1)
+        if near:
+            tr = [transfer(T, topo, core, mine, ev, rank, far), transfer(T, topo, core, handed, ev, rank, near)]
+        else:
+            tr, time, lag = [transfer(T, topo, core, handed + mine, ev, rank, far)], time / 4, lag + 2 * time
+        sent[0] += ones(far) + ones(near)
+        op("g", lambda e: e.remote_dma_fused(tr, local_sem=T.sem.sent), r=span(ev[0], ev[1], ev[2]), w=["sends"], dma="remote", kind="send")
+        op("l", None, r=["sends"], w=["links"], c=time, far=[("far%s_%d" % ev[:2], lag)], kind="link")
 
     def whole(tab):
-        return [tab + "h0", tab + "h1"] + ["far%s_%d" % e[:2] for e in EVENTS if e[0] == tab]
+        return span(tab, 0, F) + ["far%s_%d" % e[:2] for e in EVENTS if e[0] == tab] + ["pad" + tab]
 
-    def cyc(w):
-        k = w[-1].rstrip("0123456789_")
-        if k in ("dv", "du", "cg"):
-            return GATHER
-        if k in ("s", "pa", "pc", "e", "nr", "na", "pos", "adv", "au", "yes", "yds", "ptb", "rows") or k[:2] in ("xt", "xo", "nt"):
-            return 340
-        return {"tf": 210, "wf": 210, "z": 250, "pti": 180, "cl": 80, "b": 80, "df": 64, "cf": 64, "am": 270, "ab": 270}.get(k, 100)
+    def size(ap):
+        n = 1
+        for d in ap.shape[1:]:
+            n *= d
+        return n
 
-    def tt(out, a, b, alu, r, w):
-        op("v", lambda e: e.tensor_tensor(out, a, b, alu), r, w, c=cyc(w))
+    def name(w):
+        return w[-1].split(":")[0]
 
-    def ts(out, a, s1, s2, o0, o1, r, w):
+    def tt(out, a, b, alu, r, w, c=0):
+        op("v", lambda e: e.tensor_tensor(out, a, b, alu), r, w, c=c or max(64, size(out)) + 20, kind=name(w))
+
+    def ts(out, a, s1, s2, o0, o1, r, w, c=0):
         if o1 is None:
-            op("v", lambda e: e.tensor_scalar(out, a, s1, None, o0), r, w, c=cyc(w))
+            op("v", lambda e: e.tensor_scalar(out, a, s1, None, o0), r, w, c=c or max(64, size(out)) + 20, kind=name(w))
         else:
-            op("v", lambda e: e.tensor_scalar(out, a, s1, s2, o0, o1), r, w, c=cyc(w))
+            op("v", lambda e: e.tensor_scalar(out, a, s1, s2, o0, o1), r, w, c=c or max(64, size(out)) + 20, kind=name(w))
 
     def cp(out, a, r, w):
-        op("v", lambda e: e.tensor_copy(out, a), r, w, c=cyc(w))
+        op("v", lambda e: e.tensor_copy(out, a), r, w, c=max(64, size(out)) + 20, kind=name(w))
+
+    def fill(ap, v, w):
+        op("v", lambda e: e.memset(ap, v), w=w, c=max(64, size(ap) // 2) + 20, kind=name(w))
 
     def act(out, a, fn, r, w, bias=0.0, scale=1.0, c=0):
-        op("a", lambda e: e.activation(out, a, fn, bias=bias, scale=scale), r, w, c=c or cyc(w))
+        op("a", lambda e: e.activation(out, a, fn, bias=bias, scale=scale), r, w, c=c or max(64, size(out)) + 20, kind=name(w))
 
-    def mm(out, l, rh, start, stop, r, w, c=0):
-        op("p", lambda e: e.matmul(out, l, rh, start, stop), r, w, c=c or cyc(w))
+    def mm(out, l, rh, start, stop, r, w, wide=False):
+        op("p", lambda e: e.matmul(out, l, rh, start, stop), r, w, c=max(64, size(rh)) * (4 if wide else 1), kind=name(w))
 
-    op("s", lambda e: e.dma_start(T.xt0[:, base:base + F], T.x[:]), w=["xt0h0", "xt0h1", "sq"], dma=("ldx", 16), c=2200)
-    op("a", lambda e: e.dma_start(T.nbi[:], T.nb[:]), w=["nbi"], dma=("ldn", 16), c=2200)
-    op("s", lambda e: e.dma_start(T.xb0[:], T.x[:]), w=["xo0h0", "xo0h1"], dma=("ldo", 16), c=2200)
-    op("s", lambda e: e.dma_start(T.mixs[0:16, :], T.mix[:]), w=["mix"], dma=("ldm", 16), c=2200)
+    def mms(steps, r, w):
+        op("p", lambda e: [e.matmul(*s) for s in steps][-1], r, w, c=sum(max(64, size(s[2])) for s in steps), kind=name(w))
+
+    def load(q, out, in_, w, sem, r=()):
+        op(q, lambda e: e.dma_start(out, in_), r=r, w=w, dma=sem, c=LOCAL, kind=sem)
+
+    def gcost(n):
+        return GATHER[0] + GATHER[1] * n
+
+    def bank(b, c0, n, rows=slice(0, 128)):
+        return ps[rows, b * 512 + c0:b * 512 + c0 + n]
+
+    def direct(tab, c, n):
+        return T[tab][:, base + c:base + c + n]
+
+    load("s", direct("xt0", 0, F), T.x[:], span("xt0", 0, F), "ldx")
+    load("a", T.nbi[:], T.nb[:], ["nbi"], "ldn")
+    load("s", T.xo0[:], T.x[:], span("xo0", 0, F), "xo0")
+    load("s", T.mixs[0:16, :], T.mix[:], ["mix"], "ldm")
     fl = dict(allow_small_or_imprecise_dtypes=True)
-    op("g", lambda e: e.iota(T.pi[:, 0:1], [[0, 1]], 0, 1), w=["pi0"])
-    op("g", lambda e: e.iota(T.ci[:], [[1, 128]], 0, 0, **fl), w=["ci"])
-    op("g", lambda e: e.iota(T.own[:], [[HF, 2], [0, 4], [16, HL]], base, 1, **fl), w=["own"])
-    op("g", lambda e: e.iota(T.cm[:], [[0, 8], [1, 16]], 0, 0, **fl), w=["cm"])
-    op("g", lambda e: e.iota(T.ch[:], [[1, 36], [0, 2]], 0, 0, **fl), w=["ch"])
-    send("xt0", 0)
-    op("v", lambda e: e.memset(T.eq[:], 0.0), w=["eqz", "eq0_0"])
-    op("v", lambda e: e.memset(T.dm[:], 0.0), w=["dmz"])
-    op("v", lambda e: e.memset(T.tf[:], 0.0), w=["tf"])
+    op("g", lambda e: e.iota(T.pi[:, 0:1], [[0, 1]], 0, 1), w=["pi0"], c=160)
+    op("g", lambda e: e.iota(T.ci[:], [[1, 128]], 0, 0, **fl), w=["ci"], c=420)
+    op("g", lambda e: e.iota(T.cm[:], [[0, 8], [1, 16]], 0, 0, **fl), w=["cm"], c=420)
+    op("g", lambda e: e.iota(T.ch[:], [[1, 36], [0, 2]], 0, 0, **fl), w=["ch"], c=300)
+    op("g", lambda e: e.iota(T.own[:], [[HF, 2], [0, 4], [16, HL]], base, 1, **fl), w=["own"], c=480)
+    send()
+    fill(T.dm[:], 0.0, ["dmz"])
+    fill(T.tf[:], 0.0, ["tf"])
+    fill(T.zb[:], 0.0, ["zb"])
+    fill(bank(6, 128, 64), 0.0, ["B6", "df"])
+    for t in range(R):
+        fill(T["xt%d" % t][:, W:W + 16], 1024.0, ["padxt%d" % t])
     for c, m in ((1, 112), (2, 15), (3, 1)):
         ts(T.pi[:, c:c + 1], T.pi[:, 0:1], m, None, ALU.bitwise_and, None, ["pi0"], ["pi%d" % c])
-    cp(T.cf[:, 0:4], T.pi[:, 0:4], ["pi0", "pi1", "pi2", "pi3"], ["cf"])
-    P_, G16, K_, H_ = [T.cf[:, c:c + 1] for c in range(4)]
+    cp(T.cf[:, 0:4], T.pi[:, 0:4], ["pi%d" % c for c in range(4)], ["cf"])
+    col = lambda c: T.cf[:, c:c + 1]
+    P_, G16, K_, H_ = [col(c) for c in range(4)]
     ts(T.km[:], T.ci[:, 0:16], K_, None, ALU.is_equal, None, ["ci", "cf"], ["km"])
-    ts(T.cf[:, 4:5], G16, 0.25, 3.0, ALU.mult, ALU.add, ["cf"], ["cf4"])
-    ts(T.cf[:, 5:6], G16, 0.5, H_, ALU.mult, ALU.add, ["cf"], ["cf5"])
-    ts(T.cf[:, 6:7], G16, 0.5, K_, ALU.mult, ALU.add, ["cf"], ["cf6"])
-    ts(T.cf[:, 7:8], K_, 8.0, -1.0, ALU.is_lt, ALU.mult, ["cf"], ["cf7"])
+    ts(col(4), G16, 0.25, 3.0, ALU.mult, ALU.add, ["cf"], ["cf4"])
+    ts(col(5), G16, 0.5, H_, ALU.mult, ALU.add, ["cf"], ["cf5"])
+    ts(col(6), G16, 0.5, K_, ALU.mult, ALU.add, ["cf"], ["cf6"])
+    ts(col(7), K_, 8.0, -1.0, ALU.is_lt, ALU.mult, ["cf"], ["cf7"])
     for r_ in range(4):
-        ts(T.cf[:, 8 + r_:9 + r_], K_, H_, 2.0 * r_, ALU.subtract, ALU.is_equal, ["cf"], ["mask"])
+        ts(col(8 + r_), K_, H_, 2.0 * r_, ALU.subtract, ALU.is_equal, ["cf"], ["mask"])
     dmk = ["dm%d" % k for k in range(8)]
     for k in range(8):
-        ts(T.dm[:, 16 * k::129], T.eq[:, 0:16], G16, 16.0 * k, ALU.add, ALU.is_equal, ["eq0_0", "cf", "dmz"], [dmk[k]])
+        ts(T.dm[:, 16 * k::129], T.zb[:, 0:16], G16, 16.0 * k, ALU.add, ALU.is_equal, ["zb", "cf", "dmz"], [dmk[k]])
     ts(T.pti[:, 0::2, :], T.nbi[:], 4032, None, ALU.bitwise_and, None, ["nbi"], ["pti0"])
     ts(T.pti[:, 1::2, :], T.nbi[:], 63, None, ALU.bitwise_and, None, ["nbi"], ["pti1"])
     cp(T.ptb[:], T.pti[:], ["pti0", "pti1"], ["ptb"])
     zk = []
     for k in range(16):
         zk.append("z%d" % k)
-        if k % 8 < 3:
+        if k % 3 == 0:
             act(T.wide[:, k::16], T.ptb[:], AF.Copy, ["ptb", "km"], [zk[-1]], scale=T.km[:, k:k + 1])
         else:
-            ts(T.wide[:, k::16], T.ptb[:], T.km[:, k:k + 1], None, ALU.mult, None, ["ptb", "km"], [zk[-1]])
-    wide_keys = ["cg%d_%d" % (h, j) for h in range(2) for j in range(M)] + ["nr%d_%d" % (h, j) for h in range(2) for j in range(M)]
-    for h, b in ((0, 2), (1, 4)):
-        for r_ in range(8):
-            mm(ps[:, b * 512:b * 512 + HF], T.dm[:, r_ * 128:(r_ + 1) * 128], T.wide[:, r_ * F + h * HF:r_ * F + (h + 1) * HF],
-               r_ == 0, r_ == 7, zk + wide_keys + dmk, ["B%d" % b, "rows%d" % h])
-        act(T.nt0[:, base + h * HF:base + (h + 1) * HF], ps[:, b * 512:b * 512 + HF], AF.Copy, ["rows%d" % h], ["B%d" % b, "nt0h%d" % h])
-    send("nt0", 0)
+            ts(T.wide[:, k::16], T.ptb[:], T.km[:, k:k + 1], None, ALU.mult, None, ["ptb", "km"], [zk[-1]], c=180)
+    wide_keys = ["%s%d_%d" % (a, h, j) for a in ("cg", "nr") for h in range(2) for j in range(M)]
     for h in range(2):
-        cp(T.nd[:, h * 160:h * 160 + 80], T.nbi[:, :, h * HL:(h + 1) * HL], ["nbi"], ["nd%d" % h])
-        cp(T.un[:, h * 80:(h + 1) * 80], T.nbi[:, :, h * HL:(h + 1) * HL], ["nbi"], ["un%d" % h])
+        for r_ in range(8):
+            c = r_ * F + h * HF
+            mm(bank(h, 0, HF), T.dm[:, r_ * 128:(r_ + 1) * 128], T.wide[:, c:c + HF], r_ == 0, r_ == 7, zk + wide_keys + dmk, ["B%d" % h, "rows%d" % h])
+        act(direct("nt0", h * HF, HF), bank(h, 0, HF), AF.Copy, ["rows%d" % h], ["B%d" % h] + span("nt0", h * HF, HF))
+    send()
+    for b in range(2):
+        src = T.nbi[:, :, b * HL:(b + 1) * HL]
+        cp(T.un[:, b], src, ["nbi"], span("un%d" % b, 0, HF))
+        cp(T.nd[:, b, 0:4], src, ["nbi"], span("nd%d" % b, 0, HF))
+        act(T.nd[:, b, 4:7], T.nd[:, b, 0:3], AF.Copy, span("nd%d" % b, 0, HF), span("ndd%d" % b, 0, HF))
     ts(T.own[:], T.own[:], G16, None, ALU.subtract, None, ["own", "cf"], ["own"])
     ts(T.idb[:], T.ci[:], P_, None, ALU.is_equal, None, ["ci", "cf"], ["idb"])
     ts(T.neg[:], T.ci[:], P_, -1.0, ALU.is_equal, ALU.mult, ["ci", "cf"], ["neg"])
+    ts(T.far[:], T.ci[:], P_, 8192.0, ALU.is_equal, ALU.mult, ["ci", "cf"], ["far"])
     ts(T.b8[:], T.cm[:], K_, 0.125, ALU.is_equal, ALU.mult, ["cm", "cf"], ["b8"])
-    ts(T.gcf[:], T.ch[:], T.cf[:, 4:5], None, ALU.is_equal, None, ["ch", "cf4"], ["gcf"])
-    ts(T.gdf[:], T.ci[:, 0:72], T.cf[:, 5:6], 6.0, ALU.subtract, ALU.is_equal, ["ci", "cf5"], ["gdf"])
-    ts(T.gn[:], T.ci[:, 0:64], T.cf[:, 6:7], T.cf[:, 7:8], ALU.is_equal, ALU.mult, ["ci", "cf6", "cf7"], ["gn"])
-    tt(T.am[:], T.idb[:], T.b8[:], ALU.subtract, ["idb", "b8"], ["am"])
-    tt(T.ab[:], T.idb[:], T.b8[:], ALU.subtract, ["idb", "b8"], ["ab"])
+    ts(T.gcf[:], T.ch[:], col(4), None, ALU.is_equal, None, ["ch", "cf4"], ["gcf"])
+    ts(T.gdf[:], T.ci[:, 0:72], col(5), 6.0, ALU.subtract, ALU.is_equal, ["ci", "cf5"], ["gdf"])
+    ts(T.gn[:], T.ci[:, 0:64], col(6), col(7), ALU.is_equal, ALU.mult, ["ci", "cf6", "cf7"], ["gn"])
+    tt(T.amb[:], T.idb[:], T.b8[:], ALU.subtract, ["idb", "b8"], ["amb"], c=270)
+    act(T.idf[:], T.idb[:], AF.Copy, ["idb"], ["idf"])
+    act(T.amf[:], T.amb[:], AF.Copy, ["amb"], ["amf"])
 
-    def xown(t, h):
-        return T["xt%d" % t][:, base + h * HF:base + (h + 1) * HF]
+    slot_of = {"rawf": [0], "rawb": [0]}
 
-    def xmine(t, h):
-        if t < 2:
-            return (T.xb0, T.xb1)[t][:, h * HF:(h + 1) * HF]
-        return T.xo[:, (t % 2) * F + h * HF:(t % 2) * F + (h + 1) * HF]
+    def offs(b, c0, n, j):
+        return T.un[:, b, j, c0 // 16:(c0 + n) // 16]
 
-    def blk(buf, h, j):
-        return buf[:, h * 1280 + j * HF:h * 1280 + (j + 1) * HF]
-
-    def lst(buf, h, j):
-        return buf[:, h * 80 + j * HL:h * 80 + (j + 1) * HL]
-
-    def dup(h):
-        act(T.nd[:, h * 160 + 80:h * 160 + 140], T.nd[:, h * 160:h * 160 + 60], AF.Copy, ["nd%d" % h], ["ndd%d" % h])
-
-    def side(t, off, key, h, slot, out, bk, made):
-        tab, raw = "xt%d" % t, T.raw[:, slot * HF:(slot + 1) * HF]
-        act(raw, T[tab][:].indirect(off), AF.Copy, whole(tab) + [key], ["raw%d" % slot], c=GATHER)
-        mm(out, T.neg[:], xmine(t, h), True, False, ["neg", "xo%dh%d" % (t % 2, h)], [bk, made], c=HF)
-        mm(out, T.idb[:], raw, False, True, ["idb", "raw%d" % slot], [bk, made], c=HF)
-
-    def gv(t, h, j):
-        tab = "xt%d" % t
-        if t < 2 and j in SIDE_V:
-            pa, pc, ba, bc = pslots(h)
-            out, bk, made = (pc, bc, "pc%d" % h) if j == 0 else (pa, ba, "pa%d" % h)
-            side(t, lst(T.un, h, j), "un%d" % h, h, j, out, bk, made)
-            act(blk(T.adv, h, j), out, AF.Abs, [made], [bk, "adv%d_%d" % (h, j)])
+    def gather(t, b, c0, n, off, okeys, way, out, w):
+        tab, c = "xt%d" % t, b * HF + c0
+        if way is None:
+            tt(out, T[tab][:].indirect(off), T["xo%d" % t][:, c:c + n], ALU.subtract, whole(tab) + okeys + span("xo%d" % t, c, n), w, c=gcost(n))
             return
-        tt(blk(T.dv, h, j), T[tab][:].indirect(lst(T.un, h, j)), xmine(t, h), ALU.subtract,
-           whole(tab) + ["un%d" % h, "xo%dh%d" % (t % 2, h)], ["dv%d_%d" % (h, j)])
-
-    def pslots(h):
-        b = (0, 5)[h]
-        return ps[:, b * 512:b * 512 + HF], ps[:, (b + 1) * 512:(b + 1) * 512 + HF], "B%d" % b, "B%d" % (b + 1)
-
-    def prep(t, h, i):
-        pa, pc, ba, bc = pslots(h)
-        d1, src, bk = "dv%d_1" % h, blk(T.dv, h, 1), []
-        if t < 2 and 1 in SIDE_V:
-            d1, src, bk = "pa%d" % h, pa, [ba]
-        if i == 0:
-            if not (t < 2 and 0 in SIDE_V):
-                act(pc, blk(T.dv, h, 0), AF.Copy, ["dv%d_0" % h], [bc, "pc%d" % h])
-        elif i == 1:
-            act(T.na[:], src, AF.Relu, [d1], bk + ["na"], scale=-1.0)
-        elif i == 2:
-            act(T.pos[:, h * HF:(h + 1) * HF], src, AF.Relu, [d1], bk + ["pos%d" % h])
+        buf = "rawb" if way == "p" else "rawf"
+        s = slot_of[buf][0] % 4
+        slot_of[buf][0] += 1
+        raw, rk = T[buf][:, s, 0:n], "%s%d" % (buf, s)
+        act(raw, T[tab][:].indirect(off), AF.Copy, whole(tab) + okeys, [rk], c=gcost(n))
+        if way == "p":
+            mm(out, T.neg[:], direct(tab, c, n), True, False, ["neg"] + span(tab, c, n), w)
+            mm(out, T.idb[:], raw, False, True, ["idb", rk], w)
         else:
-            act(pa, T.na[:], AF.Copy, ["na"], [ba, "pa%d" % h], scale=-1.0)
+            tt(out, raw, bank(3 + b, 160 + c0, n), ALU.subtract, [rk, "xf%d" % b], ["B%d" % (3 + b)] + w)
 
-    def med(t, h, i):
-        pa, pc, ba, bc = pslots(h)
-        a, c = "pa%d" % h, "pc%d" % h
-        s = [T.tmp[:, k * HF:(k + 1) * HF] for k in range(3)]
-        d2, d3 = blk(T.dv, h, 2), blk(T.dv, h, 3)
-        e_ = (T.eb if t < 2 else T.ef)[:, h * HF:(h + 1) * HF]
-        if i == 0:
-            tt(s[0], pc, d2, ALU.min, [c, "dv%d_2" % h], [bc, "s0"])
-        elif i == 1:
-            tt(pc, pc, d2, ALU.max, [c, "dv%d_2" % h], [bc, c])
-        elif i == 2:
-            tt(pa, pa, s[0], ALU.max, [a, "s0"], [ba, a])
-        elif i == 3:
-            tt(s[1], pc, T.pos[:, h * HF:(h + 1) * HF], ALU.min, [c, "pos%d" % h], [bc, "s1"])
-        elif i == 4:
-            tt(pc, pa, s[1], ALU.max, [a, "s1"], [ba, bc, c])
-        elif i == 5:
-            tt(pa, pa, s[1], ALU.min, [a, "s1"], [ba, a])
-        elif i == 6:
-            tt(s[2], pc, d3, ALU.min, [c, "dv%d_3" % h], [bc, "s2"])
-        elif i == 7 and t < R - 1:
-            tt(e_, pa, s[2], ALU.max, [a, "s2"], [ba, "e%d" % h])
-        elif i == 7:
-            tt(pa, pa, s[2], ALU.max, [a, "s2"], [ba, a])
-        elif t == R - 1:
-            tt(e_, pa, xmine(t, h), ALU.add, [a, "xo%dh%d" % (t % 2, h)], [ba, "e%d" % h])
-
-    b2 = ps[:, 2 * 512:2 * 512 + HF]
-
-    def mixin(t, h):
-        o, bk, nx = xbank(h)
+    def medians(t, u):
+        b, c0, n = UNITS_A[u]
+        s, cc, tab = u % 2, b * HF + c0, "xt%d" % t
+        pa, pc, ba, bc = bank(5 * s, 0, n), bank(5 * s + 1, 0, n), "B%d" % (5 * s), "B%d" % (5 * s + 1)
+        a, c = "pa%d" % s, "pc%d" % s
+        tm = [T.tmp[:, s, i, 0:n] for i in range(5)]
+        tk = ["tm%d_%d" % (s, i) for i in range(5)]
+        nx, nw = bank((2, 7)[b], 160 * b + c0, n), ["B%d" % (2, 7)[b], "nx%d" % b]
+        am = "amb" if t < 2 else "amf"
         if t < R - 1:
-            mm(ps[:, o:o + HF], T.b8[0:16, :], T.mixs[0:16, h * HF:(h + 1) * HF], True, False, ["b8", "mix"], [bk, nx], c=HF)
-            mm(ps[:, o:o + HF], (T.ab if t < 2 else T.am)[:], xmine(t, h), False, False, ["ab", "am", "xo%dh%d" % (t % 2, h)], [bk, nx],
-               c=HF * (1 if t < 2 else 4))
-
-    def xbank(h):
-        return (2 * 512, 7 * 512 + 160)[h], ("B2", "B7")[h], "nx%d" % h
-
-    def newx_p(t, h):
-        cols = slice(h * HF, (h + 1) * HF)
-        o, bk, nx = xbank(h)
+            mm(nx, T.b8[0:16, :], T.mixs[0:16, cc:cc + n], True, False, ["b8", "mix"], nw)
+            mm(nx, T[am][:], direct(tab, cc, n), False, False, [am] + span(tab, cc, n), nw, wide=t >= 2)
+        d, dk = [], []
+        for j in range(M):
+            way = SIDE_V[t].get(j)
+            ap, key = T.dv[:, b, j, c0:c0 + n], span("dv%d_%d" % (b, j), c0, n)
+            bk = []
+            if way and j == 0:
+                ap, key, bk = pc, [c], [bc]
+            elif way == "p":
+                ap, key, bk = pa, [a], [ba]
+            gather(t, b, c0, n, offs(b, c0, n, j), span("un%d" % b, c0, n), way, ap, bk + key)
+            act(T.adv[:, b, j, c0:c0 + n], ap, AF.Abs, key, bk + span("adv%d_%d" % (b, j), c0, n))
+            d.append(ap)
+            dk.append(key)
+            if j == 0 and not way:
+                act(pc, ap, AF.Copy, key, [bc, c])
+            if j == 1:
+                act(tm[3], ap, AF.Relu, key, bk + [tk[3]], scale=-1.0)
+                act(tm[4], ap, AF.Relu, key, bk + [tk[4]])
+                act(pa, tm[3], AF.Copy, [tk[3]], [ba, a], scale=-1.0)
+        tt(tm[0], pc, d[2], ALU.min, [c] + dk[2], [bc, tk[0]])
+        tt(pc, pc, d[2], ALU.max, [c] + dk[2], [bc, c])
+        tt(pa, pa, tm[0], ALU.max, [a, tk[0]], [ba, a])
+        tt(tm[1], pc, tm[4], ALU.min, [c, tk[4]], [bc, tk[1]])
+        tt(pc, pa, tm[1], ALU.max, [a, tk[1]], [ba, bc, c])
+        tt(pa, pa, tm[1], ALU.min, [a, tk[1]], [ba, a])
+        tt(tm[2], pc, d[3], ALU.min, [c] + dk[3], [bc, tk[2]])
+        mo, mk = (T.mob if t < 2 else T.mof)[:, cc:cc + n], span("mo", cc, n)
         if t < R - 1:
-            mm(ps[:, o:o + HF], (T.ab if t < 2 else T.am)[:], (T.eb if t < 2 else T.ef)[:, cols], False, True, ["ab", "am", "e%d" % h],
-               [bk, nx], c=HF * (1 if t < 2 else 4))
+            tt(mo, pa, tm[2], ALU.max, [a, tk[2]], [ba] + mk)
+            nxt = "xt%d" % (t + 1)
+            mm(nx, T[am][:], mo, False, True, [am] + mk, nw, wide=t >= 2)
+            act(direct(nxt, cc, n), nx, AF.Relu, nw[1:], nw[:1] + span(nxt, cc, n))
+            send()
+            load("s", T["xo%d" % (t + 1)][:, cc:cc + n], direct(nxt, cc, n), span("xo%d" % (t + 1), cc, n), "xo%d" % (t + 1), r=span(nxt, cc, n))
         else:
-            act(T.yes[:, cols], T.ef[:, cols], AF.Square, ["e%d" % h], ["yes%d" % h])
-            mm(ps[0:16, o:o + HF], T.km[:], T.yes[:, cols], True, True, ["km", "yes%d" % h], [bk, nx], c=4 * HF)
+            tt(pa, pa, tm[2], ALU.max, [a, tk[2]], [ba, a])
+            tt(mo, pa, direct(tab, cc, n), ALU.add, [a] + span(tab, cc, n), [ba] + mk)
+            act(T.yes[:, cc:cc + n], mo, AF.Square, mk, span("yes", cc, n))
+            out = bank(5 * s + 1, 0, n, slice(0, 16))
+            mm(out, T.km[:], T.yes[:, cc:cc + n], True, True, ["km"] + span("yes", cc, n), [bc, c], wide=True)
+            act(T.yds[0:16, cc:cc + n], out, AF.Copy, [c], [bc] + span("yds", cc, n))
 
-    def newx_a(t, h):
-        cols = slice(h * HF, (h + 1) * HF)
-        o, bk, nx = xbank(h)
-        if t < R - 1:
-            act(xown(t + 1, h), ps[:, o:o + HF], AF.Relu, [nx], [bk, "xt%dh%d" % (t + 1, h)])
-            send("xt%d" % (t + 1), h * HF)
-            act(xmine(t + 1, h), ps[:, o:o + HF], AF.Relu, [nx], [bk, "xo%dh%d" % ((t + 1) % 2, h)])
-        else:
-            act(T.yds[0:16, cols], ps[0:16, o:o + HF], AF.Copy, [nx], [bk, "yds%d" % h])
-            if h == 1:
-                op("s", lambda e: e.dma_start(T.ye[:], T.yes[:]), r=["yes0", "yes1"], dma=("sto", 16))
-                op("s", lambda e: e.dma_start(T.yd[:], T.yds[0:16, :]), r=["yds0", "yds1"], dma=("sto", 32))
+    def unit_b(u):
+        b, c0, n = UNITS_B[u]
+        return b, c0, n, u % 2, n // 16, n // 4, (3, 7)[u % 2], [(o, min(128, n - o)) for o in range(0, n, 128)]
 
-    def absv(t, h, j):
-        if t < 2 and j in SIDE_V:
-            return
-        act(blk(T.adv, h, j), blk(T.dv, h, j), AF.Abs, ["dv%d_%d" % (h, j)], ["adv%d_%d" % (h, j)])
+    def tolist(out, o, n, keys, w):
+        for k0 in range(0, 16, 4):
+            mms([(out, T.dm[:, k * 128:(k + 1) * 128], T.wide[:, o + k:o + 4 * n:16], k == 0, k == 15) for k in range(k0, k0 + 4)], keys + dmk, w)
 
-    def cg(h, j):
-        return T.wide[:, h * 1280 + j * HF:h * 1280 + (j + 1) * HF]
-
-    def nr(h, j):
-        return T.wide[:, 2560 + h * 1280 + j * HF:2560 + h * 1280 + (j + 1) * HF]
-
-    def gcn(t, h, j):
-        tab, r_ = "nt%d" % t, (j + t) % M
-        act(cg(h, j), T[tab][:].indirect(lst(T.un, h, j)), AF.Copy, whole(tab) + ["un%d" % h, "mask"], ["cg%d_%d" % (h, j)],
-            scale=T.cf[:, 8 + r_:9 + r_])
-
-    def tolist(out, o, keys, w):
-        for k in range(16):
-            mm(out, T.dm[:, k * 128:(k + 1) * 128], T.wide[:, o + k:o + 1280:16], k == 0, k == 15, keys + dmk, w)
-
-    def cbank(h):
-        o = (3, 7)[h] * 512
-        return ps[:, o:o + 80], ps[:, o + 80:o + 160], "B%d" % (o // 512), o
-
-    def clist(h):
-        pc_, pt_, bk, o = cbank(h)
-        tolist(pc_, h * 1280, ["cg%d_%d" % (h, j) for j in range(M)], [bk, "cl%d" % h])
-
-    def eqs(h):
-        pc_, pt_, bk, o = cbank(h)
-        cl, n0, e0 = "cl%d" % h, h * 160, h * 560
-        cp(T.cs[:, h * 80:(h + 1) * 80], pc_, [cl], [bk, "cs%d" % h])
-        tt(T.eq[:, e0:e0 + 80], pc_, T.own[:, h * 80:(h + 1) * 80], ALU.is_equal, [cl, "own", "eqz"], [bk, "eq%d_0" % h])
+    def challengers(t, u):
+        b, c0, n, s, na, L, cb, tiles = unit_b(u)
+        tab, a0, bk = "nt%d" % t, c0 // 16, "B%d" % cb
+        for j in range(M):
+            c = s * 1280 + j * n
+            out, src, keep = T.wide[:, c:c + n], T[tab][:].indirect(offs(b, c0, n, j)), col(8 + (j + t) % M)
+            r, w = whole(tab) + span("un%d" % b, c0, n) + ["mask"], ["cg%d_%d" % (s, j)]
+            if u == 0 and j in SHARED:
+                ts(out, src, keep, None, ALU.mult, None, r, w, c=gcost(n))
+            else:
+                act(out, src, AF.Copy, r, w, scale=keep, c=gcost(n))
+        cl, pc_, pt_, cs = "cl%d" % s, bank(cb, 0, L), bank(cb, 80, L), T.cs[:, s * 80:s * 80 + L]
+        tolist(pc_, s * 1280, n, ["cg%d_%d" % (s, j) for j in range(M)], [bk, cl])
+        act(cs, pc_, AF.Copy, [cl], [bk, "cs%d" % s])
+        nk = span("nd%d" % b, c0, n)
+        tt(T.eq[:, s, 0, 0:L], pc_, T.own[:, b, :, a0:a0 + na], ALU.is_equal, [cl, "own"], [bk, "eq%d_0" % s])
         for i in range(1, M):
-            tt(T.eq[:, e0 + i * 80:e0 + (i + 1) * 80], pc_, T.nd[:, n0 + i * HL:n0 + i * HL + 80], ALU.is_equal,
-               [cl, "nd%d" % h, "ndd%d" % h], [bk, "eq%d_%d" % (h, i)])
+            tt(T.eq[:, s, i, 0:L], pc_, T.nd[:, b, i:i + 4, a0:a0 + na], ALU.is_equal, [cl] + nk + span("ndd%d" % b, c0, n), [bk, "eq%d_%d" % (s, i)])
+        tt(pt_, pc_, T.nd[:, b, 0:4, a0:a0 + na], ALU.subtract, [cl] + nk, [bk, "pt%d" % s])
         for i in range(1, M):
-            c0 = e0 + (3 + i) * 80
-            tt(T.eq[:, c0 + i * HL:c0 + 80], ps[:, o + i * HL:o + 80], T.cs[:, h * 80:(h + 1) * 80 - i * HL], ALU.is_equal,
-               [cl, "cs%d" % h], [bk, "eq%d_%d" % (h, 3 + i)])
-        tt(pt_, pc_, T.nd[:, n0:n0 + 80], ALU.subtract, [cl, "nd%d" % h], [bk, "pt%d" % h])
-
-    b4 = ps[:, 4 * 512:4 * 512 + 80]
-
-    def voids(h):
-        for i in range(7):
-            mm(b4, T.idb[:], T.eq[:, h * 560 + i * 80:h * 560 + (i + 1) * 80], i == 0, i == 6, ["idb", "eqz", "eq%d_%d" % (h, i)], ["B4", "b4"])
-        act(T.nv[:, h * 80:(h + 1) * 80], b4, AF.Relu, ["b4"], ["B4", "nv%d" % h], bias=1.0, scale=-1.0)
-
-    def chal(h, i):
-        pc_, pt_, bk, o = cbank(h)
-        cols = slice(h * 80, (h + 1) * 80)
-        if i == 0:
-            tt(pt_, pt_, T.nv[:, cols], ALU.mult, ["pt%d" % h, "nv%d" % h], [bk, "pt%d" % h])
-        elif i == 1:
-            tt(T.cn[:, cols], pt_, T.nd[:, h * 160:h * 160 + 80], ALU.add, ["pt%d" % h, "nd%d" % h], [bk, "cn%d" % h])
-        else:
-            cp(T.uc[:, cols], T.cn[:, cols], ["cn%d" % h], ["uc%d" % h])
-
-    def gu(t, h, j):
-        tab = "xt%d" % t
-        if t < 2 and j in SIDE_U:
-            return
-        tt(blk(T.du, 0, j), T[tab][:].indirect(lst(T.uc, h, j)), xmine(t, h), ALU.subtract,
-           whole(tab) + ["uc%d" % h, "xo%dh%d" % (t % 2, h)], ["du%d" % j])
-
-    def absu(t, h, j):
-        if t < 2 and j in SIDE_U:
-            out, bk = ps[:, (j % 2) * 512:(j % 2) * 512 + HF], "B%d" % (j % 2)
-            side(t, lst(T.uc, h, j), "uc%d" % h, h, 2, out, bk, "au%d" % j)
-            act(out, out, AF.Abs, ["au%d" % j], [bk, "au%d" % j])
-            return
-        act(ps[:, (j % 2) * 512:(j % 2) * 512 + HF], blk(T.du, 0, j), AF.Abs, ["du%d" % j], ["B%d" % (j % 2), "au%d" % j])
-
-    def cmpr(h, j):
-        tt(nr(h, j), ps[:, (j % 2) * 512:(j % 2) * 512 + HF], blk(T.adv, h, j), ALU.is_lt, ["au%d" % j, "adv%d_%d" % (h, j)],
-           ["B%d" % (j % 2), "nr%d_%d" % (h, j)])
-
-    def difff(t, h):
-        if t == R - 1:
-            return
-        for i, (o, n) in enumerate(TILES):
-            out = ps[0:n, 6 * 512 + i * 64:6 * 512 + (i + 1) * 64]
-            c0 = base + h * HF + o
-            mm(out, T["nt%d" % t][:, c0:c0 + n], T.gn[:], True, False, ["nt%dh%d" % (t, h), "gn"], ["B6", "df"])
-            for j in range(M):
-                c1 = h * 1280 + j * HF + o
-                mm(out, T.wide[:, c1:c1 + n], T.gdf[:, 6 - 2 * j:70 - 2 * j], False, j == M - 1, ["cg%d_%d" % (h, j), "gdf"], ["B6", "df"])
-
-    def fbank(h, i):
-        b = (5, 4, 3)[i] if h else 5
-        return b, b * 512 + 256 * (b != 5) + i * 64
-
-    def countf(t, h, js):
-        if t == R - 1:
-            return
-        for i, (o, n) in enumerate(TILES):
-            b, c0 = fbank(h, i)
-            for j in js:
-                c1 = 2560 + h * 1280 + j * HF + o
-                mm(ps[0:n, c0:c0 + 64], T.wide[:, c1:c1 + n], T.gcf[:, 6 - 2 * j:70 - 2 * j], j == 0, j == M - 1,
-                   ["nr%d_%d" % (h, j), "gcf"], ["B%d" % b, "cf_%d" % i])
+            tt(T.eq[:, s, 3 + i, i * na:L], bank(cb, i * na, L - i * na), T.cs[:, s * 80:s * 80 + L - i * na], ALU.is_equal,
+               [cl, "cs%d" % s], [bk, "eq%d_%d" % (s, 3 + i)])
+        mm(bank(4, 0, L), T.idf[:], cs, True, False, ["idf", "cs%d" % s], ["B4", "bv"], wide=True)
+        for part in ((0, 1, 2, 3), (4, 5), (6,)):
+            mms([(bank(4, max(0, i - 3) * na, L - max(0, i - 3) * na), T.far[:], T.eq[:, s, i, max(0, i - 3) * na:L], False, i == 6) for i in part],
+                ["far"] + ["eq%d_%d" % (s, i) for i in part], ["B4", "bv"])
+        ts(T.uc[:, s * 80:s * 80 + L], bank(4, 0, L), float(W), None, ALU.min, None, ["bv"], ["B4", "uc%d" % s])
 
     def wins(out, src, r, w):
         act(out, src, AF.Sigmoid, r, w, bias=-2176.0, scale=256.0)
 
-    def winf(t, h):
-        if t < R - 1 and h == 0:
-            wins(T.wf[:], ps[:, 5 * 512:5 * 512 + 192], ["cf_2"], ["B5", "wf"])
-        elif t < R - 1:
-            for i, (o, n) in enumerate(TILES):
-                b, c0 = fbank(h, i)
-                wins(T.wf[0:n, i * 64:(i + 1) * 64], ps[0:n, c0:c0 + 64], ["cf_%d" % i], ["B%d" % b, "wf", "wg"])
+    def challenge(t, u):
+        b, c0, n, s, na, L, cb, tiles = unit_b(u)
+        a0, bk, wd, cc = c0 // 16, "B%d" % cb, 64 * len(tiles), b * HF + c0
+        tab, nxt = "nt%d" % t, "nt%d" % (t + 1)
+        more = t < R - 1
+        if more:
+            for i, (o, m) in enumerate(tiles):
+                out = bank(6, i * 64, 64, slice(0, m))
+                c = s * 1280 + o
+                mms([(out, direct(tab, cc + o, m), T.gn[:], True, False)]
+                    + [(out, T.wide[:, c + j * n:c + j * n + m], T.gdf[:, 6 - 2 * j:70 - 2 * j], False, j == M - 1) for j in range(M)],
+                    span(tab, cc + o, m) + ["gn", "gdf"] + ["cg%d_%d" % (s, j) for j in range(M)], ["B6", "df"])
+            mm(bank(2, 0, n), T.idb[:], direct(tab, cc, n), True, False, ["idb"] + span(tab, cc, n), ["B2", "b2"])
+            mm(bank(5, 0, wd), T.idb[:], T.zb[:, 0:wd], True, False, ["idb", "zb"], ["B5", "cf_"])
+        for j in range(M):
+            way = SIDE_U[t].get(j)
+            au, ab, ak = bank(j % 2, 0, n), "B%d" % (j % 2), "au%d" % (j % 2)
+            off = T.uc[:, s * 80 + j * na:s * 80 + (j + 1) * na]
+            if way == "p":
+                gather(t, b, c0, n, off, ["uc%d" % s], way, au, [ab, ak])
+                act(au, au, AF.Abs, [ak], [ab, ak])
+            else:
+                gather(t, b, c0, n, off, ["uc%d" % s], way, T.du[:, j, 0:n], ["du%d" % j])
+                act(au, T.du[:, j, 0:n], AF.Abs, ["du%d" % j], [ab, ak])
+            c = 2560 + s * 1280 + j * n
+            tt(T.wide[:, c:c + n], au, T.adv[:, b, j, c0:c0 + n], ALU.is_lt, [ak] + span("adv%d_%d" % (b, j), c0, n), [ab, "nr%d_%d" % (s, j)])
+            if more:
+                mms([(bank(5, i * 64, 64, slice(0, m)), T.wide[:, c + o:c + o + m], T.gcf[:, 6 - 2 * j:70 - 2 * j], False, j == M - 1 and i == 0)
+                     for i, (o, m) in list(enumerate(tiles))[::-1]],
+                    ["nr%d_%d" % (s, j), "gcf"], ["B5", "cf_"])
+        if more:
+            wins(T.wf[:, 0:wd], bank(5, 0, wd), ["cf_"], ["B5", "wf"])
+            tt(T.tf[:, 0:wd // 8, 0:8], bank(6, 0, wd), T.wf[:, 0:wd], ALU.mult, ["df", "wf"], ["B6", "tf"])
+            mms([(bank(2, o, m), T.tf[0:m, 8 * i:8 * i + 8, :], T.idb[0:m, 0:m], False, i == len(tiles) - 1) for i, (o, m) in enumerate(tiles)],
+                ["tf", "idb"], ["B2", "b2"])
+            act(direct(nxt, cc, n), bank(2, 0, n), AF.Copy, ["b2"], ["B2"] + span(nxt, cc, n))
+            send()
+        tolist(bank(4, 80, L), 2560 + s * 1280, n, ["nr%d_%d" % (s, j) for j in range(M)], ["B4", "bc"])
+        wl, pt_, nd = T.wl[:, s * 80:s * 80 + L], bank(cb, 80, L), T.nd[:, b, 0:4, a0:a0 + na]
+        nk = span("nd%d" % b, c0, n)
+        wins(wl, bank(4, 80, L), ["bc"], ["B4", "wl%d" % s])
+        tt(pt_, pt_, wl, ALU.mult, ["pt%d" % s, "wl%d" % s], [bk, "pt%d" % s])
+        if more:
+            tt(nd, pt_, nd, ALU.add, ["pt%d" % s] + nk, [bk] + nk)
+            cp(T.un[:, b, :, a0:a0 + na], nd, nk, span("un%d" % b, c0, n))
+            act(T.nd[:, b, 4:7, a0:a0 + na], T.nd[:, b, 0:3, a0:a0 + na], AF.Copy, nk, span("ndd%d" % b, c0, n))
+        else:
+            tt(T.yns[:, :, b * HL + a0:b * HL + a0 + na], pt_, nd, ALU.add, ["pt%d" % s] + nk, [bk] + span("yns", cc, n))
 
-    def pickf(t):
-        if t < R - 1:
-            tt(T.tf[:, :, 0:8], ps[:, 6 * 512:6 * 512 + 192], T.wf[:], ALU.mult, ["df", "wf"], ["B6", "tf"])
-
-    def rows_p(t, h, first):
-        if t == R - 1:
-            return
-        if first:
-            c0 = base + h * HF
-            mm(b2, T.idb[:], T["nt%d" % t][:, c0:c0 + HF], True, False, ["idb", "nt%dh%d" % (t, h)], ["B2", "b2"], c=HF)
-            return
-        for i, (o, n) in enumerate(TILES):
-            mm(ps[:, 2 * 512 + o:2 * 512 + o + n], T.tf[0:n, 8 * i:8 * i + 8, :], T.idb[0:n, 0:n], False, i == 2, ["tf", "idb"], ["B2", "b2"], c=n)
-
-    def rows_a(t, h):
-        if t < R - 1:
-            c0 = base + h * HF
-            act(T["nt%d" % (t + 1)][:, c0:c0 + HF], b2, AF.Copy, ["b2"], ["B2", "nt%dh%d" % (t + 1, h)])
-            send("nt%d" % (t + 1), h * HF)
-
-    def countl(h):
-        tolist(b4, 2560 + h * 1280, ["nr%d_%d" % (h, j) for j in range(M)], ["B4", "b4"])
-
-    def winl(h):
-        wins(T.wl[:, h * 80:(h + 1) * 80], b4, ["b4"], ["B4", "wl%d" % h])
-
-    def pickl(t, h, i):
-        pc_, pt_, bk, o = cbank(h)
-        n_ = T.nd[:, h * 160:h * 160 + 80]
-        if i == 0:
-            tt(pt_, pt_, T.wl[:, h * 80:(h + 1) * 80], ALU.mult, ["pt%d" % h, "wl%d" % h], [bk, "pt%d" % h])
-        elif i == 1 and t == R - 1:
-            tt(T.yns[:, :, h * HL:(h + 1) * HL], pt_, n_, ALU.add, ["pt%d" % h, "nd%d" % h], [bk, "yns%d" % h])
-        elif i == 1:
-            tt(n_, pt_, n_, ALU.add, ["pt%d" % h, "nd%d" % h], [bk, "nd%d" % h])
-        elif t < R - 1:
-            cp(T.un[:, h * 80:(h + 1) * 80], n_, ["nd%d" % h], ["un%d" % h])
-            dup(h)
-
-    dup(0)
-    dup(1)
     for t in range(R):
-        u = t - 1
-        if t:
-            winf(u, 1)
-        gv(t, 0, 0); prep(t, 0, 0)
-        if t:
-            pickf(u); rows_p(u, 1, False); countl(1); rows_a(u, 1)
-        gv(t, 0, 1); prep(t, 0, 1)
-        gv(t, 0, 2); prep(t, 0, 2); prep(t, 0, 3); gv(t, 0, 3)
-        if t:
-            winl(1)
-        mixin(t, 0)
-        for j in range(M):
-            absv(t, 0, j)
-        med(t, 0, 0); med(t, 0, 1); med(t, 0, 2)
-        if t:
-            pickl(u, 1, 0)
-        med(t, 0, 3)
-        if t:
-            pickl(u, 1, 1)
-        med(t, 0, 4)
-        if t:
-            pickl(u, 1, 2)
-        med(t, 0, 5); gv(t, 1, 0); prep(t, 1, 0); med(t, 0, 6); gv(t, 1, 1); med(t, 0, 7)
-        prep(t, 1, 1); prep(t, 1, 2); prep(t, 1, 3)
-        gv(t, 1, 2); med(t, 0, 8); newx_p(t, 0); gv(t, 1, 3)
-        for j in range(M):
-            absv(t, 1, j)
-        newx_a(t, 0); mixin(t, 1)
-        for i in range(9):
-            med(t, 1, i)
-        for j in range(M):
-            gcn(t, 0, j)
-        newx_p(t, 1); clist(0); newx_a(t, 1); gcn(t, 1, 0)
-        eqs(0); voids(0); chal(0, 0); gcn(t, 1, 1); chal(0, 1); chal(0, 2); difff(t, 0); rows_p(t, 0, True)
-        gu(t, 0, 0); absu(t, 0, 0); gcn(t, 1, 2); gu(t, 0, 1); absu(t, 0, 1); gcn(t, 1, 3); clist(1); cmpr(0, 0)
-        gu(t, 0, 2); absu(t, 0, 2); cmpr(0, 1); gu(t, 0, 3); absu(t, 0, 3); eqs(1); voids(1); cmpr(0, 2)
-        cmpr(0, 3); chal(1, 0); countf(t, 0, range(M)); countl(0); chal(1, 1); chal(1, 2)
-        gu(t, 1, 0); absu(t, 1, 0); winf(t, 0); gu(t, 1, 1); absu(t, 1, 1); winl(0); pickf(t); rows_p(t, 0, False); difff(t, 1); cmpr(1, 0)
-        gu(t, 1, 2); absu(t, 1, 2); rows_a(t, 0); pickl(t, 0, 0); cmpr(1, 1); pickl(t, 0, 1)
-        gu(t, 1, 3); absu(t, 1, 3); rows_p(t, 1, True); countf(t, 1, [0, 1]); pickl(t, 0, 2)
-        cmpr(1, 2); countf(t, 1, [2]); cmpr(1, 3); countf(t, 1, [3])
-    countl(1); winl(1); pickl(R - 1, 1, 0); pickl(R - 1, 1, 1)
-    op("s", lambda e: e.dma_start(T.yn[:], T.yns[:]), r=["yns0", "yns1"], dma=("sto", 48))
-    finish([("sto", 48), ("sent", sent[0]), ("ldx", 16), ("ldo", 16), ("ldn", 16), ("ldm", 16)])
+        if "s" in list(SIDE_V[t].values()) + list(SIDE_U[t].values()):
+            for b in range(2):
+                act(bank(3 + b, 160, HF), direct("xt%d" % t, b * HF, HF), AF.Copy, span("xt%d" % t, b * HF, HF), ["B%d" % (3 + b), "xf%d" % b])
+        for u in range(len(UNITS_A)):
+            medians(t, u)
+        if t == R - 1:
+            load("s", T.ye[:], T.yes[:], [], "sto", r=span("yes", 0, F))
+            load("s", T.yd[:], T.yds[0:16, :], [], "sto", r=span("yds", 0, F))
+        challengers(t, 0)
+        for u in range(len(UNITS_B)):
+            if u + 1 < len(UNITS_B):
+                challengers(t, u + 1)
+            challenge(t, u)
+    load("s", T.yn[:], T.yns[:], [], "sto", r=span("yns", 0, F))
+    finish([("sent", sent[0])])

@@ -8,9 +8,11 @@ XD = ["bfloat16", "bfloat16", "float32", "float32", "float32"]
 
 UNITS_A = [(0, 0, 320), (1, 0, 192), (1, 192, 128)]
 UNITS_B = [(0, 0, 320), (1, 0, 320)]
-SIDE_V = [{0: "p"}, {0: "p"}, {0: "s", 3: "s"}, {0: "s", 3: "s"}, {0: "s", 3: "s"}]
+PARTS = [[(0, 320)], [(0, 320)]]
+SIDE_V = [{0: "p", 1: "p"}, {0: "p", 1: "p"}, {0: "s", 3: "s"}, {0: "s", 3: "s"}, {0: "s", 3: "s"}]
+SIDE_F = [{0: "p", 1: "p"}, {0: "p"}, {3: "s"}, {3: "s"}, {3: "s"}]
 SIDE_U = [{3: "p"}, {3: "p"}, {3: "s"}, {3: "s"}, {3: "s"}]
-SHARED = (0,)
+SHARED = (0, 1)
 
 SCRATCH = {
     "nbi": ("sbuf", [128, 4, 40], "int32"), "pti": ("sbuf", [128, 8, 40], "int32"), "ptb": ("sbuf", [128, 320], "bfloat16"),
@@ -37,16 +39,20 @@ for _t in range(R):
     SCRATCH["nt%d" % _t] = ("sbuf", [128, W], "bfloat16")
     SCRATCH["xo%d" % _t] = ("sbuf", [128, F], XD[_t])
 
-EVENTS = [("xt0", 0, F, "late"), ("nt0", 0, F, "early")]
+EVENTS = [("xt0", 0, HF, "a"), ("xt0", HF, HF, "b"), ("nt0", 0, F, "a")]
 for _t in range(1, R):
-    EVENTS += [("xt%d" % _t, u[0] * HF + u[1], u[2], "late" if u == UNITS_A[-1] else "early") for u in UNITS_A]
-    EVENTS += [("nt%d" % _t, u[0] * HF + u[1], u[2], "late" if u == UNITS_B[-1] else "mate") for u in UNITS_B]
+    EVENTS += [("xt%d" % _t, u[0] * HF + u[1], u[2], "ab"[UNITS_A.index(u) % 2]) for u in UNITS_A]
+    EVENTS += [("nt%d" % _t, u[0] * HF + u[1] + o, n, ("c", "a" if (o, n) == ps_[-1] else "b")[u[0]]) for u, ps_ in zip(UNITS_B, PARTS) for o, n in ps_]
+WAYS = {"a": [(None, 0), (None, 2), ("own", None), ("other", None), ("other", None)],
+        "b": [(None, 1), (None, 3), ("own", None), ("other", None), ("other", None)],
+        "c": [(None, None), (None, 0), ("other", 1), ("other", 2), ("other", 3)]}
+ROUTES = []
 
-GATHER, HAND, FLY, LOCAL = (65, 1.6), 140, (4200, 3.5, 4000), 2300
-SPEEDS = [(1.2, 1.2), (1.6, 1.0), (2.0, 0.75)]
-SHIFT, SLACK = 1500, 500
+GATHER, HAND, FLY, LOCAL = (65, 1.6), 260, (4200, 2.8, 4000), 2300
+SPEEDS = [(1.2, 1.2, 320), (1.6, 1.0, 260), (2.0, 0.8, 180)]
+SHIFT, SLACK, POLISH, EASE = 1500, 500, 24000, 100
 SAME = {"au0": ["pa0"], "au1": ["pc0"], "rows0": ["pa0"], "rows1": ["pc0"], "cf_": ["pa1"], "df": ["pc1"], "b2": ["nx0"]}
-TURNS, TRIES, ORDER = 4, 2500, []
+TURNS, TRIES, ORDER = 4, 300, []
 SEMAPHORES = (["sv", "sa", "sp", "sg", "ldx", "ldn", "ldm", "sto", "sent"] + ["xo%d" % t for t in range(R)]
               + ["e%s_%d" % e[:2] for e in EVENTS])
 
@@ -56,34 +62,42 @@ def ones(m):
 
 
 def routes(T, topo):
+    if ROUTES:
+        return ROUTES
     cores = list(T.cores)
-    cross = lambda s, ds: sum(1 for d in ds if not topo.same_plane(cores[s], cores[(s + d) % N]))
-    pairs = [(a, b) for a in range(1, N) for b in range(a + 1, N)]
-    two = min(pairs, key=lambda p: max(max(cross(s, p), cross(s, [d for d in range(1, N) if d not in p])) for s in range(N)))
-    three = [d for d in range(1, N) if d not in two]
-    out = []
-    for s, c in enumerate(cores):
-        mates_ = [h for h in topo.cores_of(c) if h != c]
-        ways = {}
-        for last in (False, True):
-            straight, helped = (three[:2], list(two) + three[2:]) if last else (list(two), three)
-            way, used = [((s + d) % N, None) for d in straight], []
-            dies = [True, True, not last]
-            order = sorted(range(3), key=lambda i: topo.same_plane(c, cores[(s + helped[i]) % N]))
-            for i in order:
-                to = cores[(s + helped[i]) % N]
-                able = [h for h in mates_ if (topo.die(h) != topo.die(c)) == dies[i] and topo.may_write(h, to)]
-                able.sort(key=lambda h: (used.count(h), all(topo.may_write(h, x) for x in cores if x != c) and topo.same_plane(c, to)))
-                used.append(able[0])
-                way.append(((s + helped[i]) % N, able[0]))
-            ways["late" if last else "early"] = way
-        way = [((s + two[0]) % N, None)]
-        for i, d in enumerate(d for d in range(1, N) if d != two[0]):
-            to = cores[(s + d) % N]
-            way.append(((s + d) % N, [h for h in range(WORLD) if topo.mates(h, to) and topo.may_write(h, to)][i]))
-        ways["mate"] = way
-        out.append(ways)
-    return out
+    beside = [[h for h in range(WORLD) if topo.mates(h, c) and topo.may_write(h, c)] for c in cores]
+    firsts = sorted(set(topo.cores_of(c)[0] for c in range(WORLD)))
+    mate = {a: b for a in firsts for b in firsts if topo.mates(a, b)}
+
+    def deal(roles, ds):
+        ways, load = [], {}
+        for s, c in enumerate(cores):
+            way, used = [], []
+            legs = [(die, ([] if relay is None else [beside[(s + d) % N][relay]]) + [cores[(s + d) % N]]) for (die, relay), d in zip(roles, ds)]
+            for die, path in sorted(legs, key=lambda x: topo.same_plane(c, x[1][0])):
+                if die:
+                    able = [h for h in topo.cores_of(c) if h != c and (topo.die(h) == topo.die(c)) == (die == "own") and topo.may_write(h, path[0])]
+                    used.append(min(able, key=lambda h: (h in used, all(topo.may_write(h, x) for x in cores if x != c) and topo.same_plane(c, path[0]))))
+                    path = used[-1:] + path
+                path = [c] + path
+                for a, b in zip(path, path[1:]):
+                    links, here = [], topo.cores_of(a)[0]
+                    if a not in topo.cores_of(b) and not topo.same_plane(a, b):
+                        links.append(("mate", here))
+                        here = mate[here]
+                    if here not in topo.cores_of(b):
+                        links += [("out", here), ("in", topo.cores_of(b)[0])]
+                    for k in links:
+                        load[k, topo.die(a)] = load.get((k, topo.die(a)), 0) + 1
+                way.append(path)
+            ways.append(way)
+        return sorted(load.values(), reverse=True), ways
+
+    def orders(left):
+        return [[d] + rest for d in left for rest in orders([x for x in left if x != d])] if left else [[]]
+    best = {k: min((deal(roles, ds) for ds in orders(list(range(1, N)))), key=lambda x: x[0])[1] for k, roles in WAYS.items()}
+    ROUTES.extend({k: best[k][s] for k in WAYS} for s in range(N))
+    return ROUTES
 
 
 def piece(T, ev, rank):
@@ -101,10 +115,11 @@ def helper_program(g, core, T, topo, rts):
     sent = 0
     for ev in EVENTS:
         for rank in range(N):
-            dsts = [cores[d] for d, h in rts[rank][ev[3]] if h == core]
-            if dsts:
+            paths = [p for p in rts[rank][ev[3]] if core in p]
+            if paths:
+                dsts = [p[p.index(core) + 1] for p in paths]
                 far = topo.mask(core, dsts[0])
-                g.wait_ge(T.sem["e%s_%d" % ev[:2]], ones(far if ev[3] == "mate" else topo.mask(cores[rank], core) & ~far))
+                g.wait_ge(T.sem["e%s_%d" % ev[:2]], ones(topo.mask(paths[0][paths[0].index(core) - 1], core) & ~far or far))
                 g.remote_dma_fused([transfer(T, topo, core, dsts, ev, rank, far)], local_sem=T.sem.sent)
                 sent += ones(far)
     if sent:
@@ -259,28 +274,33 @@ def make_emitter(g, T):
             key = [-x for x in late]
             done = run(pre, key, False)
             order = sorted(range(n_), key=lambda i: (done[i] - length[i], i))
-            return sum(replay(order, *s) for s in speeds) / len(speeds), key, done
+            return sum(max(replay(order, *s)[0]) for s in speeds) / len(speeds), key, done
 
-        def replay(order, long_, slow):
-            done, free, who = [0] * n_, {k: 0 for k in spots_}, {}
-            for i in order:
-                at = 0
-                for d, lag in pre[i].items():
-                    x = done[d] + (lag * slow if lag > 1000 else lag)
-                    if x > at:
-                        at = x
+        def replay(order, long_, hold, waits, hand, first=0, known_=None):
+            done, why = (list(known_[0]), list(known_[1])) if known_ else ([0] * n_, [-1] * n_)
+            free, who = {k: 0 for k in spots_}, {k: -1 for k in spots_}
+            for i in order[max(0, first - 150):first]:
+                for k in uses[i]:
+                    free[k], who[k] = done[i] - long_[i] + hold[i], i
+            for i in order[first:]:
+                at, by = 0, -1
+                for d, lag in waits[i]:
+                    if done[d] + lag > at:
+                        at, by = done[d] + lag, d
                 e = eng[i]
                 for k in uses[i]:
-                    x = free[k] if who.get(k, e) == e else free[k] + HAND
+                    x = free[k] if eng[who[k]] == e or who[k] < 0 else free[k] + hand
                     if x > at:
-                        at = x
-                done[i] = at + long_[i]
+                        at, by = x, who[k]
+                done[i], why[i] = at + long_[i], by
                 for k in uses[i]:
-                    free[k], who[k] = at + (long_[i] if busy[i] == length[i] else busy[i]), e
-            return max(done)
+                    free[k], who[k] = at + hold[i], i
+            return done, why
 
         speeds = [([x * slow if c[0] == "l" or c[4] else (x - GATHER[0]) * quick / GATHER[1] + GATHER[0] if isinstance(x, float) else x
-                    for x, c in zip(length, calls)], slow) for quick, slow in SPEEDS]
+                    for x, c in zip(length, calls)], slow, hand) for quick, slow, hand in SPEEDS]
+        speeds = [(long_, [x if b == y else b for x, y, b in zip(long_, length, busy)],
+                   [[(d, hand if lag == HAND else lag * slow) for d, lag in p.items()] for p in pre], hand) for long_, slow, hand in speeds]
 
         if not ORDER:
             best = improve([-x for x in rest])
@@ -300,7 +320,34 @@ def make_emitter(g, T):
                     last = trial
                 best = min(best, last)
             order = sorted(range(n_), key=lambda i: (best[2][i] - length[i], i))
-            ORDER.append((best[0], order, best[1], best[2], kind, max(rest), pre, length))
+            now = top = (best[0], order)
+            runs = [replay(order, *s) for s in speeds]
+            for turn in range(POLISH):
+                done, why = runs[turn % len(speeds)]
+                held, i = [], done.index(max(done))
+                while why[i] >= 0:
+                    if why[i] not in pre[i]:
+                        held.append((why[i], i))
+                    i = why[i]
+                if not held:
+                    continue
+                a, b = held[int(draw() * len(held))]
+                at, to = now[1].index(a), now[1].index(b)
+                ahead = {b}
+                for i in now[1][to - 1:at - 1 if at else None:-1]:
+                    if any(j in ahead for j in back[i]):
+                        ahead.add(i)
+                if a in ahead:
+                    continue
+                between = now[1][at:to + 1]
+                order = now[1][:at] + [i for i in between if i in ahead] + [i for i in between if i not in ahead] + now[1][to + 1:]
+                trial = [replay(order, *s, at, k) for s, k in zip(speeds, runs)]
+                span = sum(max(x[0]) for x in trial) / len(speeds)
+                if span <= now[0] + EASE * (1.0 - turn / POLISH):
+                    now, runs = (span, order), trial
+                    top = min(top, now)
+            done = replay(top[1], *speeds[len(speeds) // 2])[0]
+            ORDER.append((top[0], top[1], best[1], done, kind, max(rest), pre, length))
         for i in ORDER[0][1]:
             if eng[i] != "l":
                 op(*calls[i][:5])
@@ -326,7 +373,7 @@ def rank_program(g, core, T, topo):
     base = rank * F
     sent, turn = [0], [0]
     for ev in EVENTS:
-        n = sum(ones(topo.mask(cores[s] if h is None else h, core)) for s in range(N) for d, h in rts[s][ev[3]] if d == rank)
+        n = sum(ones(topo.mask(p[-2], core)) for s in range(N) for p in rts[s][ev[3]] if p[-1] == core)
         outside("far%s_%d" % ev[:2], "e%s_%d" % ev[:2], n)
 
     def span(name, c0, n):
@@ -335,16 +382,18 @@ def rank_program(g, core, T, topo):
     def send():
         ev = EVENTS[turn[0]]
         turn[0] += 1
-        mine = [cores[d] for d, h in rts[rank][ev[3]] if h is None]
-        handed = sorted(set(h for d, h in rts[rank][ev[3]] if h is not None), key=lambda h: topo.die(h) == topo.die(core))
+        paths = sorted(rts[rank][ev[3]], key=lambda p: (-len(p), topo.die(p[1]) == topo.die(core)))
+        handed = []
+        for p in paths:
+            if p[1] in topo.cores_of(core) and p[1] not in handed:
+                handed.append(p[1])
+        mine = [p[1] for p in paths if p[1] not in handed]
         far = topo.mask(core, mine[0])
-        near = topo.mask(core, handed[0]) & ~far
         time, lag = FLY[1] * ev[2] * (4 if ev[0] in ("xt2", "xt3", "xt4") else 2), FLY[0] + FLY[2] * (turn[0] == 1)
-        if near:
-            tr = [transfer(T, topo, core, mine, ev, rank, far), transfer(T, topo, core, handed, ev, rank, near)]
-        else:
-            tr, time, lag = [transfer(T, topo, core, handed + mine, ev, rank, far)], time / 4, lag + 2 * time
-        sent[0] += ones(far) + ones(near)
+        tr = [transfer(T, topo, core, mine, ev, rank, far), transfer(T, topo, core, handed, ev, rank, topo.mask(core, handed[0]) & ~far)]
+        if len(paths[0]) == 4:
+            time, lag = time / 2, lag * 1.5 + time
+        sent[0] += ones(far) * len(tr)
         op("g", lambda e: e.remote_dma_fused(tr, local_sem=T.sem.sent), r=span(ev[0], ev[1], ev[2]), w=["sends"], dma="remote", kind="send")
         op("l", None, r=["sends"], w=["links"], c=time, far=[("far%s_%d" % ev[:2], lag)], kind="link")
 
@@ -403,13 +452,15 @@ def rank_program(g, core, T, topo):
     fl = dict(allow_small_or_imprecise_dtypes=True)
     op("g", lambda e: e.iota(T.pi[:, 0:1], [[0, 1]], 0, 1), w=["pi0"], c=160)
     op("g", lambda e: e.iota(T.ci[:], [[1, 128]], 0, 0, **fl), w=["ci"], c=420)
-    op("g", lambda e: e.iota(T.cm[:], [[0, 8], [1, 16]], 0, 0, **fl), w=["cm"], c=420)
-    op("g", lambda e: e.iota(T.ch[:], [[1, 36], [0, 2]], 0, 0, **fl), w=["ch"], c=300)
-    op("g", lambda e: e.iota(T.own[:], [[HF, 2], [0, 4], [16, HL]], base, 1, **fl), w=["own"], c=480)
     send()
+    send()
+    op("g", lambda e: e.iota(T.cm[:], [[0, 8], [1, 16]], 0, 0, **fl), r=["sends"], w=["cm"], c=420)
+    op("g", lambda e: e.iota(T.ch[:], [[1, 36], [0, 2]], 0, 0, **fl), r=["sends"], w=["ch"], c=300)
+    op("g", lambda e: e.iota(T.own[:], [[HF, 2], [0, 4], [16, HL]], base, 1, **fl), r=["sends"], w=["own"], c=480)
     fill(T.dm[:], 0.0, ["dmz"])
     fill(T.tf[:], 0.0, ["tf"])
-    fill(T.zb[:], 0.0, ["zb"])
+    fill(T.zb[:, 0:64], 0.0, ["zb"])
+    act(T.zb[:, 64:192], T.ci[:], AF.Sigmoid, ["ci"], ["zc"], bias=-2176.0, c=1700)
     fill(bank(6, 128, 64), 0.0, ["B6", "df"])
     for t in range(R):
         fill(T["xt%d" % t][:, W:W + 16], 1024.0, ["padxt%d" % t])
@@ -497,7 +548,7 @@ def rank_program(g, core, T, topo):
             mm(nx, T[am][:], direct(tab, cc, n), False, False, [am] + span(tab, cc, n), nw, wide=t >= 2)
         d, dk = [], []
         for j in range(M):
-            way = SIDE_V[t].get(j)
+            way = (SIDE_V if u else SIDE_F)[t].get(j)
             ap, key = T.dv[:, b, j, c0:c0 + n], span("dv%d_%d" % (b, j), c0, n)
             bk = []
             if way and j == 0:
@@ -539,7 +590,7 @@ def rank_program(g, core, T, topo):
 
     def unit_b(u):
         b, c0, n = UNITS_B[u]
-        return b, c0, n, u % 2, n // 16, n // 4, (3, 7)[u % 2], [(o, min(128, n - o)) for o in range(0, n, 128)]
+        return b, c0, n, u % 2, n // 16, n // 4, (3, 7)[u % 2], [(o, min(128, o0 + n0 - o)) for o0, n0 in PARTS[u] for o in range(o0, o0 + n0, 128)]
 
     def tolist(out, o, n, keys, w):
         for k0 in range(0, 16, 4):
@@ -588,31 +639,36 @@ def rank_program(g, core, T, topo):
                 mms([(out, direct(tab, cc + o, m), T.gn[:], True, False)]
                     + [(out, T.wide[:, c + j * n:c + j * n + m], T.gdf[:, 6 - 2 * j:70 - 2 * j], False, j == M - 1) for j in range(M)],
                     span(tab, cc + o, m) + ["gn", "gdf"] + ["cg%d_%d" % (s, j) for j in range(M)], ["B6", "df"])
-            mm(bank(2, 0, n), T.idb[:], direct(tab, cc, n), True, False, ["idb"] + span(tab, cc, n), ["B2", "b2"])
-            mm(bank(5, 0, wd), T.idb[:], T.zb[:, 0:wd], True, False, ["idb", "zb"], ["B5", "cf_"])
-        for j in range(M):
-            way = SIDE_U[t].get(j)
-            au, ab, ak = bank(j % 2, 0, n), "B%d" % (j % 2), "au%d" % (j % 2)
-            off = T.uc[:, s * 80 + j * na:s * 80 + (j + 1) * na]
-            if way == "p":
-                gather(t, b, c0, n, off, ["uc%d" % s], way, au, [ab, ak])
-                act(au, au, AF.Abs, [ak], [ab, ak])
-            else:
-                gather(t, b, c0, n, off, ["uc%d" % s], way, T.du[:, j, 0:n], ["du%d" % j])
-                act(au, T.du[:, j, 0:n], AF.Abs, ["du%d" % j], [ab, ak])
-            c = 2560 + s * 1280 + j * n
-            tt(T.wide[:, c:c + n], au, T.adv[:, b, j, c0:c0 + n], ALU.is_lt, [ak] + span("adv%d_%d" % (b, j), c0, n), [ab, "nr%d_%d" % (s, j)])
+        for o0, n0 in (PARTS[u] if more else [(0, n)]):
+            some = [(i, o, m) for i, (o, m) in enumerate(tiles) if o0 <= o < o0 + n0]
+            w0, wd, tk = 64 * some[0][0], 64 * len(some), "%d" % some[0][0]
             if more:
-                mms([(bank(5, i * 64, 64, slice(0, m)), T.wide[:, c + o:c + o + m], T.gcf[:, 6 - 2 * j:70 - 2 * j], False, j == M - 1 and i == 0)
-                     for i, (o, m) in list(enumerate(tiles))[::-1]],
-                    ["nr%d_%d" % (s, j), "gcf"], ["B5", "cf_"])
-        if more:
-            wins(T.wf[:, 0:wd], bank(5, 0, wd), ["cf_"], ["B5", "wf"])
-            tt(T.tf[:, 0:wd // 8, 0:8], bank(6, 0, wd), T.wf[:, 0:wd], ALU.mult, ["df", "wf"], ["B6", "tf"])
-            mms([(bank(2, o, m), T.tf[0:m, 8 * i:8 * i + 8, :], T.idb[0:m, 0:m], False, i == len(tiles) - 1) for i, (o, m) in enumerate(tiles)],
-                ["tf", "idb"], ["B2", "b2"])
-            act(direct(nxt, cc, n), bank(2, 0, n), AF.Copy, ["b2"], ["B2"] + span(nxt, cc, n))
-            send()
+                mm(bank(2, o0, n0), T.idb[:], direct(tab, cc + o0, n0), True, False, ["idb"] + span(tab, cc + o0, n0), ["B2", "b2"])
+                mm(bank(5, w0, wd), T.idb[:], T.zb[:, 0:wd], True, False, ["idb", "zb", "zc"], ["B5", "cf_"])
+            for j in range(M):
+                way = SIDE_U[t].get(j)
+                au, ab, ak = bank(j % 2, 0, n0), "B%d" % (j % 2), "au%d" % (j % 2)
+                a1 = s * 80 + j * na + o0 // 16
+                off, du, dk = T.uc[:, a1:a1 + n0 // 16], T.du[:, j, o0:o0 + n0], span("du%d" % j, o0, n0)
+                if way == "p":
+                    gather(t, b, c0 + o0, n0, off, ["uc%d" % s], way, au, [ab, ak])
+                    act(au, au, AF.Abs, [ak], [ab, ak])
+                else:
+                    gather(t, b, c0 + o0, n0, off, ["uc%d" % s], way, du, dk)
+                    act(au, du, AF.Abs, dk, [ab, ak])
+                c = 2560 + s * 1280 + j * n
+                tt(T.wide[:, c + o0:c + o0 + n0], au, T.adv[:, b, j, c0 + o0:c0 + o0 + n0], ALU.is_lt,
+                   [ak] + span("adv%d_%d" % (b, j), c0 + o0, n0), [ab, "nr%d_%d" % (s, j)])
+                if more:
+                    mms([(bank(5, i * 64, 64, slice(0, m)), T.wide[:, c + o:c + o + m], T.gcf[:, 6 - 2 * j:70 - 2 * j], False,
+                          j == M - 1 and i == some[0][0]) for i, o, m in some[::-1]], ["nr%d_%d" % (s, j), "gcf"], ["B5", "cf_"])
+            if more:
+                wins(T.wf[:, w0:w0 + wd], bank(5, w0, wd), ["cf_"], ["B5", "wf" + tk])
+                tt(T.tf[:, w0 // 8:(w0 + wd) // 8, 0:8], bank(6, w0, wd), T.wf[:, w0:w0 + wd], ALU.mult, ["df", "wf" + tk, "tf"], ["B6", "tf" + tk])
+                mms([(bank(2, o, m), T.tf[0:m, 8 * i:8 * i + 8, :], T.idb[0:m, 0:m], False, i == some[-1][0]) for i, o, m in some],
+                    ["tf" + tk, "idb"], ["B2", "b2"])
+                act(direct(nxt, cc + o0, n0), bank(2, o0, n0), AF.Copy, ["b2"], ["B2"] + span(nxt, cc + o0, n0))
+                send()
         tolist(bank(4, 80, L), 2560 + s * 1280, n, ["nr%d_%d" % (s, j) for j in range(M)], ["B4", "bc"])
         wl, pt_, nd = T.wl[:, s * 80:s * 80 + L], bank(cb, 80, L), T.nd[:, b, 0:4, a0:a0 + na]
         nk = span("nd%d" % b, c0, n)

@@ -1,58 +1,69 @@
 from concourse.bass import DstId, RemoteDMATransfer
-from concourse.mybir import AluOpType as ALU, ActivationFunctionType as AF
+from concourse.mybir import AluOpType as ALU, ActivationFunctionType as AF, AxisListType as AX
 
 N, F, M, R, WORLD = 6, 640, 4, 5, 256
 W = N * F
 HF, HL = F // 2, F // 32
 XD = ["bfloat16", "bfloat16", "float32", "float32", "float32"]
 
-UNITS_A = [(0, 0, 320), (1, 0, 192), (1, 192, 128)]
+UNITS_A = [(0, 0, 320), (1, 0, 320)]
+PAIRS = "VUS"
 UNITS_B = [(0, 0, 320), (1, 0, 320)]
 PARTS = [[(0, 320)], [(0, 320)]]
-SIDE_V = [{0: "p", 1: "p"}, {0: "p", 1: "p"}, {0: "s", 3: "s"}, {0: "s", 3: "s"}, {0: "s", 3: "s"}]
-SIDE_F = [{0: "p", 1: "p"}, {0: "p"}, {3: "s"}, {3: "s"}, {3: "s"}]
-SIDE_U = [{3: "p"}, {3: "p"}, {3: "s"}, {3: "s"}, {3: "s"}]
-SHARED = (0, 1)
+SIDE_V = [{0: "p", 3: "s"}] * 2 + [{0: "s", 3: "s"}] * 3
+SIDE_F = SIDE_V
+SIDE_U = [[{3: "s"}, {3: "s"}]] * 2 + [[{2: "s", 3: "s"}, {2: "s", 3: "s"}]] * 3
+SHARED = [[(0, 1), ()]] * 2 + [[(0,), ()]] * 3
+LOW, COPY, SIZE, LIST = "aaaaa", "aaaaa", "aaaaa", "va"
+BANKS = [("pa0 au0 rows0", "df0"), ("pc0 au1 rows1", "df1"), ("nx0 b20 b21", "cl0 cl1"), ("nx1", "bc0 bc1"),
+         ("xf0", "cf0"), ("xf1", "cf1"), ("au2 pa1", "pt0 pt1"), ("au3 pc1", "bv0 bv1")]
+AU = [["au0", "au1", "au2", "au3"]] * 2
 
 SCRATCH = {
-    "nbi": ("sbuf", [128, 4, 40], "int32"), "pti": ("sbuf", [128, 8, 40], "int32"), "ptb": ("sbuf", [128, 320], "bfloat16"),
+    "nbi": ("sbuf", [128, 4, 40], "int32"), "pti": ("sbuf", [128, 8, 40], "int32"), "ptb": ("sbuf", [128, 2, 160], "bfloat16"),
     "mixs": ("sbuf", [128, F], "bfloat16"), "wide": ("sbuf", [128, 5120], "bfloat16"),
-    "dv": ("sbuf", [128, 2, 4, HF], "float32"), "adv": ("sbuf", [128, 2, 4, HF], "float32"), "du": ("sbuf", [128, 4, HF], "float32"),
-    "tmp": ("sbuf", [128, 2, 5, HF], "float32"), "rawf": ("sbuf", [128, 4, HF], "float32"), "rawb": ("sbuf", [128, 4, HF], "bfloat16"),
-    "mob": ("sbuf", [128, F], "bfloat16"), "mof": ("sbuf", [128, F], "float32"),
+    "tmp": ("sbuf", [128, 3, 4, HF], "float32"),
     "yes": ("sbuf", [128, F], "float32"), "yds": ("sbuf", [128, F], "float32"), "yns": ("sbuf", [128, 4, 40], "float32"),
     "nd": ("sbuf", [128, 2, 7, HL], "float32"), "own": ("sbuf", [128, 2, 4, HL], "float32"),
-    "un": ("sbuf", [128, 2, 4, HL], "uint16"), "cs": ("sbuf", [128, 160], "float32"), "uc": ("sbuf", [128, 160], "uint16"),
-    "eq": ("sbuf", [128, 2, 7, 80], "bfloat16"), "wl": ("sbuf", [128, 160], "bfloat16"),
-    "wf": ("sbuf", [128, 192], "bfloat16"), "tf": ("sbuf", [128, 24, 16], "bfloat16"), "zb": ("sbuf", [128, 192], "bfloat16"),
+    "un": ("sbuf", [128, 2, 4 * HL], "uint16"), "cs": ("sbuf", [128, 160], "float32"), "uc": ("sbuf", [128, 160], "uint16"),
+    "eq": ("sbuf", [128, 2, 7, 80], "bfloat16"), "wl": ("sbuf", [128, 160], "bfloat16"), "zt": ("sbuf", [128, 2, 160], "bfloat16"),
+    "far": ("sbuf", [128, 128], "bfloat16"), "off": ("sbuf", [128, 128], "bfloat16"),
+    "wf": ("sbuf", [128, 2, 192], "bfloat16"), "tf": ("sbuf", [128, 48, 16], "bfloat16"), "zb": ("sbuf", [128, 192], "bfloat16"),
     "ci": ("sbuf", [128, 128], "float32"), "cm": ("sbuf", [128, 128], "float32"), "ch": ("sbuf", [128, 72], "float32"),
-    "pi": ("sbuf", [128, 8], "int32"), "cf": ("sbuf", [128, 16], "float32"), "km": ("sbuf", [128, 16], "float32"),
-    "dm": ("sbuf", [128, 2048], "bfloat16"),
-    "idb": ("sbuf", [128, 128], "bfloat16"), "idf": ("sbuf", [128, 128], "float32"), "neg": ("sbuf", [128, 128], "bfloat16"),
-    "far": ("sbuf", [128, 128], "bfloat16"), "b8": ("sbuf", [128, 128], "bfloat16"),
-    "amb": ("sbuf", [128, 128], "bfloat16"), "amf": ("sbuf", [128, 128], "float32"),
+    "pi": ("sbuf", [128, 8], "int32"), "cf": ("sbuf", [128, 24], "float32"), "km": ("sbuf", [128, 16], "float32"),
+    "b8": ("sbuf", [128, 128], "bfloat16"),
     "gcf": ("sbuf", [128, 72], "bfloat16"), "gdf": ("sbuf", [128, 72], "bfloat16"), "gn": ("sbuf", [128, 64], "bfloat16"),
     "ps": ("psum", [128, 4096], "float32"),
 }
+for _k, _d in (("b", "bfloat16"), ("f", "float32")):
+    SCRATCH.update({"dv" + _k: ("sbuf", [128, 2, 4 * HF], _d), "adv" + _k: ("sbuf", [128, 2, 4 * HF], _d), "du" + _k: ("sbuf", [128, 2, 4 * HF], _d),
+                    "up" + _k: ("sbuf", [128, 2, HF], _d), "mo" + _k: ("sbuf", [128, F], _d)})
+    SCRATCH.update({_m + _k: ("sbuf", [128, 128], _d) for _m in ("id", "neg", "two", "am")})
 for _t in range(R):
-    SCRATCH["xt%d" % _t] = ("sbuf", [128, W + 16], XD[_t])
+    SCRATCH["xt%d" % _t] = ("sbuf", [128, W + 16 * (_t < R - 1)], XD[_t])
     SCRATCH["nt%d" % _t] = ("sbuf", [128, W], "bfloat16")
-    SCRATCH["xo%d" % _t] = ("sbuf", [128, F], XD[_t])
+    SCRATCH["xo%d" % _t] = ("sbuf", [128, 2, F], XD[_t])
+PLACE = {k: (b, 0, HF) for b, x in enumerate(BANKS) for k in x[0].split()}
+PLACE.update({k: (b, HF + 80 * i, 80 if " " in y else 192)
+              for b, x in enumerate(BANKS) for y in x[1].split("|") for i, k in enumerate(y.split())})
 
-EVENTS = [("xt0", 0, HF, "a"), ("xt0", HF, HF, "b"), ("nt0", 0, F, "a")]
+EVENTS = [("xt0", 0, HF, "a"), ("xt0", HF, HF, "b"), ("nt0", 0, HF, "e"), ("nt0", HF, HF, "d")]
 for _t in range(1, R):
-    EVENTS += [("xt%d" % _t, u[0] * HF + u[1], u[2], "ab"[UNITS_A.index(u) % 2]) for u in UNITS_A]
-    EVENTS += [("nt%d" % _t, u[0] * HF + u[1] + o, n, ("c", "a" if (o, n) == ps_[-1] else "b")[u[0]]) for u, ps_ in zip(UNITS_B, PARTS) for o, n in ps_]
+    EVENTS += [("xt%d" % _t, u[0] * HF + u[1], u[2], "ca"[UNITS_A.index(u)]) for u in UNITS_A]
+    EVENTS += [("nt%d" % _t, u[0] * HF + u[1] + o, n, "ed"[u[0]]) for u, ps_ in zip(UNITS_B, PARTS) for o, n in ps_]
 WAYS = {"a": [(None, 0), (None, 2), ("own", None), ("other", None), ("other", None)],
         "b": [(None, 1), (None, 3), ("own", None), ("other", None), ("other", None)],
-        "c": [(None, None), (None, 0), ("other", 1), ("other", 2), ("other", 3)]}
+        "c": [(None, None), (None, 1), ("other", None), ("other", 0), ("other", 3)],
+        "d": [(None, 0), (None, None), ("own", None), ("other", None), ("other", None)],
+        "e": [(None, 1), (None, 3), ("own", None), ("own", None), ("other", None)]}
 ROUTES = []
 
-GATHER, HAND, FLY, LOCAL = (65, 1.6), 260, (4200, 2.8, 4000), 2300
-SPEEDS = [(1.2, 1.2, 320), (1.6, 1.0, 260), (2.0, 0.8, 180)]
-SHIFT, SLACK, POLISH, EASE = 1500, 500, 24000, 100
-SAME = {"au0": ["pa0"], "au1": ["pc0"], "rows0": ["pa0"], "rows1": ["pc0"], "cf_": ["pa1"], "df": ["pc1"], "b2": ["nx0"]}
-TURNS, TRIES, ORDER = 4, 300, []
+GATHER, HAND, FLY, LOCAL, PE = (65, 1.6), 230, (4200, 2.8, 4000), 2300, 0.9
+SPEEDS = [(1.2, 1.05, 270, 1.0), (1.6, 0.9, 220, 0.6), (1.9, 0.75, 180, 1.0)]
+TESTS = []
+PLANS, TURNS, TRIES, SHIFT, SLACK, ALL = 7, 7, 150, 1000, 200, 0.3
+POLISH, LAST, WIDTH, BAR, EASE = 400, 600, 8, 100, 30
+ORDER = []
 SEMAPHORES = (["sv", "sa", "sp", "sg", "ldx", "ldn", "ldm", "sto", "sent"] + ["xo%d" % t for t in range(R)]
               + ["e%s_%d" % e[:2] for e in EVENTS])
 
@@ -91,12 +102,25 @@ def routes(T, topo):
                         load[k, topo.die(a)] = load.get((k, topo.die(a)), 0) + 1
                 way.append(path)
             ways.append(way)
-        return sorted(load.values(), reverse=True), ways
+        return sorted(load.values(), reverse=True), ways, load
 
     def orders(left):
         return [[d] + rest for d in left for rest in orders([x for x in left if x != d])] if left else [[]]
-    best = {k: min((deal(roles, ds) for ds in orders(list(range(1, N)))), key=lambda x: x[0])[1] for k, roles in WAYS.items()}
-    ROUTES.extend({k: best[k][s] for k in WAYS} for s in range(N))
+    alone = {k: [deal(roles, ds) for ds in orders(list(range(1, N)))] for k, roles in WAYS.items()}
+    alone = {k: [x for x in v if x[0][0] == min(y[0][0] for y in v)] for k, v in alone.items()}
+    share = {k: sum(e[2] * (2 if T[e[0]].dtype == T.xt4.dtype else 1) for e in EVENTS if e[3] == k) for k in WAYS}
+    best = {k: v[0] for k, v in alone.items()}
+
+    def together(k, x):
+        load = {}
+        for k2 in WAYS:
+            for link, n in (x if k2 == k else best[k2])[2].items():
+                load[link] = load.get(link, 0) + n * share[k2]
+        return sorted(load.values(), reverse=True)
+    for turn in range(2):
+        for k in WAYS:
+            best[k] = min(alone[k], key=lambda x: together(k, x))
+    ROUTES.extend({k: best[k][1][s] for k in WAYS} for s in range(N))
     return ROUTES
 
 
@@ -111,7 +135,6 @@ def transfer(T, topo, src, dsts, ev, rank, mask):
 
 
 def helper_program(g, core, T, topo, rts):
-    cores = list(T.cores)
     sent = 0
     for ev in EVENTS:
         for rank in range(N):
@@ -134,7 +157,10 @@ def make_emitter(g, T):
     clock, writer, readers = {}, {}, {}
 
     def apart(e, k, r):
-        return e in "pgsl" or k[0] == "B" or k == "mask" or (e == "v" and k[:2] in ("pa", "pc", "pt") and k in r)
+        return e in "pgsl" or k[0] == "B" or k == "mask" or (e == "v" and k[0] == "P" and k in r)
+
+    edges = {b: sorted(set(x for p in PLACE.values() if p[0] == b for x in (p[1], p[1] + p[2]))) for b in range(8)}
+    same = {k: ["P%d:%d" % (b, x) for x in edges[b] if c <= x < c + n] for k, (b, c, n) in PLACE.items()}
 
     def need(e, s, n):
         if known[e].get(s, 0) >= n:
@@ -182,7 +208,7 @@ def make_emitter(g, T):
     calls, total = [], {}
 
     def note(e, call, r=(), w=(), dma=None, c=100, far=(), kind=""):
-        r, w = [[x for k in keys for x in SAME.get(k, [k])] for keys in (r, w)]
+        r, w = [[x for k in keys for x in same.get(k, [k])] for keys in (r, w)]
         calls.append((e, call, r, w, dma, c, far, e + kind))
         if dma and dma != "remote":
             total[dma] = total.get(dma, 0) + 16
@@ -192,8 +218,6 @@ def make_emitter(g, T):
         pre = [dict() for c in calls]
         wr, rd, sends = {}, {}, {}
         for i, (e, call, r, w, dma, c, far, kind) in enumerate(calls):
-            if e != "p":
-                r = r + [k for k in w if k[0] == "B"]
             for k in r:
                 if k in wr:
                     pre[i][wr[k]] = max(pre[i].get(wr[k], 0), HAND)
@@ -297,57 +321,158 @@ def make_emitter(g, T):
                     free[k], who[k] = at + hold[i], i
             return done, why
 
-        speeds = [([x * slow if c[0] == "l" or c[4] else (x - GATHER[0]) * quick / GATHER[1] + GATHER[0] if isinstance(x, float) else x
-                    for x, c in zip(length, calls)], slow, hand) for quick, slow, hand in SPEEDS]
+        def tails(order, s, aft, last, known_):
+            long_, hold, waits, hand = s
+            tail, who = list(known_), {}
+            for i in order[last + 150:last:-1]:
+                for k in uses[i]:
+                    who[k] = i
+            for i in order[last::-1]:
+                x, e = 0, eng[i]
+                for j, lag in aft[i]:
+                    if lag + tail[j] > x:
+                        x = lag + tail[j]
+                x += long_[i]
+                for k in uses[i]:
+                    j = who.get(k)
+                    if j is not None:
+                        y = hold[i] + tail[j] + (0 if eng[j] == e else hand)
+                        if y > x:
+                            x = y
+                    who[k] = i
+                tail[i] = x
+            return tail
+
+        def guess(order, at, to, seq, runs, ends):
+            inside, before, behind, total_ = set(seq), {}, {}, 0
+            for i in order[max(0, at - 40):at]:
+                for k in uses[i]:
+                    before[k] = i
+            for i in order[to + 40:to:-1]:
+                for k in uses[i]:
+                    behind[k] = i
+            for (long_, hold, waits, hand), aft, (done, why), tail in zip(speeds, after, runs, ends):
+                new, free, who, most = {}, {k: done[i] - long_[i] + hold[i] for k, i in before.items()}, dict(before), 0
+                for i in seq:
+                    x, e = 0, eng[i]
+                    for d, lag in waits[i]:
+                        y = (new[d] if d in inside else done[d]) + lag
+                        if y > x:
+                            x = y
+                    for k in uses[i]:
+                        if k in who:
+                            y = free[k] if eng[who[k]] == e else free[k] + hand
+                            if y > x:
+                                x = y
+                    for k in uses[i]:
+                        free[k], who[k] = x + hold[i], i
+                    x = new[i] = x + long_[i]
+                    if x > most:
+                        most = x
+                    for j, lag in aft[i]:
+                        if j not in inside and x + lag + tail[j] > most:
+                            most = x + lag + tail[j]
+                for k, j in behind.items():
+                    if k in who:
+                        most = max(most, free[k] + tail[j] + (0 if eng[who[k]] == eng[j] else hand))
+                total_ += most
+            return total_ / len(speeds)
+
+        speeds = [([x * slow if c[0] == "l" or c[4] else x * pe / PE if c[0] == "p" else
+                    (x - GATHER[0]) * quick / GATHER[1] + GATHER[0] if isinstance(x, float) else x
+                    for x, c in zip(length, calls)], slow, hand) for quick, slow, hand, pe in SPEEDS + TESTS]
         speeds = [(long_, [x if b == y else b for x, y, b in zip(long_, length, busy)],
                    [[(d, hand if lag == HAND else lag * slow) for d, lag in p.items()] for p in pre], hand) for long_, slow, hand in speeds]
+        speeds, tests = speeds[:len(SPEEDS)], speeds[len(SPEEDS):]
+        after = [[[] for i in range(n_)] for s in speeds]
+        for s, x in zip(speeds, after):
+            for i in range(n_):
+                for d, lag in s[2][i]:
+                    x[d].append((i, lag))
 
-        if not ORDER:
-            best = improve([-x for x in rest])
-            for turn in range(TURNS):
-                best = min(best, improve(best[1]))
-            kind = [c[7] for c in calls]
-            kinds = sorted(set(kind))
-            seed, last = [12345], best
+        kind = [c[7] for c in calls]
+        kinds = sorted(set(kind))
+        seed = [99]
 
-            def draw():
-                seed[0] = (seed[0] * 1103515245 + 12345) % 2147483648
-                return (seed[0] >> 8) / 8388608.0
+        def draw():
+            seed[0] = (seed[0] * 1103515245 + 12345) % 2147483648
+            return (seed[0] >> 8) / 8388608.0
+
+        def shaken():
+            best = last = improve([-x + draw() * SHIFT for x in rest])
             for turn in range(TRIES):
                 shift = {k: (draw() + draw() - 1.0) * SHIFT for k in kinds if draw() < 0.1}
-                trial = improve([x + shift.get(k, 0.0) for x, k in zip(last[1], kind)])
+                lo, hi = (0, n_) if draw() < ALL else sorted((int(draw() * n_), int(draw() * n_)))
+                trial = improve([x + shift.get(k, 0.0) if lo <= i < hi else x for i, (x, k) in enumerate(zip(last[1], kind))])
                 if trial[0] <= last[0] + SLACK * (1.0 - turn / TRIES):
                     last = trial
                 best = min(best, last)
-            order = sorted(range(n_), key=lambda i: (best[2][i] - length[i], i))
-            now = top = (best[0], order)
+            return sorted(range(n_), key=lambda i: (best[2][i] - length[i], i))
+
+        def joined(best, plans):
+            for mark in [i for i in range(n_) if calls[i][4] == "remote"]:
+                for span, other in plans:
+                    for x, y in ((best[1], other), (other, best[1])):
+                        head = x[:x.index(mark)]
+                        some = set(head)
+                        order = head + [i for i in y if i not in some]
+                        best = min(best, (sum(max(replay(order, *s)[0]) for s in speeds) / len(speeds), order))
+            return best
+
+        def polished(order, POLISH):
             runs = [replay(order, *s) for s in speeds]
+            ends = [tails(order, s, x, n_ - 1, [0] * n_) for s, x in zip(speeds, after)]
+            span = sum(max(x[0]) for x in runs) / len(speeds)
+            top, barred = (span, order), {}
             for turn in range(POLISH):
                 done, why = runs[turn % len(speeds)]
-                held, i = [], done.index(max(done))
-                while why[i] >= 0:
-                    if why[i] not in pre[i]:
-                        held.append((why[i], i))
+                chain, i = [], done.index(max(done))
+                while i >= 0:
+                    chain.append(i)
                     i = why[i]
-                if not held:
-                    continue
-                a, b = held[int(draw() * len(held))]
-                at, to = now[1].index(a), now[1].index(b)
-                ahead = {b}
-                for i in now[1][to - 1:at - 1 if at else None:-1]:
-                    if any(j in ahead for j in back[i]):
-                        ahead.add(i)
-                if a in ahead:
-                    continue
-                between = now[1][at:to + 1]
-                order = now[1][:at] + [i for i in between if i in ahead] + [i for i in between if i not in ahead] + now[1][to + 1:]
-                trial = [replay(order, *s, at, k) for s, k in zip(speeds, runs)]
-                span = sum(max(x[0]) for x in trial) / len(speeds)
-                if span <= now[0] + EASE * (1.0 - turn / POLISH):
-                    now, runs = (span, order), trial
-                    top = min(top, now)
-            done = replay(top[1], *speeds[len(speeds) // 2])[0]
-            ORDER.append((top[0], top[1], best[1], done, kind, max(rest), pre, length))
+                held = [x for x in range(len(chain) - 1) if chain[x + 1] not in pre[chain[x]]]
+                place = {i: x for x, i in enumerate(order)}
+                moves = []
+                for trial in range(WIDTH if held else 0):
+                    x = y = held[int(draw() * len(held))]
+                    while draw() < 0.4 and y + 2 < len(chain) and chain[y + 2] not in pre[chain[y + 1]]:
+                        y += 1
+                    a, b = chain[y + 1], chain[x]
+                    at, to = place[a], place[b]
+                    if barred.get((chain[x + 1], b), -1) > turn or to - at > 120:
+                        continue
+                    between = order[at:to + 1]
+                    if draw() < 0.5:
+                        some = {b}
+                        for i in between[-2::-1]:
+                            if any(j in some for j in back[i]):
+                                some.add(i)
+                        seq = [i for i in between if i in some] + [i for i in between if i not in some]
+                    else:
+                        some = {a}
+                        for i in between[1:]:
+                            if any(j in some for j in pre[i]):
+                                some.add(i)
+                        seq = [i for i in between if i not in some] + [i for i in between if i in some]
+                    if (a in some) != (b in some):
+                        moves.append((guess(order, at, to, seq, runs, ends), at, to, seq, a, b))
+                if moves and min(moves)[0] <= span + EASE:
+                    x, at, to, seq, a, b = min(moves)
+                    order = order[:at] + seq + order[to + 1:]
+                    runs = [replay(order, *s, at, k) for s, k in zip(speeds, runs)]
+                    ends = [tails(order, s, x, to, k) for s, x, k in zip(speeds, after, ends)]
+                    span = sum(max(x[0]) for x in runs) / len(speeds)
+                    barred[b, a] = turn + BAR
+                    top = min(top, (span, order))
+            return top
+
+        if not ORDER:
+            plans = [polished(shaken(), POLISH) for turn in range(PLANS)]
+            top = min(plans)
+            for turn in range(TURNS):
+                top = polished(joined(top, plans)[1], LAST)
+            done, why = replay(top[1], *speeds[len(speeds) // 2])
+            ORDER.append((top[0], top[1], why, done, kind, max(rest), pre, length, [int(max(replay(top[1], *s)[0])) // 100 for s in speeds + tests]))
         for i in ORDER[0][1]:
             if eng[i] != "l":
                 op(*calls[i][:5])
@@ -364,7 +489,6 @@ def make_emitter(g, T):
 def rank_program(g, core, T, topo):
     rts = routes(T, topo)
     rank = T.rank_of(core)
-    cores = list(T.cores)
     if rank is None:
         helper_program(g, core, T, topo, rts)
         return
@@ -390,9 +514,9 @@ def rank_program(g, core, T, topo):
         mine = [p[1] for p in paths if p[1] not in handed]
         far = topo.mask(core, mine[0])
         time, lag = FLY[1] * ev[2] * (4 if ev[0] in ("xt2", "xt3", "xt4") else 2), FLY[0] + FLY[2] * (turn[0] == 1)
-        tr = [transfer(T, topo, core, mine, ev, rank, far), transfer(T, topo, core, handed, ev, rank, topo.mask(core, handed[0]) & ~far)]
         if len(paths[0]) == 4:
             time, lag = time / 2, lag * 1.5 + time
+        tr = [transfer(T, topo, core, mine, ev, rank, far), transfer(T, topo, core, handed, ev, rank, topo.mask(core, handed[0]) & ~far)]
         sent[0] += ones(far) * len(tr)
         op("g", lambda e: e.remote_dma_fused(tr, local_sem=T.sem.sent), r=span(ev[0], ev[1], ev[2]), w=["sends"], dma="remote", kind="send")
         op("l", None, r=["sends"], w=["links"], c=time, far=[("far%s_%d" % ev[:2], lag)], kind="link")
@@ -428,10 +552,10 @@ def rank_program(g, core, T, topo):
         op("a", lambda e: e.activation(out, a, fn, bias=bias, scale=scale), r, w, c=c or max(64, size(out)) + 20, kind=name(w))
 
     def mm(out, l, rh, start, stop, r, w, wide=False):
-        op("p", lambda e: e.matmul(out, l, rh, start, stop), r, w, c=max(64, size(rh)) * (4 if wide else 1), kind=name(w))
+        op("p", lambda e: e.matmul(out, l, rh, start, stop), r, w, c=int(max(64, size(rh)) * (4 if wide else 1) * PE), kind=name(w))
 
     def mms(steps, r, w):
-        op("p", lambda e: [e.matmul(*s) for s in steps][-1], r, w, c=sum(max(64, size(s[2])) for s in steps), kind=name(w))
+        op("p", lambda e: [e.matmul(*s) for s in steps][-1], r, w, c=int(sum(max(64, size(s[2])) for s in steps) * PE), kind=name(w))
 
     def load(q, out, in_, w, sem, r=()):
         op(q, lambda e: e.dma_start(out, in_), r=r, w=w, dma=sem, c=LOCAL, kind=sem)
@@ -439,15 +563,23 @@ def rank_program(g, core, T, topo):
     def gcost(n):
         return GATHER[0] + GATHER[1] * n
 
-    def bank(b, c0, n, rows=slice(0, 128)):
-        return ps[rows, b * 512 + c0:b * 512 + c0 + n]
+    def at(name_, c0=0, n=None, rows=slice(0, 128)):
+        b, c, m = PLACE[name_]
+        return ps[rows, b * 512 + c + c0:b * 512 + c + c0 + (n or m)]
+
+    def bk(name_):
+        return "B%d" % PLACE[name_][0]
+
+    def kind(t):
+        return "b" if t < 2 else "f"
 
     def direct(tab, c, n):
         return T[tab][:, base + c:base + c + n]
 
     load("s", direct("xt0", 0, F), T.x[:], span("xt0", 0, F), "ldx")
     load("a", T.nbi[:], T.nb[:], ["nbi"], "ldn")
-    load("s", T.xo0[:], T.x[:], span("xo0", 0, F), "xo0")
+    for h in range(2):
+        load("s", T.xo0[:, :, h * HF:(h + 1) * HF], T.x[:], span("xo0" + "ab"[h], 0, F), "xo0")
     load("s", T.mixs[0:16, :], T.mix[:], ["mix"], "ldm")
     fl = dict(allow_small_or_imprecise_dtypes=True)
     op("g", lambda e: e.iota(T.pi[:, 0:1], [[0, 1]], 0, 1), w=["pi0"], c=160)
@@ -457,13 +589,14 @@ def rank_program(g, core, T, topo):
     op("g", lambda e: e.iota(T.cm[:], [[0, 8], [1, 16]], 0, 0, **fl), r=["sends"], w=["cm"], c=420)
     op("g", lambda e: e.iota(T.ch[:], [[1, 36], [0, 2]], 0, 0, **fl), r=["sends"], w=["ch"], c=300)
     op("g", lambda e: e.iota(T.own[:], [[HF, 2], [0, 4], [16, HL]], base, 1, **fl), r=["sends"], w=["own"], c=480)
-    fill(T.dm[:], 0.0, ["dmz"])
+    fill(T.zt[:], 0.0, ["zt"])
+    for t in range(R - 1):
+        fill(T["xt%d" % t][:, W:W + 16], 1024.0, ["padxt%d" % t])
     fill(T.tf[:], 0.0, ["tf"])
     fill(T.zb[:, 0:64], 0.0, ["zb"])
     act(T.zb[:, 64:192], T.ci[:], AF.Sigmoid, ["ci"], ["zc"], bias=-2176.0, c=1700)
-    fill(bank(6, 128, 64), 0.0, ["B6", "df"])
-    for t in range(R):
-        fill(T["xt%d" % t][:, W:W + 16], 1024.0, ["padxt%d" % t])
+    for df in ("df0", "df1"):
+        fill(at(df, 128, 64), 0.0, [bk(df), df])
     for c, m in ((1, 112), (2, 15), (3, 1)):
         ts(T.pi[:, c:c + 1], T.pi[:, 0:1], m, None, ALU.bitwise_and, None, ["pi0"], ["pi%d" % c])
     cp(T.cf[:, 0:4], T.pi[:, 0:4], ["pi%d" % c for c in range(4)], ["cf"])
@@ -474,28 +607,30 @@ def rank_program(g, core, T, topo):
     ts(col(5), G16, 0.5, H_, ALU.mult, ALU.add, ["cf"], ["cf5"])
     ts(col(6), G16, 0.5, K_, ALU.mult, ALU.add, ["cf"], ["cf6"])
     ts(col(7), K_, 8.0, -1.0, ALU.is_lt, ALU.mult, ["cf"], ["cf7"])
-    for r_ in range(4):
+    for r_ in range(M):
         ts(col(8 + r_), K_, H_, 2.0 * r_, ALU.subtract, ALU.is_equal, ["cf"], ["mask"])
-    dmk = ["dm%d" % k for k in range(8)]
-    for k in range(8):
-        ts(T.dm[:, 16 * k::129], T.zb[:, 0:16], G16, 16.0 * k, ALU.add, ALU.is_equal, ["zb", "cf", "dmz"], [dmk[k]])
+
+    def onto(k):
+        return T.zt[:, k % 2, 16 - k + k % 2:144 - k + k % 2]
+    dmk = ["zs", "zu"]
+    ts(T.zt[:, 0, 16:144], T.ci[:], G16, None, ALU.is_equal, None, ["ci", "cf", "zt"], ["zs"])
+    ts(T.zt[:, 1, 17:145], T.ci[:], G16, None, ALU.is_equal, None, ["ci", "cf", "zt"], ["zu"])
     ts(T.pti[:, 0::2, :], T.nbi[:], 4032, None, ALU.bitwise_and, None, ["nbi"], ["pti0"])
     ts(T.pti[:, 1::2, :], T.nbi[:], 63, None, ALU.bitwise_and, None, ["nbi"], ["pti1"])
-    cp(T.ptb[:], T.pti[:], ["pti0", "pti1"], ["ptb"])
-    zk = []
-    for k in range(16):
-        zk.append("z%d" % k)
-        if k % 3 == 0:
-            act(T.wide[:, k::16], T.ptb[:], AF.Copy, ["ptb", "km"], [zk[-1]], scale=T.km[:, k:k + 1])
-        else:
-            ts(T.wide[:, k::16], T.ptb[:], T.km[:, k:k + 1], None, ALU.mult, None, ["ptb", "km"], [zk[-1]], c=180)
     wide_keys = ["%s%d_%d" % (a, h, j) for a in ("cg", "nr") for h in range(2) for j in range(M)]
     for h in range(2):
-        for r_ in range(8):
-            c = r_ * F + h * HF
-            mm(bank(h, 0, HF), T.dm[:, r_ * 128:(r_ + 1) * 128], T.wide[:, c:c + HF], r_ == 0, r_ == 7, zk + wide_keys + dmk, ["B%d" % h, "rows%d" % h])
-        act(direct("nt0", h * HF, HF), bank(h, 0, HF), AF.Copy, ["rows%d" % h], ["B%d" % h] + span("nt0", h * HF, HF))
-    send()
+        cp(T.ptb[:, h], T.pti[:, :, h * HL:(h + 1) * HL], ["pti0", "pti1"], ["ptb%d" % h])
+        zk = ["z%d_%d" % (h, k) for k in range(16)]
+        for k in range(16):
+            out = T.wide[:, h * 2560 + k:(h + 1) * 2560:16]
+            if k % 3 == 0:
+                act(out, T.ptb[:, h], AF.Copy, ["ptb%d" % h, "km"], [zk[k]], scale=T.km[:, k:k + 1])
+            else:
+                ts(out, T.ptb[:, h], T.km[:, k:k + 1], None, ALU.mult, None, ["ptb%d" % h, "km"], [zk[k]], c=100)
+        mms([(at("rows%d" % h), onto(r_), T.wide[:, h * 2560 + r_ * HF:h * 2560 + (r_ + 1) * HF], r_ == 0, r_ == 7) for r_ in range(8)],
+            zk + wide_keys + dmk, [bk("rows%d" % h), "rows%d" % h])
+        act(direct("nt0", h * HF, HF), at("rows%d" % h), AF.Copy, ["rows%d" % h], [bk("rows%d" % h)] + span("nt0", h * HF, HF))
+        send()
     for b in range(2):
         src = T.nbi[:, :, b * HL:(b + 1) * HL]
         cp(T.un[:, b], src, ["nbi"], span("un%d" % b, 0, HF))
@@ -503,188 +638,250 @@ def rank_program(g, core, T, topo):
         act(T.nd[:, b, 4:7], T.nd[:, b, 0:3], AF.Copy, span("nd%d" % b, 0, HF), span("ndd%d" % b, 0, HF))
     ts(T.own[:], T.own[:], G16, None, ALU.subtract, None, ["own", "cf"], ["own"])
     ts(T.idb[:], T.ci[:], P_, None, ALU.is_equal, None, ["ci", "cf"], ["idb"])
-    ts(T.neg[:], T.ci[:], P_, -1.0, ALU.is_equal, ALU.mult, ["ci", "cf"], ["neg"])
-    ts(T.far[:], T.ci[:], P_, 8192.0, ALU.is_equal, ALU.mult, ["ci", "cf"], ["far"])
+    for m, v in (("far", 8192.0), ("off", -16.0), ("idf", 1.0)):
+        act(T[m][:], T.idb[:], AF.Copy, ["idb"], [m], scale=v)
     ts(T.b8[:], T.cm[:], K_, 0.125, ALU.is_equal, ALU.mult, ["cm", "cf"], ["b8"])
     ts(T.gcf[:], T.ch[:], col(4), None, ALU.is_equal, None, ["ch", "cf4"], ["gcf"])
     ts(T.gdf[:], T.ci[:, 0:72], col(5), 6.0, ALU.subtract, ALU.is_equal, ["ci", "cf5"], ["gdf"])
     ts(T.gn[:], T.ci[:, 0:64], col(6), col(7), ALU.is_equal, ALU.mult, ["ci", "cf6", "cf7"], ["gn"])
     tt(T.amb[:], T.idb[:], T.b8[:], ALU.subtract, ["idb", "b8"], ["amb"], c=270)
-    act(T.idf[:], T.idb[:], AF.Copy, ["idb"], ["idf"])
     act(T.amf[:], T.amb[:], AF.Copy, ["amb"], ["amf"])
-
-    slot_of = {"rawf": [0], "rawb": [0]}
+    made = ["idb", "idf"]
 
     def offs(b, c0, n, j):
-        return T.un[:, b, j, c0 // 16:(c0 + n) // 16]
+        return T.un[:, b, j * HL + c0 // 16:j * HL + (c0 + n) // 16]
 
-    def gather(t, b, c0, n, off, okeys, way, out, w):
+    def sums(t, out, w, terms):
+        for i, (v, ap, keys) in enumerate(terms):
+            m = {1: "id", -1: "neg", 2: "two"}[v] + kind(t)
+            if m not in made:
+                made.append(m)
+                act(T[m][:], T.idb[:], AF.Copy, ["idb"], [m], scale=float(v))
+            mm(out, T[m][:], ap, i == 0, i == len(terms) - 1, [m] + keys, w, wide=t >= 2)
+
+    def pair(t, b, off, okeys, way, out, w):
+        tab = "xt%d" % t
+        if way is None:
+            tt(out, T[tab][:].indirect(off), T["xo%d" % t][:, b], ALU.subtract,
+               whole(tab) + okeys + span("xo%da" % t, b * HF, HF) + span("xo%db" % t, b * HF, HF), w, c=gcost(F))
+        else:
+            act(out, T[tab][:].indirect(off), AF.Copy, whole(tab) + okeys, w, c=gcost(F))
+
+    def gather(t, b, c0, n, off, okeys, way, held, hk, out, w):
         tab, c = "xt%d" % t, b * HF + c0
         if way is None:
-            tt(out, T[tab][:].indirect(off), T["xo%d" % t][:, c:c + n], ALU.subtract, whole(tab) + okeys + span("xo%d" % t, c, n), w, c=gcost(n))
+            if off is not None:
+                tt(out, T[tab][:].indirect(off), T["xo%d" % t][:, b, c0:c0 + n], ALU.subtract, whole(tab) + okeys + span("xo%da" % t, c, n), w, c=gcost(n))
             return
-        buf = "rawb" if way == "p" else "rawf"
-        s = slot_of[buf][0] % 4
-        slot_of[buf][0] += 1
-        raw, rk = T[buf][:, s, 0:n], "%s%d" % (buf, s)
-        act(raw, T[tab][:].indirect(off), AF.Copy, whole(tab) + okeys, [rk], c=gcost(n))
+        if off is not None:
+            act(held, T[tab][:].indirect(off), AF.Copy, whole(tab) + okeys, hk, c=gcost(n))
         if way == "p":
-            mm(out, T.neg[:], direct(tab, c, n), True, False, ["neg"] + span(tab, c, n), w)
-            mm(out, T.idb[:], raw, False, True, ["idb", rk], w)
+            sums(t, out, w, [(-1, direct(tab, c, n), span(tab, c, n)), (1, held, hk)])
         else:
-            tt(out, raw, bank(3 + b, 160 + c0, n), ALU.subtract, [rk, "xf%d" % b], ["B%d" % (3 + b)] + w)
+            tt(out, held, at("xf%d" % b, c0, n), ALU.subtract, hk + ["xf%d" % b], [bk("xf%d" % b)] + w)
+
+    def first(t, b, c0, n, sign):
+        u = [i for i, x in enumerate(UNITS_A) if x[0] == b and x[1] <= c0 < x[1] + x[2]][0]
+        tab, c = "xt%d" % t, b * HF + c0
+        d = [(sign, T["dv" + kind(t)][:, b, HF + c0:HF + c0 + n], span("dv%d_1" % b, c0, n))]
+        return d + ([(-sign, direct(tab, c, n), span(tab, c, n))] if (SIDE_V if u else SIDE_F)[t].get(1) == "p" else [])
 
     def medians(t, u):
         b, c0, n = UNITS_A[u]
-        s, cc, tab = u % 2, b * HF + c0, "xt%d" % t
-        pa, pc, ba, bc = bank(5 * s, 0, n), bank(5 * s + 1, 0, n), "B%d" % (5 * s), "B%d" % (5 * s + 1)
+        s, cc, tab, k = u, b * HF + c0, "xt%d" % t, kind(t)
         a, c = "pa%d" % s, "pc%d" % s
-        tm = [T.tmp[:, s, i, 0:n] for i in range(5)]
-        tk = ["tm%d_%d" % (s, i) for i in range(5)]
-        nx, nw = bank((2, 7)[b], 160 * b + c0, n), ["B%d" % (2, 7)[b], "nx%d" % b]
-        am = "amb" if t < 2 else "amf"
+        pa, pc, ba, bc = at(a, 0, n), at(c, 0, n), bk(a), bk(c)
+        tm = [T.tmp[:, s, i, 0:n] for i in range(4)]
+        tk = ["tm%d_%d" % (s, i) for i in range(4)]
+        up, uk = T["up" + k][:, b, c0:c0 + n], span("up%d" % b, c0, n)
+        nx, nw = at("nx%d" % b, c0, n), [bk("nx%d" % b), "nx%d" % b]
         if t < R - 1:
             mm(nx, T.b8[0:16, :], T.mixs[0:16, cc:cc + n], True, False, ["b8", "mix"], nw)
-            mm(nx, T[am][:], direct(tab, cc, n), False, False, [am] + span(tab, cc, n), nw, wide=t >= 2)
+            mm(nx, T["am" + k][:], direct(tab, cc, n), False, False, ["am" + k] + span(tab, cc, n), nw, wide=t >= 2)
         d, dk = [], []
         for j in range(M):
             way = (SIDE_V if u else SIDE_F)[t].get(j)
-            ap, key = T.dv[:, b, j, c0:c0 + n], span("dv%d_%d" % (b, j), c0, n)
-            bk = []
+            held, hk = T["dv" + k][:, b, j * HF + c0:j * HF + c0 + n], span("dv%d_%d" % (b, j), c0, n)
+            two = n == HF and j in (1, 2) and "V" in PAIRS
+            if two and j == 1:
+                both, bk_ = T["dv" + k][:, b, HF:3 * HF], span("dv%d_2" % b, 0, HF) + hk
+                pair(t, b, offs(b, 0, F, 1), span("un%d" % b, 0, HF), None, both, bk_)
+                act(T["adv" + k][:, b, HF:3 * HF], both, AF.Abs, bk_, span("adv%d_2" % b, 0, HF) + span("adv%d_1" % b, 0, HF))
+            ap, key, bank_ = held, hk, []
             if way and j == 0:
-                ap, key, bk = pc, [c], [bc]
+                ap, key, bank_ = pc, [c], [bc]
             elif way == "p":
-                ap, key, bk = pa, [a], [ba]
-            gather(t, b, c0, n, offs(b, c0, n, j), span("un%d" % b, c0, n), way, ap, bk + key)
-            act(T.adv[:, b, j, c0:c0 + n], ap, AF.Abs, key, bk + span("adv%d_%d" % (b, j), c0, n))
+                ap, key, bank_ = pa, [a], [ba]
+            gather(t, b, c0, n, None if two else offs(b, c0, n, j), span("un%d" % b, c0, n), way, held, hk, ap, bank_ + key)
+            if not two and (j != 1 or SIZE[t] == "a"):
+                act(T["adv" + k][:, b, j * HF + c0:j * HF + c0 + n], ap, AF.Abs, key, bank_ + span("adv%d_%d" % (b, j), c0, n))
             d.append(ap)
             dk.append(key)
             if j == 0 and not way:
-                act(pc, ap, AF.Copy, key, [bc, c])
+                if COPY[t] == "a":
+                    act(pc, ap, AF.Copy, key, [bc, c])
+                else:
+                    sums(t, pc, [bc, c], [(1, ap, key)])
             if j == 1:
-                act(tm[3], ap, AF.Relu, key, bk + [tk[3]], scale=-1.0)
-                act(tm[4], ap, AF.Relu, key, bk + [tk[4]])
-                act(pa, tm[3], AF.Copy, [tk[3]], [ba, a], scale=-1.0)
+                act(up, ap, AF.Relu, key, bank_ + uk)
+                if LOW[t] == "a":
+                    act(tm[3], ap, AF.Relu, key, bank_ + [tk[3]], scale=-1.0)
+                    act(pa, tm[3], AF.Copy, [tk[3]], [ba, a], scale=-1.0)
+                elif LOW[t] == "v":
+                    ts(pa, ap, 0.0, None, ALU.min, None, key, [ba, a])
+                else:
+                    sums(t, pa, [ba, a], first(t, b, c0, n, 1) + [(-1, up, uk)])
         tt(tm[0], pc, d[2], ALU.min, [c] + dk[2], [bc, tk[0]])
         tt(pc, pc, d[2], ALU.max, [c] + dk[2], [bc, c])
         tt(pa, pa, tm[0], ALU.max, [a, tk[0]], [ba, a])
-        tt(tm[1], pc, tm[4], ALU.min, [c, tk[4]], [bc, tk[1]])
+        tt(tm[1], pc, up, ALU.min, [c] + uk, [bc, tk[1]])
         tt(pc, pa, tm[1], ALU.max, [a, tk[1]], [ba, bc, c])
         tt(pa, pa, tm[1], ALU.min, [a, tk[1]], [ba, a])
         tt(tm[2], pc, d[3], ALU.min, [c] + dk[3], [bc, tk[2]])
-        mo, mk = (T.mob if t < 2 else T.mof)[:, cc:cc + n], span("mo", cc, n)
+        mo, mk = T["mo" + k][:, cc:cc + n], span("mo", cc, n)
         if t < R - 1:
             tt(mo, pa, tm[2], ALU.max, [a, tk[2]], [ba] + mk)
             nxt = "xt%d" % (t + 1)
-            mm(nx, T[am][:], mo, False, True, [am] + mk, nw, wide=t >= 2)
+            mm(nx, T["am" + k][:], mo, False, True, ["am" + k] + mk, nw, wide=t >= 2)
             act(direct(nxt, cc, n), nx, AF.Relu, nw[1:], nw[:1] + span(nxt, cc, n))
             send()
-            load("s", T["xo%d" % (t + 1)][:, cc:cc + n], direct(nxt, cc, n), span("xo%d" % (t + 1), cc, n), "xo%d" % (t + 1), r=span(nxt, cc, n))
+            for h in range(2):
+                load("s", T["xo%d" % (t + 1)][:, b, h * HF + c0:h * HF + c0 + n], direct(nxt, cc, n), span("xo%d%s" % (t + 1, "ab"[h]), cc, n),
+                     "xo%d" % (t + 1), r=span(nxt, cc, n))
         else:
             tt(pa, pa, tm[2], ALU.max, [a, tk[2]], [ba, a])
             tt(mo, pa, direct(tab, cc, n), ALU.add, [a] + span(tab, cc, n), [ba] + mk)
             act(T.yes[:, cc:cc + n], mo, AF.Square, mk, span("yes", cc, n))
-            out = bank(5 * s + 1, 0, n, slice(0, 16))
+            out = at(c, 0, n, slice(0, 16))
             mm(out, T.km[:], T.yes[:, cc:cc + n], True, True, ["km"] + span("yes", cc, n), [bc, c], wide=True)
             act(T.yds[0:16, cc:cc + n], out, AF.Copy, [c], [bc] + span("yds", cc, n))
 
     def unit_b(u):
         b, c0, n = UNITS_B[u]
-        return b, c0, n, u % 2, n // 16, n // 4, (3, 7)[u % 2], [(o, min(128, o0 + n0 - o)) for o0, n0 in PARTS[u] for o in range(o0, o0 + n0, 128)]
+        return b, c0, n, u % 2, n // 16, n // 4, [(o, min(128, o0 + n0 - o)) for o0, n0 in PARTS[u] for o in range(o0, o0 + n0, 128)]
 
-    def tolist(out, o, n, keys, w):
+    def tolist(out, o, n, keys, w, start=True, stop=True):
         for k0 in range(0, 16, 4):
-            mms([(out, T.dm[:, k * 128:(k + 1) * 128], T.wide[:, o + k:o + 4 * n:16], k == 0, k == 15) for k in range(k0, k0 + 4)], keys + dmk, w)
+            mms([(out, onto(k), T.wide[:, o + k:o + 4 * n:16], start and k == 0, stop and k == 15) for k in range(k0, k0 + 4)], keys + dmk, w)
 
     def challengers(t, u):
-        b, c0, n, s, na, L, cb, tiles = unit_b(u)
-        tab, a0, bk = "nt%d" % t, c0 // 16, "B%d" % cb
+        b, c0, n, s, na, L, tiles = unit_b(u)
+        tab, a0 = "nt%d" % t, c0 // 16
         for j in range(M):
             c = s * 1280 + j * n
             out, src, keep = T.wide[:, c:c + n], T[tab][:].indirect(offs(b, c0, n, j)), col(8 + (j + t) % M)
             r, w = whole(tab) + span("un%d" % b, c0, n) + ["mask"], ["cg%d_%d" % (s, j)]
-            if u == 0 and j in SHARED:
+            if j in SHARED[t][u]:
                 ts(out, src, keep, None, ALU.mult, None, r, w, c=gcost(n))
             else:
                 act(out, src, AF.Copy, r, w, scale=keep, c=gcost(n))
-        cl, pc_, pt_, cs = "cl%d" % s, bank(cb, 0, L), bank(cb, 80, L), T.cs[:, s * 80:s * 80 + L]
-        tolist(pc_, s * 1280, n, ["cg%d_%d" % (s, j) for j in range(M)], [bk, cl])
-        act(cs, pc_, AF.Copy, [cl], [bk, "cs%d" % s])
+        cl, pt = "cl%d" % s, "pt%d" % s
+        pc_, cs, bl = at(cl, 0, L), T.cs[:, s * 80:s * 80 + L], bk(cl)
+        tolist(pc_, s * 1280, n, ["cg%d_%d" % (s, j) for j in range(M)], [bl, cl])
+        if LIST[u] == "a":
+            act(cs, pc_, AF.Copy, [cl], [bl, "cs%d" % s])
+        else:
+            cp(cs, pc_, [cl], [bl, "cs%d" % s])
         nk = span("nd%d" % b, c0, n)
-        tt(T.eq[:, s, 0, 0:L], pc_, T.own[:, b, :, a0:a0 + na], ALU.is_equal, [cl, "own"], [bk, "eq%d_0" % s])
+        tt(T.eq[:, s, 0, 0:L], pc_, T.own[:, b, :, a0:a0 + na], ALU.is_equal, [cl, "own"], [bl, "eq%d_0" % s])
         for i in range(1, M):
-            tt(T.eq[:, s, i, 0:L], pc_, T.nd[:, b, i:i + 4, a0:a0 + na], ALU.is_equal, [cl] + nk + span("ndd%d" % b, c0, n), [bk, "eq%d_%d" % (s, i)])
-        tt(pt_, pc_, T.nd[:, b, 0:4, a0:a0 + na], ALU.subtract, [cl] + nk, [bk, "pt%d" % s])
+            tt(T.eq[:, s, i, 0:L], pc_, T.nd[:, b, i:i + 4, a0:a0 + na], ALU.is_equal, [cl] + nk + span("ndd%d" % b, c0, n), [bl, "eq%d_%d" % (s, i)])
         for i in range(1, M):
-            tt(T.eq[:, s, 3 + i, i * na:L], bank(cb, i * na, L - i * na), T.cs[:, s * 80:s * 80 + L - i * na], ALU.is_equal,
-               [cl, "cs%d" % s], [bk, "eq%d_%d" % (s, 3 + i)])
-        mm(bank(4, 0, L), T.idf[:], cs, True, False, ["idf", "cs%d" % s], ["B4", "bv"], wide=True)
-        for part in ((0, 1, 2, 3), (4, 5), (6,)):
-            mms([(bank(4, max(0, i - 3) * na, L - max(0, i - 3) * na), T.far[:], T.eq[:, s, i, max(0, i - 3) * na:L], False, i == 6) for i in part],
-                ["far"] + ["eq%d_%d" % (s, i) for i in part], ["B4", "bv"])
-        ts(T.uc[:, s * 80:s * 80 + L], bank(4, 0, L), float(W), None, ALU.min, None, ["bv"], ["B4", "uc%d" % s])
+            tt(T.eq[:, s, 3 + i, i * na:L], at(cl, i * na, L - i * na), T.cs[:, s * 80:s * 80 + L - i * na], ALU.is_equal,
+               [cl, "cs%d" % s], [bl, "eq%d_%d" % (s, 3 + i)])
+        if t < R - 1:
+            bv = "bv%d" % s
+            mm(at(bv, 0, L), T.idf[:], cs, True, False, ["idf", "cs%d" % s], [bk(bv), bv], wide=True)
+            for part in ((0, 1, 2, 3), (4, 5, 6)):
+                mms([(at(bv, max(0, i - 3) * na, L - max(0, i - 3) * na), T.far[:], T.eq[:, s, i, max(0, i - 3) * na:L], False, i == 6) for i in part],
+                    ["far"] + ["eq%d_%d" % (s, i) for i in part], [bk(bv), bv])
+            ts(T.uc[:, s * 80:s * 80 + L], at(bv, 0, L), float(W), None, ALU.min, None, [bv], [bk(bv), "uc%d" % s])
+        else:
+            cp(T.uc[:, s * 80:s * 80 + L], pc_, [cl], [bl, "uc%d" % s])
+        tt(at(pt, 0, L), pc_, T.nd[:, b, 0:4, a0:a0 + na], ALU.subtract, [cl] + nk, [bl, bk(pt), pt])
 
     def wins(out, src, r, w):
         act(out, src, AF.Sigmoid, r, w, bias=-2176.0, scale=256.0)
 
     def challenge(t, u):
-        b, c0, n, s, na, L, cb, tiles = unit_b(u)
-        a0, bk, wd, cc = c0 // 16, "B%d" % cb, 64 * len(tiles), b * HF + c0
+        b, c0, n, s, na, L, tiles = unit_b(u)
+        a0, cc, k = c0 // 16, b * HF + c0, kind(t)
         tab, nxt = "nt%d" % t, "nt%d" % (t + 1)
+        cf, df, b2, bc, pt = ["%s%d" % (x, s) for x in ("cf", "df", "b2", "bc", "pt")]
         more = t < R - 1
         if more:
             for i, (o, m) in enumerate(tiles):
-                out = bank(6, i * 64, 64, slice(0, m))
+                out = at(df, i * 64, 64, slice(0, m))
                 c = s * 1280 + o
                 mms([(out, direct(tab, cc + o, m), T.gn[:], True, False)]
                     + [(out, T.wide[:, c + j * n:c + j * n + m], T.gdf[:, 6 - 2 * j:70 - 2 * j], False, j == M - 1) for j in range(M)],
-                    span(tab, cc + o, m) + ["gn", "gdf"] + ["cg%d_%d" % (s, j) for j in range(M)], ["B6", "df"])
+                    span(tab, cc + o, m) + ["gn", "gdf"] + ["cg%d_%d" % (s, j) for j in range(M)], [bk(df), df])
         for o0, n0 in (PARTS[u] if more else [(0, n)]):
             some = [(i, o, m) for i, (o, m) in enumerate(tiles) if o0 <= o < o0 + n0]
-            w0, wd, tk = 64 * some[0][0], 64 * len(some), "%d" % some[0][0]
+            w0, wd, tk = 64 * some[0][0], 64 * len(some), "%d_%d" % (s, some[0][0])
             if more:
-                mm(bank(2, o0, n0), T.idb[:], direct(tab, cc + o0, n0), True, False, ["idb"] + span(tab, cc + o0, n0), ["B2", "b2"])
-                mm(bank(5, w0, wd), T.idb[:], T.zb[:, 0:wd], True, False, ["idb", "zb", "zc"], ["B5", "cf_"])
+                mm(at(b2, o0, n0), T.idb[:], direct(tab, cc + o0, n0), True, False, ["idb"] + span(tab, cc + o0, n0), [bk(b2), b2])
+                mm(at(cf, w0, wd), T.idb[:], T.zb[:, 0:wd], True, False, ["idb", "zb", "zc"], [bk(cf), cf])
             for j in range(M):
-                way = SIDE_U[t].get(j)
-                au, ab, ak = bank(j % 2, 0, n0), "B%d" % (j % 2), "au%d" % (j % 2)
+                way = SIDE_U[t][u].get(j)
+                ak = AU[u][j]
+                au, ab = at(ak, 0, n0), bk(ak)
                 a1 = s * 80 + j * na + o0 // 16
-                off, du, dk = T.uc[:, a1:a1 + n0 // 16], T.du[:, j, o0:o0 + n0], span("du%d" % j, o0, n0)
+                off, du, dk = T.uc[:, a1:a1 + n0 // 16], T["du" + k][:, s, j * HF + o0:j * HF + o0 + n0], span("du%d_%d" % (s, j), o0, n0)
+                if n0 == HF and way == SIDE_U[t][u].get(j ^ 1) and ("U" if way is None else "S") in PAIRS:
+                    if j % 2 == 0:
+                        pair(t, b, T.uc[:, a1:a1 + 2 * na], ["uc%d" % s], way, T["du" + k][:, s, j * HF:(j + 2) * HF],
+                             span("du%d_%d" % (s, j + 1), 0, HF) + dk)
+                    off = None
+                c = 2560 + s * 1280 + j * n
+                nr, nrk = T.wide[:, c + o0:c + o0 + n0], "nr%d_%d" % (s, j)
                 if way == "p":
-                    gather(t, b, c0 + o0, n0, off, ["uc%d" % s], way, au, [ab, ak])
+                    gather(t, b, c0 + o0, n0, off, ["uc%d" % s], way, du, dk, au, [ab, ak])
                     act(au, au, AF.Abs, [ak], [ab, ak])
                 else:
-                    gather(t, b, c0 + o0, n0, off, ["uc%d" % s], way, du, dk)
-                    act(au, du, AF.Abs, dk, [ab, ak])
-                c = 2560 + s * 1280 + j * n
-                tt(T.wide[:, c + o0:c + o0 + n0], au, T.adv[:, b, j, c0 + o0:c0 + o0 + n0], ALU.is_lt,
-                   [ak] + span("adv%d_%d" % (b, j), c0 + o0, n0), [ab, "nr%d_%d" % (s, j)])
+                    gather(t, b, c0 + o0, n0, off, ["uc%d" % s], way, du, dk, du, dk)
+                if j == 1 and SIZE[t] == "p":
+                    act(du, du, AF.Abs, dk, dk)
+                    for b_, o, m in UNITS_A:
+                        lo, hi = max(o, c0 + o0), min(o + m, c0 + o0 + n0)
+                        if b_ == b and lo < hi:
+                            sums(t, at(ak, lo - c0 - o0, hi - lo), [ab, ak],
+                                 [(2, T["up" + k][:, b, lo:hi], span("up%d" % b, lo, hi - lo))] + first(t, b, lo, hi - lo, -1))
+                    tt(nr, au, du, ALU.is_gt, [ak] + dk, [ab, nrk])
+                else:
+                    if way != "p":
+                        act(au, du, AF.Abs, dk, [ab, ak])
+                    tt(nr, au, T["adv" + k][:, b, j * HF + c0 + o0:j * HF + c0 + o0 + n0], ALU.is_lt, [ak] + span("adv%d_%d" % (b, j), c0 + o0, n0), [ab, nrk])
                 if more:
-                    mms([(bank(5, i * 64, 64, slice(0, m)), T.wide[:, c + o:c + o + m], T.gcf[:, 6 - 2 * j:70 - 2 * j], False,
-                          j == M - 1 and i == some[0][0]) for i, o, m in some[::-1]], ["nr%d_%d" % (s, j), "gcf"], ["B5", "cf_"])
+                    mms([(at(cf, i * 64, 64, slice(0, m)), T.wide[:, c + o:c + o + m], T.gcf[:, 6 - 2 * j:70 - 2 * j], False,
+                          j == M - 1 and i == some[0][0]) for i, o, m in some[::-1]], [nrk, "gcf"], [bk(cf), cf])
             if more:
-                wins(T.wf[:, w0:w0 + wd], bank(5, w0, wd), ["cf_"], ["B5", "wf" + tk])
-                tt(T.tf[:, w0 // 8:(w0 + wd) // 8, 0:8], bank(6, w0, wd), T.wf[:, w0:w0 + wd], ALU.mult, ["df", "wf" + tk, "tf"], ["B6", "tf" + tk])
-                mms([(bank(2, o, m), T.tf[0:m, 8 * i:8 * i + 8, :], T.idb[0:m, 0:m], False, i == some[-1][0]) for i, o, m in some],
-                    ["tf" + tk, "idb"], ["B2", "b2"])
-                act(direct(nxt, cc + o0, n0), bank(2, o0, n0), AF.Copy, ["b2"], ["B2"] + span(nxt, cc + o0, n0))
+                wf, tf = T.wf[:, s, w0:w0 + wd], T.tf[:, s * 24 + w0 // 8:s * 24 + (w0 + wd) // 8, 0:8]
+                wins(wf, at(cf, w0, wd), [cf], [bk(cf), "wf" + tk])
+                tt(tf, at(df, w0, wd), wf, ALU.mult, [df, "wf" + tk, "tf"], [bk(df), "tf" + tk])
+                mms([(at(b2, o, m), T.tf[0:m, s * 24 + 8 * i:s * 24 + 8 * i + 8, :], T.idb[0:m, 0:m], False, i == some[-1][0]) for i, o, m in some],
+                    ["tf" + tk, "idb"], [bk(b2), b2])
+                act(direct(nxt, cc + o0, n0), at(b2, o0, n0), AF.Copy, [b2], [bk(b2)] + span(nxt, cc + o0, n0))
                 send()
-        tolist(bank(4, 80, L), 2560 + s * 1280, n, ["nr%d_%d" % (s, j) for j in range(M)], ["B4", "bc"])
-        wl, pt_, nd = T.wl[:, s * 80:s * 80 + L], bank(cb, 80, L), T.nd[:, b, 0:4, a0:a0 + na]
+        if not more:
+            mms([(at(bc, max(0, i - 3) * na, L - max(0, i - 3) * na), T.off[:], T.eq[:, s, i, max(0, i - 3) * na:L], i == 0, False) for i in range(7)],
+                ["off"] + ["eq%d_%d" % (s, i) for i in range(7)], [bk(bc), bc])
+        tolist(at(bc, 0, L), 2560 + s * 1280, n, ["nr%d_%d" % (s, j) for j in range(M)], [bk(bc), bc], more)
+        wl, pt_, nd = T.wl[:, s * 80:s * 80 + L], at(pt, 0, L), T.nd[:, b, 0:4, a0:a0 + na]
         nk = span("nd%d" % b, c0, n)
-        wins(wl, bank(4, 80, L), ["bc"], ["B4", "wl%d" % s])
-        tt(pt_, pt_, wl, ALU.mult, ["pt%d" % s, "wl%d" % s], [bk, "pt%d" % s])
+        wins(wl, at(bc, 0, L), [bc], [bk(bc), "wl%d" % s])
+        tt(pt_, pt_, wl, ALU.mult, [pt, "wl%d" % s], [bk(pt), pt])
         if more:
-            tt(nd, pt_, nd, ALU.add, ["pt%d" % s] + nk, [bk] + nk)
-            cp(T.un[:, b, :, a0:a0 + na], nd, nk, span("un%d" % b, c0, n))
+            tt(nd, pt_, nd, ALU.add, [pt] + nk, [bk(pt)] + nk)
+            cp(T.un[:, b], nd, nk, span("un%d" % b, c0, n))
             act(T.nd[:, b, 4:7, a0:a0 + na], T.nd[:, b, 0:3, a0:a0 + na], AF.Copy, nk, span("ndd%d" % b, c0, n))
         else:
-            tt(T.yns[:, :, b * HL + a0:b * HL + a0 + na], pt_, nd, ALU.add, ["pt%d" % s] + nk, [bk] + span("yns", cc, n))
+            tt(T.yns[:, :, b * HL + a0:b * HL + a0 + na], pt_, nd, ALU.add, [pt] + nk, [bk(pt)] + span("yns", cc, n))
 
     for t in range(R):
-        if "s" in list(SIDE_V[t].values()) + list(SIDE_U[t].values()):
+        if "s" in list(SIDE_V[t].values()) + list(SIDE_F[t].values()) + [x for ways in SIDE_U[t] for x in ways.values()]:
             for b in range(2):
-                act(bank(3 + b, 160, HF), direct("xt%d" % t, b * HF, HF), AF.Copy, span("xt%d" % t, b * HF, HF), ["B%d" % (3 + b), "xf%d" % b])
+                act(at("xf%d" % b), direct("xt%d" % t, b * HF, HF), AF.Copy, span("xt%d" % t, b * HF, HF), [bk("xf%d" % b), "xf%d" % b])
         for u in range(len(UNITS_A)):
             medians(t, u)
         if t == R - 1:

from concourse.bass import DstId, RemoteDMATransfer
from concourse.mybir import AluOpType as ALU, ActivationFunctionType as AF, AxisListType as AX

N, F, M, R, WORLD = 6, 640, 4, 5, 256
W = N * F
HF, HL = F // 2, F // 32
XD = ["bfloat16", "bfloat16", "float32", "float32", "float32"]

UNITS_A = [(0, 0, 320), (1, 0, 320)]
PAIRS = "VUS"
UNITS_B = [(0, 0, 320), (1, 0, 320)]
PARTS = [[(0, 320)], [(0, 320)]]
SIDE_V = [{0: "p", 3: "s"}] * 2 + [{0: "s", 3: "s"}] * 3
SIDE_F = SIDE_V
SIDE_U = [[{3: "s"}, {3: "s"}]] * 2 + [[{2: "s", 3: "s"}, {2: "s", 3: "s"}]] * 3
SHARED = [[(0, 1), ()]] * 2 + [[(0,), ()]] * 3
LOW, COPY, SIZE, LIST = "aaaaa", "aaaaa", "aaaaa", "va"
BANKS = [("pa0 au0 rows0", "df0"), ("pc0 au1 rows1", "df1"), ("nx0 b20 b21", "cl0 cl1"), ("nx1", "bc0 bc1"),
         ("xf0", "cf0"), ("xf1", "cf1"), ("au2 pa1", "pt0 pt1"), ("au3 pc1", "bv0 bv1")]
AU = [["au0", "au1", "au2", "au3"]] * 2

SCRATCH = {
    "nbi": ("sbuf", [128, 4, 40], "int32"), "pti": ("sbuf", [128, 8, 40], "int32"), "ptb": ("sbuf", [128, 2, 160], "bfloat16"),
    "mixs": ("sbuf", [128, F], "bfloat16"), "wide": ("sbuf", [128, 5120], "bfloat16"),
    "tmp": ("sbuf", [128, 3, 4, HF], "float32"),
    "yes": ("sbuf", [128, F], "float32"), "yds": ("sbuf", [128, F], "float32"), "yns": ("sbuf", [128, 4, 40], "float32"),
    "nd": ("sbuf", [128, 2, 7, HL], "float32"), "own": ("sbuf", [128, 2, 4, HL], "float32"),
    "un": ("sbuf", [128, 2, 4 * HL], "uint16"), "cs": ("sbuf", [128, 160], "float32"), "uc": ("sbuf", [128, 160], "uint16"),
    "eq": ("sbuf", [128, 2, 7, 80], "bfloat16"), "wl": ("sbuf", [128, 160], "bfloat16"), "zt": ("sbuf", [128, 2, 160], "bfloat16"),
    "far": ("sbuf", [128, 128], "bfloat16"), "off": ("sbuf", [128, 128], "bfloat16"),
    "wf": ("sbuf", [128, 2, 192], "bfloat16"), "tf": ("sbuf", [128, 48, 16], "bfloat16"), "zb": ("sbuf", [128, 192], "bfloat16"),
    "ci": ("sbuf", [128, 128], "float32"), "cm": ("sbuf", [128, 128], "float32"), "ch": ("sbuf", [128, 72], "float32"),
    "pi": ("sbuf", [128, 8], "int32"), "cf": ("sbuf", [128, 24], "float32"), "km": ("sbuf", [128, 16], "float32"),
    "b8": ("sbuf", [128, 128], "bfloat16"),
    "gcf": ("sbuf", [128, 72], "bfloat16"), "gdf": ("sbuf", [128, 72], "bfloat16"), "gn": ("sbuf", [128, 64], "bfloat16"),
    "ps": ("psum", [128, 4096], "float32"),
}
for _k, _d in (("b", "bfloat16"), ("f", "float32")):
    SCRATCH.update({"dv" + _k: ("sbuf", [128, 2, 4 * HF], _d), "adv" + _k: ("sbuf", [128, 2, 4 * HF], _d), "du" + _k: ("sbuf", [128, 2, 4 * HF], _d),
                    "up" + _k: ("sbuf", [128, 2, HF], _d), "mo" + _k: ("sbuf", [128, F], _d)})
    SCRATCH.update({_m + _k: ("sbuf", [128, 128], _d) for _m in ("id", "neg", "two", "am")})
for _t in range(R):
    SCRATCH["xt%d" % _t] = ("sbuf", [128, W + 16 * (_t < R - 1)], XD[_t])
    SCRATCH["nt%d" % _t] = ("sbuf", [128, W], "bfloat16")
    SCRATCH["xo%d" % _t] = ("sbuf", [128, 2, F], XD[_t])
PLACE = {k: (b, 0, HF) for b, x in enumerate(BANKS) for k in x[0].split()}
PLACE.update({k: (b, HF + 80 * i, 80 if " " in y else 192)
              for b, x in enumerate(BANKS) for y in x[1].split("|") for i, k in enumerate(y.split())})

EVENTS = [("xt0", 0, HF, "a"), ("xt0", HF, HF, "b"), ("nt0", 0, HF, "e"), ("nt0", HF, HF, "d")]
for _t in range(1, R):
    EVENTS += [("xt%d" % _t, u[0] * HF + u[1], u[2], "ca"[UNITS_A.index(u)]) for u in UNITS_A]
    EVENTS += [("nt%d" % _t, u[0] * HF + u[1] + o, n, "ed"[u[0]]) for u, ps_ in zip(UNITS_B, PARTS) for o, n in ps_]
WAYS = {"a": [(None, 0), (None, 2), ("own", None), ("other", None), ("other", None)],
        "b": [(None, 1), (None, 3), ("own", None), ("other", None), ("other", None)],
        "c": [(None, None), (None, 1), ("other", None), ("other", 0), ("other", 3)],
        "d": [(None, 0), (None, None), ("own", None), ("other", None), ("other", None)],
        "e": [(None, 1), (None, 3), ("own", None), ("own", None), ("other", None)]}
ROUTES = []

GATHER, HAND, FLY, LOCAL, PE = (65, 1.6), 230, (4200, 2.8, 4000), 2300, 0.9
SPEEDS = [(1.2, 1.05, 270, 1.0), (1.6, 0.9, 220, 0.6), (1.9, 0.75, 180, 1.0)]
TESTS = []
PLANS, TURNS, TRIES, SHIFT, SLACK, ALL = 7, 7, 150, 1000, 200, 0.3
POLISH, LAST, WIDTH, BAR, EASE = 400, 600, 8, 100, 30
ORDER = []
SEMAPHORES = (["sv", "sa", "sp", "sg", "ldx", "ldn", "ldm", "sto", "sent"] + ["xo%d" % t for t in range(R)]
              + ["e%s_%d" % e[:2] for e in EVENTS])


def ones(m):
    return bin(m).count("1")


def routes(T, topo):
    if ROUTES:
        return ROUTES
    cores = list(T.cores)
    beside = [[h for h in range(WORLD) if topo.mates(h, c) and topo.may_write(h, c)] for c in cores]
    firsts = sorted(set(topo.cores_of(c)[0] for c in range(WORLD)))
    mate = {a: b for a in firsts for b in firsts if topo.mates(a, b)}

    def deal(roles, ds):
        ways, load = [], {}
        for s, c in enumerate(cores):
            way, used = [], []
            legs = [(die, ([] if relay is None else [beside[(s + d) % N][relay]]) + [cores[(s + d) % N]]) for (die, relay), d in zip(roles, ds)]
            for die, path in sorted(legs, key=lambda x: topo.same_plane(c, x[1][0])):
                if die:
                    able = [h for h in topo.cores_of(c) if h != c and (topo.die(h) == topo.die(c)) == (die == "own") and topo.may_write(h, path[0])]
                    used.append(min(able, key=lambda h: (h in used, all(topo.may_write(h, x) for x in cores if x != c) and topo.same_plane(c, path[0]))))
                    path = used[-1:] + path
                path = [c] + path
                for a, b in zip(path, path[1:]):
                    links, here = [], topo.cores_of(a)[0]
                    if a not in topo.cores_of(b) and not topo.same_plane(a, b):
                        links.append(("mate", here))
                        here = mate[here]
                    if here not in topo.cores_of(b):
                        links += [("out", here), ("in", topo.cores_of(b)[0])]
                    for k in links:
                        load[k, topo.die(a)] = load.get((k, topo.die(a)), 0) + 1
                way.append(path)
            ways.append(way)
        return sorted(load.values(), reverse=True), ways, load

    def orders(left):
        return [[d] + rest for d in left for rest in orders([x for x in left if x != d])] if left else [[]]
    alone = {k: [deal(roles, ds) for ds in orders(list(range(1, N)))] for k, roles in WAYS.items()}
    alone = {k: [x for x in v if x[0][0] == min(y[0][0] for y in v)] for k, v in alone.items()}
    share = {k: sum(e[2] * (2 if T[e[0]].dtype == T.xt4.dtype else 1) for e in EVENTS if e[3] == k) for k in WAYS}
    best = {k: v[0] for k, v in alone.items()}

    def together(k, x):
        load = {}
        for k2 in WAYS:
            for link, n in (x if k2 == k else best[k2])[2].items():
                load[link] = load.get(link, 0) + n * share[k2]
        return sorted(load.values(), reverse=True)
    for turn in range(2):
        for k in WAYS:
            best[k] = min(alone[k], key=lambda x: together(k, x))
    ROUTES.extend({k: best[k][1][s] for k in WAYS} for s in range(N))
    return ROUTES


def piece(T, ev, rank):
    return T[ev[0]][:, rank * F + ev[1]:rank * F + ev[1] + ev[2]]


def transfer(T, topo, src, dsts, ev, rank, mask):
    ids = [DstId(rid=topo.addr(d, src)[0], pnc=topo.addr(d, src)[1]) for d in dsts]
    return RemoteDMATransfer(dst_ids=ids, dma_engine_mask=mask, remote_sem=T.sem["e%s_%d" % ev[:2]],
                             srcs=[piece(T, ev, rank)], dsts=[piece(T, ev, rank) for d in dsts])


def helper_program(g, core, T, topo, rts):
    sent = 0
    for ev in EVENTS:
        for rank in range(N):
            paths = [p for p in rts[rank][ev[3]] if core in p]
            if paths:
                dsts = [p[p.index(core) + 1] for p in paths]
                far = topo.mask(core, dsts[0])
                g.wait_ge(T.sem["e%s_%d" % ev[:2]], ones(topo.mask(paths[0][paths[0].index(core) - 1], core) & ~far or far))
                g.remote_dma_fused([transfer(T, topo, core, dsts, ev, rank, far)], local_sem=T.sem.sent)
                sent += ones(far)
    if sent:
        g.wait_ge(T.sem.sent, sent)


def make_emitter(g, T):
    q = {"v": g.vector, "a": g.scalar, "p": g.tensor, "g": g, "s": g.sync}
    sem = {"v": "sv", "a": "sa", "p": "sp", "g": "sg"}
    count = {k: 0 for k in sem}
    known = {k: {} for k in q}
    clock, writer, readers = {}, {}, {}

    def apart(e, k, r):
        return e in "pgsl" or k[0] == "B" or k == "mask" or (e == "v" and k[0] == "P" and k in r)

    edges = {b: sorted(set(x for p in PLACE.values() if p[0] == b for x in (p[1], p[1] + p[2]))) for b in range(8)}
    same = {k: ["P%d:%d" % (b, x) for x in edges[b] if c <= x < c + n] for k, (b, c, n) in PLACE.items()}

    def need(e, s, n):
        if known[e].get(s, 0) >= n:
            return
        q[e].wait_ge(T.sem[s], n)
        known[e][s] = n
        for s2, n2 in clock.get((s, n), {}).items():
            known[e][s2] = max(known[e].get(s2, 0), n2)

    def op(e, call, r, w, dma):
        deps = {}
        mine = sem.get(e)
        for k in r:
            if k in writer:
                deps[writer[k]] = 1
        for k in w:
            for d in readers.get(k, []) + ([writer[k]] if k in writer else []):
                if d[0] != mine or dma or not apart(e, k, r):
                    deps[d] = 1
        top = {}
        for s, n in deps:
            top[s] = max(top.get(s, 0), n)
        for s in sorted(top, key=lambda s: s == mine):
            need(e, s, top[s])
        ins = call(q[e])
        if dma == "remote":
            return
        if dma:
            ins.then_inc(T.sem[dma], 16)
            me = (dma, total[dma])
        else:
            count[e] += 1
            ins.then_inc(T.sem[mine], 1)
            me = (mine, count[e])
        clock[me] = dict(known[e])
        for k in r:
            readers.setdefault(k, []).append(me)
        for k in w:
            writer[k] = me
            readers[k] = []

    def outside(key, s, n):
        writer[key] = (s, n)

    calls, total = [], {}

    def note(e, call, r=(), w=(), dma=None, c=100, far=(), kind=""):
        r, w = [[x for k in keys for x in same.get(k, [k])] for keys in (r, w)]
        calls.append((e, call, r, w, dma, c, far, e + kind))
        if dma and dma != "remote":
            total[dma] = total.get(dma, 0) + 16

    def arrange():
        n_ = len(calls)
        pre = [dict() for c in calls]
        wr, rd, sends = {}, {}, {}
        for i, (e, call, r, w, dma, c, far, kind) in enumerate(calls):
            for k in r:
                if k in wr:
                    pre[i][wr[k]] = max(pre[i].get(wr[k], 0), HAND)
                if k in sends:
                    pre[i][sends[k][0]] = max(pre[i].get(sends[k][0], 0), sends[k][1])
            for k in w:
                if k[0] == "B" and e != "p":
                    continue
                for d in rd.get(k, []) + ([wr[k]] if k in wr else []):
                    if d != i and (calls[d][0] != "l" or e == "l"):
                        pre[i][d] = max(pre[i].get(d, 0), HAND if calls[d][0] != e or not apart(e, k, r) else 0)
            for k in r:
                rd.setdefault(k, []).append(i)
            for k in w:
                if k[0] != "B" or e == "p":
                    wr[k] = i
                    rd[k] = []
            for k, lag in far:
                sends[k] = (i, lag)
        length = [c[5] for c in calls]
        rest, back = list(length), [dict() for c in calls]
        for i in range(n_ - 1, -1, -1):
            for d, lag in pre[i].items():
                rest[d] = max(rest[d], length[d] + lag + rest[i])
                back[d][i] = lag
        eng = [c[0] for c in calls]
        busy = [(100 if c[4] == "remote" else 150) if c[4] else c[5] for c in calls]
        uses = [[c[0]] + sorted(set(k for k in c[3] if k[0] == "B")) for c in calls]
        spots_ = list(q) + ["l"] + ["B%d" % b for b in range(8)]

        def run(before, key, turned):
            seq = range(n_ - 1, -1, -1) if turned else range(n_)
            key = list(key)
            for i in seq:
                for d in before[i]:
                    if key[d] >= key[i]:
                        key[i] = key[d] + 0.01
            done, starts, ends, whose = [0] * n_, {k: [] for k in spots_}, {k: [] for k in spots_}, {k: [] for k in spots_}
            for i in sorted(seq, key=lambda i: key[i]):
                at = 0
                for d, lag in before[i].items():
                    if done[d] + lag > at:
                        at = done[d] + lag
                lead = length[i] - busy[i] if turned else 0
                at += lead
                moved = True
                while moved:
                    moved, spots = False, []
                    for k in uses[i]:
                        st, en, by = starts[k], ends[k], whose[k]
                        lo, hi = 0, len(en)
                        while lo < hi:
                            mid = (lo + hi) // 2
                            if en[mid] + HAND <= at:
                                lo = mid + 1
                            else:
                                hi = mid
                        while lo < len(st):
                            gap = 0 if by[lo] == eng[i] else HAND
                            if en[lo] + gap <= at:
                                lo += 1
                            elif st[lo] < at + busy[i] + gap:
                                at, moved = en[lo] + gap, len(uses[i]) > 1
                                lo += 1
                            else:
                                break
                        spots.append(lo)
                for k, lo in zip(uses[i], spots):
                    starts[k].insert(lo, at)
                    ends[k].insert(lo, at + busy[i])
                    whose[k].insert(lo, eng[i])
                done[i] = at - lead + length[i]
            return done

        def improve(key):
            done = run(pre, key, False)
            late = run(back, [-x for x in done], True)
            key = [-x for x in late]
            done = run(pre, key, False)
            order = sorted(range(n_), key=lambda i: (done[i] - length[i], i))
            return sum(max(replay(order, *s)[0]) for s in speeds) / len(speeds), key, done

        def replay(order, long_, hold, waits, hand, first=0, known_=None):
            done, why = (list(known_[0]), list(known_[1])) if known_ else ([0] * n_, [-1] * n_)
            free, who = {k: 0 for k in spots_}, {k: -1 for k in spots_}
            for i in order[max(0, first - 150):first]:
                for k in uses[i]:
                    free[k], who[k] = done[i] - long_[i] + hold[i], i
            for i in order[first:]:
                at, by = 0, -1
                for d, lag in waits[i]:
                    if done[d] + lag > at:
                        at, by = done[d] + lag, d
                e = eng[i]
                for k in uses[i]:
                    x = free[k] if eng[who[k]] == e or who[k] < 0 else free[k] + hand
                    if x > at:
                        at, by = x, who[k]
                done[i], why[i] = at + long_[i], by
                for k in uses[i]:
                    free[k], who[k] = at + hold[i], i
            return done, why

        def tails(order, s, aft, last, known_):
            long_, hold, waits, hand = s
            tail, who = list(known_), {}
            for i in order[last + 150:last:-1]:
                for k in uses[i]:
                    who[k] = i
            for i in order[last::-1]:
                x, e = 0, eng[i]
                for j, lag in aft[i]:
                    if lag + tail[j] > x:
                        x = lag + tail[j]
                x += long_[i]
                for k in uses[i]:
                    j = who.get(k)
                    if j is not None:
                        y = hold[i] + tail[j] + (0 if eng[j] == e else hand)
                        if y > x:
                            x = y
                    who[k] = i
                tail[i] = x
            return tail

        def guess(order, at, to, seq, runs, ends):
            inside, before, behind, total_ = set(seq), {}, {}, 0
            for i in order[max(0, at - 40):at]:
                for k in uses[i]:
                    before[k] = i
            for i in order[to + 40:to:-1]:
                for k in uses[i]:
                    behind[k] = i
            for (long_, hold, waits, hand), aft, (done, why), tail in zip(speeds, after, runs, ends):
                new, free, who, most = {}, {k: done[i] - long_[i] + hold[i] for k, i in before.items()}, dict(before), 0
                for i in seq:
                    x, e = 0, eng[i]
                    for d, lag in waits[i]:
                        y = (new[d] if d in inside else done[d]) + lag
                        if y > x:
                            x = y
                    for k in uses[i]:
                        if k in who:
                            y = free[k] if eng[who[k]] == e else free[k] + hand
                            if y > x:
                                x = y
                    for k in uses[i]:
                        free[k], who[k] = x + hold[i], i
                    x = new[i] = x + long_[i]
                    if x > most:
                        most = x
                    for j, lag in aft[i]:
                        if j not in inside and x + lag + tail[j] > most:
                            most = x + lag + tail[j]
                for k, j in behind.items():
                    if k in who:
                        most = max(most, free[k] + tail[j] + (0 if eng[who[k]] == eng[j] else hand))
                total_ += most
            return total_ / len(speeds)

        speeds = [([x * slow if c[0] == "l" or c[4] else x * pe / PE if c[0] == "p" else
                    (x - GATHER[0]) * quick / GATHER[1] + GATHER[0] if isinstance(x, float) else x
                    for x, c in zip(length, calls)], slow, hand) for quick, slow, hand, pe in SPEEDS + TESTS]
        speeds = [(long_, [x if b == y else b for x, y, b in zip(long_, length, busy)],
                   [[(d, hand if lag == HAND else lag * slow) for d, lag in p.items()] for p in pre], hand) for long_, slow, hand in speeds]
        speeds, tests = speeds[:len(SPEEDS)], speeds[len(SPEEDS):]
        after = [[[] for i in range(n_)] for s in speeds]
        for s, x in zip(speeds, after):
            for i in range(n_):
                for d, lag in s[2][i]:
                    x[d].append((i, lag))

        kind = [c[7] for c in calls]
        kinds = sorted(set(kind))
        seed = [99]

        def draw():
            seed[0] = (seed[0] * 1103515245 + 12345) % 2147483648
            return (seed[0] >> 8) / 8388608.0

        def shaken():
            best = last = improve([-x + draw() * SHIFT for x in rest])
            for turn in range(TRIES):
                shift = {k: (draw() + draw() - 1.0) * SHIFT for k in kinds if draw() < 0.1}
                lo, hi = (0, n_) if draw() < ALL else sorted((int(draw() * n_), int(draw() * n_)))
                trial = improve([x + shift.get(k, 0.0) if lo <= i < hi else x for i, (x, k) in enumerate(zip(last[1], kind))])
                if trial[0] <= last[0] + SLACK * (1.0 - turn / TRIES):
                    last = trial
                best = min(best, last)
            return sorted(range(n_), key=lambda i: (best[2][i] - length[i], i))

        def joined(best, plans):
            for mark in [i for i in range(n_) if calls[i][4] == "remote"]:
                for span, other in plans:
                    for x, y in ((best[1], other), (other, best[1])):
                        head = x[:x.index(mark)]
                        some = set(head)
                        order = head + [i for i in y if i not in some]
                        best = min(best, (sum(max(replay(order, *s)[0]) for s in speeds) / len(speeds), order))
            return best

        def polished(order, POLISH):
            runs = [replay(order, *s) for s in speeds]
            ends = [tails(order, s, x, n_ - 1, [0] * n_) for s, x in zip(speeds, after)]
            span = sum(max(x[0]) for x in runs) / len(speeds)
            top, barred = (span, order), {}
            for turn in range(POLISH):
                done, why = runs[turn % len(speeds)]
                chain, i = [], done.index(max(done))
                while i >= 0:
                    chain.append(i)
                    i = why[i]
                held = [x for x in range(len(chain) - 1) if chain[x + 1] not in pre[chain[x]]]
                place = {i: x for x, i in enumerate(order)}
                moves = []
                for trial in range(WIDTH if held else 0):
                    x = y = held[int(draw() * len(held))]
                    while draw() < 0.4 and y + 2 < len(chain) and chain[y + 2] not in pre[chain[y + 1]]:
                        y += 1
                    a, b = chain[y + 1], chain[x]
                    at, to = place[a], place[b]
                    if barred.get((chain[x + 1], b), -1) > turn or to - at > 120:
                        continue
                    between = order[at:to + 1]
                    if draw() < 0.5:
                        some = {b}
                        for i in between[-2::-1]:
                            if any(j in some for j in back[i]):
                                some.add(i)
                        seq = [i for i in between if i in some] + [i for i in between if i not in some]
                    else:
                        some = {a}
                        for i in between[1:]:
                            if any(j in some for j in pre[i]):
                                some.add(i)
                        seq = [i for i in between if i not in some] + [i for i in between if i in some]
                    if (a in some) != (b in some):
                        moves.append((guess(order, at, to, seq, runs, ends), at, to, seq, a, b))
                if moves and min(moves)[0] <= span + EASE:
                    x, at, to, seq, a, b = min(moves)
                    order = order[:at] + seq + order[to + 1:]
                    runs = [replay(order, *s, at, k) for s, k in zip(speeds, runs)]
                    ends = [tails(order, s, x, to, k) for s, x, k in zip(speeds, after, ends)]
                    span = sum(max(x[0]) for x in runs) / len(speeds)
                    barred[b, a] = turn + BAR
                    top = min(top, (span, order))
            return top

        if not ORDER:
            plans = [polished(shaken(), POLISH) for turn in range(PLANS)]
            top = min(plans)
            for turn in range(TURNS):
                top = polished(joined(top, plans)[1], LAST)
            done, why = replay(top[1], *speeds[len(speeds) // 2])
            ORDER.append((top[0], top[1], why, done, kind, max(rest), pre, length, [int(max(replay(top[1], *s)[0])) // 100 for s in speeds + tests]))
        for i in ORDER[0][1]:
            if eng[i] != "l":
                op(*calls[i][:5])

    def finish(extra):
        arrange()
        for e in sem:
            need("g", sem[e], count[e])
        for s, n in list(total.items()) + extra:
            need("g", s, n)
    return note, outside, finish


def rank_program(g, core, T, topo):
    rts = routes(T, topo)
    rank = T.rank_of(core)
    if rank is None:
        helper_program(g, core, T, topo, rts)
        return
    op, outside, finish = make_emitter(g, T)
    ps = T.ps
    base = rank * F
    sent, turn = [0], [0]
    for ev in EVENTS:
        n = sum(ones(topo.mask(p[-2], core)) for s in range(N) for p in rts[s][ev[3]] if p[-1] == core)
        outside("far%s_%d" % ev[:2], "e%s_%d" % ev[:2], n)

    def span(name, c0, n):
        return ["%s:%d" % (name, c) for c in range(c0 // 32, (c0 + n) // 32)]

    def send():
        ev = EVENTS[turn[0]]
        turn[0] += 1
        paths = sorted(rts[rank][ev[3]], key=lambda p: (-len(p), topo.die(p[1]) == topo.die(core)))
        handed = []
        for p in paths:
            if p[1] in topo.cores_of(core) and p[1] not in handed:
                handed.append(p[1])
        mine = [p[1] for p in paths if p[1] not in handed]
        far = topo.mask(core, mine[0])
        time, lag = FLY[1] * ev[2] * (4 if ev[0] in ("xt2", "xt3", "xt4") else 2), FLY[0] + FLY[2] * (turn[0] == 1)
        if len(paths[0]) == 4:
            time, lag = time / 2, lag * 1.5 + time
        tr = [transfer(T, topo, core, mine, ev, rank, far), transfer(T, topo, core, handed, ev, rank, topo.mask(core, handed[0]) & ~far)]
        sent[0] += ones(far) * len(tr)
        op("g", lambda e: e.remote_dma_fused(tr, local_sem=T.sem.sent), r=span(ev[0], ev[1], ev[2]), w=["sends"], dma="remote", kind="send")
        op("l", None, r=["sends"], w=["links"], c=time, far=[("far%s_%d" % ev[:2], lag)], kind="link")

    def whole(tab):
        return span(tab, 0, F) + ["far%s_%d" % e[:2] for e in EVENTS if e[0] == tab] + ["pad" + tab]

    def size(ap):
        n = 1
        for d in ap.shape[1:]:
            n *= d
        return n

    def name(w):
        return w[-1].split(":")[0]

    def tt(out, a, b, alu, r, w, c=0):
        op("v", lambda e: e.tensor_tensor(out, a, b, alu), r, w, c=c or max(64, size(out)) + 20, kind=name(w))

    def ts(out, a, s1, s2, o0, o1, r, w, c=0):
        if o1 is None:
            op("v", lambda e: e.tensor_scalar(out, a, s1, None, o0), r, w, c=c or max(64, size(out)) + 20, kind=name(w))
        else:
            op("v", lambda e: e.tensor_scalar(out, a, s1, s2, o0, o1), r, w, c=c or max(64, size(out)) + 20, kind=name(w))

    def cp(out, a, r, w):
        op("v", lambda e: e.tensor_copy(out, a), r, w, c=max(64, size(out)) + 20, kind=name(w))

    def fill(ap, v, w):
        op("v", lambda e: e.memset(ap, v), w=w, c=max(64, size(ap) // 2) + 20, kind=name(w))

    def act(out, a, fn, r, w, bias=0.0, scale=1.0, c=0):
        op("a", lambda e: e.activation(out, a, fn, bias=bias, scale=scale), r, w, c=c or max(64, size(out)) + 20, kind=name(w))

    def mm(out, l, rh, start, stop, r, w, wide=False):
        op("p", lambda e: e.matmul(out, l, rh, start, stop), r, w, c=int(max(64, size(rh)) * (4 if wide else 1) * PE), kind=name(w))

    def mms(steps, r, w):
        op("p", lambda e: [e.matmul(*s) for s in steps][-1], r, w, c=int(sum(max(64, size(s[2])) for s in steps) * PE), kind=name(w))

    def load(q, out, in_, w, sem, r=()):
        op(q, lambda e: e.dma_start(out, in_), r=r, w=w, dma=sem, c=LOCAL, kind=sem)

    def gcost(n):
        return GATHER[0] + GATHER[1] * n

    def at(name_, c0=0, n=None, rows=slice(0, 128)):
        b, c, m = PLACE[name_]
        return ps[rows, b * 512 + c + c0:b * 512 + c + c0 + (n or m)]

    def bk(name_):
        return "B%d" % PLACE[name_][0]

    def kind(t):
        return "b" if t < 2 else "f"

    def direct(tab, c, n):
        return T[tab][:, base + c:base + c + n]

    load("s", direct("xt0", 0, F), T.x[:], span("xt0", 0, F), "ldx")
    load("a", T.nbi[:], T.nb[:], ["nbi"], "ldn")
    for h in range(2):
        load("s", T.xo0[:, :, h * HF:(h + 1) * HF], T.x[:], span("xo0" + "ab"[h], 0, F), "xo0")
    load("s", T.mixs[0:16, :], T.mix[:], ["mix"], "ldm")
    fl = dict(allow_small_or_imprecise_dtypes=True)
    op("g", lambda e: e.iota(T.pi[:, 0:1], [[0, 1]], 0, 1), w=["pi0"], c=160)
    op("g", lambda e: e.iota(T.ci[:], [[1, 128]], 0, 0, **fl), w=["ci"], c=420)
    send()
    send()
    op("g", lambda e: e.iota(T.cm[:], [[0, 8], [1, 16]], 0, 0, **fl), r=["sends"], w=["cm"], c=420)
    op("g", lambda e: e.iota(T.ch[:], [[1, 36], [0, 2]], 0, 0, **fl), r=["sends"], w=["ch"], c=300)
    op("g", lambda e: e.iota(T.own[:], [[HF, 2], [0, 4], [16, HL]], base, 1, **fl), r=["sends"], w=["own"], c=480)
    fill(T.zt[:], 0.0, ["zt"])
    for t in range(R - 1):
        fill(T["xt%d" % t][:, W:W + 16], 1024.0, ["padxt%d" % t])
    fill(T.tf[:], 0.0, ["tf"])
    fill(T.zb[:, 0:64], 0.0, ["zb"])
    act(T.zb[:, 64:192], T.ci[:], AF.Sigmoid, ["ci"], ["zc"], bias=-2176.0, c=1700)
    for df in ("df0", "df1"):
        fill(at(df, 128, 64), 0.0, [bk(df), df])
    for c, m in ((1, 112), (2, 15), (3, 1)):
        ts(T.pi[:, c:c + 1], T.pi[:, 0:1], m, None, ALU.bitwise_and, None, ["pi0"], ["pi%d" % c])
    cp(T.cf[:, 0:4], T.pi[:, 0:4], ["pi%d" % c for c in range(4)], ["cf"])
    col = lambda c: T.cf[:, c:c + 1]
    P_, G16, K_, H_ = [col(c) for c in range(4)]
    ts(T.km[:], T.ci[:, 0:16], K_, None, ALU.is_equal, None, ["ci", "cf"], ["km"])
    ts(col(4), G16, 0.25, 3.0, ALU.mult, ALU.add, ["cf"], ["cf4"])
    ts(col(5), G16, 0.5, H_, ALU.mult, ALU.add, ["cf"], ["cf5"])
    ts(col(6), G16, 0.5, K_, ALU.mult, ALU.add, ["cf"], ["cf6"])
    ts(col(7), K_, 8.0, -1.0, ALU.is_lt, ALU.mult, ["cf"], ["cf7"])
    for r_ in range(M):
        ts(col(8 + r_), K_, H_, 2.0 * r_, ALU.subtract, ALU.is_equal, ["cf"], ["mask"])

    def onto(k):
        return T.zt[:, k % 2, 16 - k + k % 2:144 - k + k % 2]
    dmk = ["zs", "zu"]
    ts(T.zt[:, 0, 16:144], T.ci[:], G16, None, ALU.is_equal, None, ["ci", "cf", "zt"], ["zs"])
    ts(T.zt[:, 1, 17:145], T.ci[:], G16, None, ALU.is_equal, None, ["ci", "cf", "zt"], ["zu"])
    ts(T.pti[:, 0::2, :], T.nbi[:], 4032, None, ALU.bitwise_and, None, ["nbi"], ["pti0"])
    ts(T.pti[:, 1::2, :], T.nbi[:], 63, None, ALU.bitwise_and, None, ["nbi"], ["pti1"])
    wide_keys = ["%s%d_%d" % (a, h, j) for a in ("cg", "nr") for h in range(2) for j in range(M)]
    for h in range(2):
        cp(T.ptb[:, h], T.pti[:, :, h * HL:(h + 1) * HL], ["pti0", "pti1"], ["ptb%d" % h])
        zk = ["z%d_%d" % (h, k) for k in range(16)]
        for k in range(16):
            out = T.wide[:, h * 2560 + k:(h + 1) * 2560:16]
            if k % 3 == 0:
                act(out, T.ptb[:, h], AF.Copy, ["ptb%d" % h, "km"], [zk[k]], scale=T.km[:, k:k + 1])
            else:
                ts(out, T.ptb[:, h], T.km[:, k:k + 1], None, ALU.mult, None, ["ptb%d" % h, "km"], [zk[k]], c=100)
        mms([(at("rows%d" % h), onto(r_), T.wide[:, h * 2560 + r_ * HF:h * 2560 + (r_ + 1) * HF], r_ == 0, r_ == 7) for r_ in range(8)],
            zk + wide_keys + dmk, [bk("rows%d" % h), "rows%d" % h])
        act(direct("nt0", h * HF, HF), at("rows%d" % h), AF.Copy, ["rows%d" % h], [bk("rows%d" % h)] + span("nt0", h * HF, HF))
        send()
    for b in range(2):
        src = T.nbi[:, :, b * HL:(b + 1) * HL]
        cp(T.un[:, b], src, ["nbi"], span("un%d" % b, 0, HF))
        cp(T.nd[:, b, 0:4], src, ["nbi"], span("nd%d" % b, 0, HF))
        act(T.nd[:, b, 4:7], T.nd[:, b, 0:3], AF.Copy, span("nd%d" % b, 0, HF), span("ndd%d" % b, 0, HF))
    ts(T.own[:], T.own[:], G16, None, ALU.subtract, None, ["own", "cf"], ["own"])
    ts(T.idb[:], T.ci[:], P_, None, ALU.is_equal, None, ["ci", "cf"], ["idb"])
    for m, v in (("far", 8192.0), ("off", -16.0), ("idf", 1.0)):
        act(T[m][:], T.idb[:], AF.Copy, ["idb"], [m], scale=v)
    ts(T.b8[:], T.cm[:], K_, 0.125, ALU.is_equal, ALU.mult, ["cm", "cf"], ["b8"])
    ts(T.gcf[:], T.ch[:], col(4), None, ALU.is_equal, None, ["ch", "cf4"], ["gcf"])
    ts(T.gdf[:], T.ci[:, 0:72], col(5), 6.0, ALU.subtract, ALU.is_equal, ["ci", "cf5"], ["gdf"])
    ts(T.gn[:], T.ci[:, 0:64], col(6), col(7), ALU.is_equal, ALU.mult, ["ci", "cf6", "cf7"], ["gn"])
    tt(T.amb[:], T.idb[:], T.b8[:], ALU.subtract, ["idb", "b8"], ["amb"], c=270)
    act(T.amf[:], T.amb[:], AF.Copy, ["amb"], ["amf"])
    made = ["idb", "idf"]

    def offs(b, c0, n, j):
        return T.un[:, b, j * HL + c0 // 16:j * HL + (c0 + n) // 16]

    def sums(t, out, w, terms):
        for i, (v, ap, keys) in enumerate(terms):
            m = {1: "id", -1: "neg", 2: "two"}[v] + kind(t)
            if m not in made:
                made.append(m)
                act(T[m][:], T.idb[:], AF.Copy, ["idb"], [m], scale=float(v))
            mm(out, T[m][:], ap, i == 0, i == len(terms) - 1, [m] + keys, w, wide=t >= 2)

    def pair(t, b, off, okeys, way, out, w):
        tab = "xt%d" % t
        if way is None:
            tt(out, T[tab][:].indirect(off), T["xo%d" % t][:, b], ALU.subtract,
               whole(tab) + okeys + span("xo%da" % t, b * HF, HF) + span("xo%db" % t, b * HF, HF), w, c=gcost(F))
        else:
            act(out, T[tab][:].indirect(off), AF.Copy, whole(tab) + okeys, w, c=gcost(F))

    def gather(t, b, c0, n, off, okeys, way, held, hk, out, w):
        tab, c = "xt%d" % t, b * HF + c0
        if way is None:
            if off is not None:
                tt(out, T[tab][:].indirect(off), T["xo%d" % t][:, b, c0:c0 + n], ALU.subtract, whole(tab) + okeys + span("xo%da" % t, c, n), w, c=gcost(n))
            return
        if off is not None:
            act(held, T[tab][:].indirect(off), AF.Copy, whole(tab) + okeys, hk, c=gcost(n))
        if way == "p":
            sums(t, out, w, [(-1, direct(tab, c, n), span(tab, c, n)), (1, held, hk)])
        else:
            tt(out, held, at("xf%d" % b, c0, n), ALU.subtract, hk + ["xf%d" % b], [bk("xf%d" % b)] + w)

    def first(t, b, c0, n, sign):
        u = [i for i, x in enumerate(UNITS_A) if x[0] == b and x[1] <= c0 < x[1] + x[2]][0]
        tab, c = "xt%d" % t, b * HF + c0
        d = [(sign, T["dv" + kind(t)][:, b, HF + c0:HF + c0 + n], span("dv%d_1" % b, c0, n))]
        return d + ([(-sign, direct(tab, c, n), span(tab, c, n))] if (SIDE_V if u else SIDE_F)[t].get(1) == "p" else [])

    def medians(t, u):
        b, c0, n = UNITS_A[u]
        s, cc, tab, k = u, b * HF + c0, "xt%d" % t, kind(t)
        a, c = "pa%d" % s, "pc%d" % s
        pa, pc, ba, bc = at(a, 0, n), at(c, 0, n), bk(a), bk(c)
        tm = [T.tmp[:, s, i, 0:n] for i in range(4)]
        tk = ["tm%d_%d" % (s, i) for i in range(4)]
        up, uk = T["up" + k][:, b, c0:c0 + n], span("up%d" % b, c0, n)
        nx, nw = at("nx%d" % b, c0, n), [bk("nx%d" % b), "nx%d" % b]
        if t < R - 1:
            mm(nx, T.b8[0:16, :], T.mixs[0:16, cc:cc + n], True, False, ["b8", "mix"], nw)
            mm(nx, T["am" + k][:], direct(tab, cc, n), False, False, ["am" + k] + span(tab, cc, n), nw, wide=t >= 2)
        d, dk = [], []
        for j in range(M):
            way = (SIDE_V if u else SIDE_F)[t].get(j)
            held, hk = T["dv" + k][:, b, j * HF + c0:j * HF + c0 + n], span("dv%d_%d" % (b, j), c0, n)
            two = n == HF and j in (1, 2) and "V" in PAIRS
            if two and j == 1:
                both, bk_ = T["dv" + k][:, b, HF:3 * HF], span("dv%d_2" % b, 0, HF) + hk
                pair(t, b, offs(b, 0, F, 1), span("un%d" % b, 0, HF), None, both, bk_)
                act(T["adv" + k][:, b, HF:3 * HF], both, AF.Abs, bk_, span("adv%d_2" % b, 0, HF) + span("adv%d_1" % b, 0, HF))
            ap, key, bank_ = held, hk, []
            if way and j == 0:
                ap, key, bank_ = pc, [c], [bc]
            elif way == "p":
                ap, key, bank_ = pa, [a], [ba]
            gather(t, b, c0, n, None if two else offs(b, c0, n, j), span("un%d" % b, c0, n), way, held, hk, ap, bank_ + key)
            if not two and (j != 1 or SIZE[t] == "a"):
                act(T["adv" + k][:, b, j * HF + c0:j * HF + c0 + n], ap, AF.Abs, key, bank_ + span("adv%d_%d" % (b, j), c0, n))
            d.append(ap)
            dk.append(key)
            if j == 0 and not way:
                if COPY[t] == "a":
                    act(pc, ap, AF.Copy, key, [bc, c])
                else:
                    sums(t, pc, [bc, c], [(1, ap, key)])
            if j == 1:
                act(up, ap, AF.Relu, key, bank_ + uk)
                if LOW[t] == "a":
                    act(tm[3], ap, AF.Relu, key, bank_ + [tk[3]], scale=-1.0)
                    act(pa, tm[3], AF.Copy, [tk[3]], [ba, a], scale=-1.0)
                elif LOW[t] == "v":
                    ts(pa, ap, 0.0, None, ALU.min, None, key, [ba, a])
                else:
                    sums(t, pa, [ba, a], first(t, b, c0, n, 1) + [(-1, up, uk)])
        tt(tm[0], pc, d[2], ALU.min, [c] + dk[2], [bc, tk[0]])
        tt(pc, pc, d[2], ALU.max, [c] + dk[2], [bc, c])
        tt(pa, pa, tm[0], ALU.max, [a, tk[0]], [ba, a])
        tt(tm[1], pc, up, ALU.min, [c] + uk, [bc, tk[1]])
        tt(pc, pa, tm[1], ALU.max, [a, tk[1]], [ba, bc, c])
        tt(pa, pa, tm[1], ALU.min, [a, tk[1]], [ba, a])
        tt(tm[2], pc, d[3], ALU.min, [c] + dk[3], [bc, tk[2]])
        mo, mk = T["mo" + k][:, cc:cc + n], span("mo", cc, n)
        if t < R - 1:
            tt(mo, pa, tm[2], ALU.max, [a, tk[2]], [ba] + mk)
            nxt = "xt%d" % (t + 1)
            mm(nx, T["am" + k][:], mo, False, True, ["am" + k] + mk, nw, wide=t >= 2)
            act(direct(nxt, cc, n), nx, AF.Relu, nw[1:], nw[:1] + span(nxt, cc, n))
            send()
            for h in range(2):
                load("s", T["xo%d" % (t + 1)][:, b, h * HF + c0:h * HF + c0 + n], direct(nxt, cc, n), span("xo%d%s" % (t + 1, "ab"[h]), cc, n),
                     "xo%d" % (t + 1), r=span(nxt, cc, n))
        else:
            tt(pa, pa, tm[2], ALU.max, [a, tk[2]], [ba, a])
            tt(mo, pa, direct(tab, cc, n), ALU.add, [a] + span(tab, cc, n), [ba] + mk)
            act(T.yes[:, cc:cc + n], mo, AF.Square, mk, span("yes", cc, n))
            out = at(c, 0, n, slice(0, 16))
            mm(out, T.km[:], T.yes[:, cc:cc + n], True, True, ["km"] + span("yes", cc, n), [bc, c], wide=True)
            act(T.yds[0:16, cc:cc + n], out, AF.Copy, [c], [bc] + span("yds", cc, n))

    def unit_b(u):
        b, c0, n = UNITS_B[u]
        return b, c0, n, u % 2, n // 16, n // 4, [(o, min(128, o0 + n0 - o)) for o0, n0 in PARTS[u] for o in range(o0, o0 + n0, 128)]

    def tolist(out, o, n, keys, w, start=True, stop=True):
        for k0 in range(0, 16, 4):
            mms([(out, onto(k), T.wide[:, o + k:o + 4 * n:16], start and k == 0, stop and k == 15) for k in range(k0, k0 + 4)], keys + dmk, w)

    def challengers(t, u):
        b, c0, n, s, na, L, tiles = unit_b(u)
        tab, a0 = "nt%d" % t, c0 // 16
        for j in range(M):
            c = s * 1280 + j * n
            out, src, keep = T.wide[:, c:c + n], T[tab][:].indirect(offs(b, c0, n, j)), col(8 + (j + t) % M)
            r, w = whole(tab) + span("un%d" % b, c0, n) + ["mask"], ["cg%d_%d" % (s, j)]
            if j in SHARED[t][u]:
                ts(out, src, keep, None, ALU.mult, None, r, w, c=gcost(n))
            else:
                act(out, src, AF.Copy, r, w, scale=keep, c=gcost(n))
        cl, pt = "cl%d" % s, "pt%d" % s
        pc_, cs, bl = at(cl, 0, L), T.cs[:, s * 80:s * 80 + L], bk(cl)
        tolist(pc_, s * 1280, n, ["cg%d_%d" % (s, j) for j in range(M)], [bl, cl])
        if LIST[u] == "a":
            act(cs, pc_, AF.Copy, [cl], [bl, "cs%d" % s])
        else:
            cp(cs, pc_, [cl], [bl, "cs%d" % s])
        nk = span("nd%d" % b, c0, n)
        tt(T.eq[:, s, 0, 0:L], pc_, T.own[:, b, :, a0:a0 + na], ALU.is_equal, [cl, "own"], [bl, "eq%d_0" % s])
        for i in range(1, M):
            tt(T.eq[:, s, i, 0:L], pc_, T.nd[:, b, i:i + 4, a0:a0 + na], ALU.is_equal, [cl] + nk + span("ndd%d" % b, c0, n), [bl, "eq%d_%d" % (s, i)])
        for i in range(1, M):
            tt(T.eq[:, s, 3 + i, i * na:L], at(cl, i * na, L - i * na), T.cs[:, s * 80:s * 80 + L - i * na], ALU.is_equal,
               [cl, "cs%d" % s], [bl, "eq%d_%d" % (s, 3 + i)])
        if t < R - 1:
            bv = "bv%d" % s
            mm(at(bv, 0, L), T.idf[:], cs, True, False, ["idf", "cs%d" % s], [bk(bv), bv], wide=True)
            for part in ((0, 1, 2, 3), (4, 5, 6)):
                mms([(at(bv, max(0, i - 3) * na, L - max(0, i - 3) * na), T.far[:], T.eq[:, s, i, max(0, i - 3) * na:L], False, i == 6) for i in part],
                    ["far"] + ["eq%d_%d" % (s, i) for i in part], [bk(bv), bv])
            ts(T.uc[:, s * 80:s * 80 + L], at(bv, 0, L), float(W), None, ALU.min, None, [bv], [bk(bv), "uc%d" % s])
        else:
            cp(T.uc[:, s * 80:s * 80 + L], pc_, [cl], [bl, "uc%d" % s])
        tt(at(pt, 0, L), pc_, T.nd[:, b, 0:4, a0:a0 + na], ALU.subtract, [cl] + nk, [bl, bk(pt), pt])

    def wins(out, src, r, w):
        act(out, src, AF.Sigmoid, r, w, bias=-2176.0, scale=256.0)

    def challenge(t, u):
        b, c0, n, s, na, L, tiles = unit_b(u)
        a0, cc, k = c0 // 16, b * HF + c0, kind(t)
        tab, nxt = "nt%d" % t, "nt%d" % (t + 1)
        cf, df, b2, bc, pt = ["%s%d" % (x, s) for x in ("cf", "df", "b2", "bc", "pt")]
        more = t < R - 1
        if more:
            for i, (o, m) in enumerate(tiles):
                out = at(df, i * 64, 64, slice(0, m))
                c = s * 1280 + o
                mms([(out, direct(tab, cc + o, m), T.gn[:], True, False)]
                    + [(out, T.wide[:, c + j * n:c + j * n + m], T.gdf[:, 6 - 2 * j:70 - 2 * j], False, j == M - 1) for j in range(M)],
                    span(tab, cc + o, m) + ["gn", "gdf"] + ["cg%d_%d" % (s, j) for j in range(M)], [bk(df), df])
        for o0, n0 in (PARTS[u] if more else [(0, n)]):
            some = [(i, o, m) for i, (o, m) in enumerate(tiles) if o0 <= o < o0 + n0]
            w0, wd, tk = 64 * some[0][0], 64 * len(some), "%d_%d" % (s, some[0][0])
            if more:
                mm(at(b2, o0, n0), T.idb[:], direct(tab, cc + o0, n0), True, False, ["idb"] + span(tab, cc + o0, n0), [bk(b2), b2])
                mm(at(cf, w0, wd), T.idb[:], T.zb[:, 0:wd], True, False, ["idb", "zb", "zc"], [bk(cf), cf])
            for j in range(M):
                way = SIDE_U[t][u].get(j)
                ak = AU[u][j]
                au, ab = at(ak, 0, n0), bk(ak)
                a1 = s * 80 + j * na + o0 // 16
                off, du, dk = T.uc[:, a1:a1 + n0 // 16], T["du" + k][:, s, j * HF + o0:j * HF + o0 + n0], span("du%d_%d" % (s, j), o0, n0)
                if n0 == HF and way == SIDE_U[t][u].get(j ^ 1) and ("U" if way is None else "S") in PAIRS:
                    if j % 2 == 0:
                        pair(t, b, T.uc[:, a1:a1 + 2 * na], ["uc%d" % s], way, T["du" + k][:, s, j * HF:(j + 2) * HF],
                             span("du%d_%d" % (s, j + 1), 0, HF) + dk)
                    off = None
                c = 2560 + s * 1280 + j * n
                nr, nrk = T.wide[:, c + o0:c + o0 + n0], "nr%d_%d" % (s, j)
                if way == "p":
                    gather(t, b, c0 + o0, n0, off, ["uc%d" % s], way, du, dk, au, [ab, ak])
                    act(au, au, AF.Abs, [ak], [ab, ak])
                else:
                    gather(t, b, c0 + o0, n0, off, ["uc%d" % s], way, du, dk, du, dk)
                if j == 1 and SIZE[t] == "p":
                    act(du, du, AF.Abs, dk, dk)
                    for b_, o, m in UNITS_A:
                        lo, hi = max(o, c0 + o0), min(o + m, c0 + o0 + n0)
                        if b_ == b and lo < hi:
                            sums(t, at(ak, lo - c0 - o0, hi - lo), [ab, ak],
                                 [(2, T["up" + k][:, b, lo:hi], span("up%d" % b, lo, hi - lo))] + first(t, b, lo, hi - lo, -1))
                    tt(nr, au, du, ALU.is_gt, [ak] + dk, [ab, nrk])
                else:
                    if way != "p":
                        act(au, du, AF.Abs, dk, [ab, ak])
                    tt(nr, au, T["adv" + k][:, b, j * HF + c0 + o0:j * HF + c0 + o0 + n0], ALU.is_lt, [ak] + span("adv%d_%d" % (b, j), c0 + o0, n0), [ab, nrk])
                if more:
                    mms([(at(cf, i * 64, 64, slice(0, m)), T.wide[:, c + o:c + o + m], T.gcf[:, 6 - 2 * j:70 - 2 * j], False,
                          j == M - 1 and i == some[0][0]) for i, o, m in some[::-1]], [nrk, "gcf"], [bk(cf), cf])
            if more:
                wf, tf = T.wf[:, s, w0:w0 + wd], T.tf[:, s * 24 + w0 // 8:s * 24 + (w0 + wd) // 8, 0:8]
                wins(wf, at(cf, w0, wd), [cf], [bk(cf), "wf" + tk])
                tt(tf, at(df, w0, wd), wf, ALU.mult, [df, "wf" + tk, "tf"], [bk(df), "tf" + tk])
                mms([(at(b2, o, m), T.tf[0:m, s * 24 + 8 * i:s * 24 + 8 * i + 8, :], T.idb[0:m, 0:m], False, i == some[-1][0]) for i, o, m in some],
                    ["tf" + tk, "idb"], [bk(b2), b2])
                act(direct(nxt, cc + o0, n0), at(b2, o0, n0), AF.Copy, [b2], [bk(b2)] + span(nxt, cc + o0, n0))
                send()
        if not more:
            mms([(at(bc, max(0, i - 3) * na, L - max(0, i - 3) * na), T.off[:], T.eq[:, s, i, max(0, i - 3) * na:L], i == 0, False) for i in range(7)],
                ["off"] + ["eq%d_%d" % (s, i) for i in range(7)], [bk(bc), bc])
        tolist(at(bc, 0, L), 2560 + s * 1280, n, ["nr%d_%d" % (s, j) for j in range(M)], [bk(bc), bc], more)
        wl, pt_, nd = T.wl[:, s * 80:s * 80 + L], at(pt, 0, L), T.nd[:, b, 0:4, a0:a0 + na]
        nk = span("nd%d" % b, c0, n)
        wins(wl, at(bc, 0, L), [bc], [bk(bc), "wl%d" % s])
        tt(pt_, pt_, wl, ALU.mult, [pt, "wl%d" % s], [bk(pt), pt])
        if more:
            tt(nd, pt_, nd, ALU.add, [pt] + nk, [bk(pt)] + nk)
            cp(T.un[:, b], nd, nk, span("un%d" % b, c0, n))
            act(T.nd[:, b, 4:7, a0:a0 + na], T.nd[:, b, 0:3, a0:a0 + na], AF.Copy, nk, span("ndd%d" % b, c0, n))
        else:
            tt(T.yns[:, :, b * HL + a0:b * HL + a0 + na], pt_, nd, ALU.add, [pt] + nk, [bk(pt)] + span("yns", cc, n))

    for t in range(R):
        if "s" in list(SIDE_V[t].values()) + list(SIDE_F[t].values()) + [x for ways in SIDE_U[t] for x in ways.values()]:
            for b in range(2):
                act(at("xf%d" % b), direct("xt%d" % t, b * HF, HF), AF.Copy, span("xt%d" % t, b * HF, HF), [bk("xf%d" % b), "xf%d" % b])
        for u in range(len(UNITS_A)):
            medians(t, u)
        if t == R - 1:
            load("s", T.ye[:], T.yes[:], [], "sto", r=span("yes", 0, F))
            load("s", T.yd[:], T.yds[0:16, :], [], "sto", r=span("yds", 0, F))
        challengers(t, 0)
        for u in range(len(UNITS_B)):
            if u + 1 < len(UNITS_B):
                challengers(t, u + 1)
            challenge(t, u)
    load("s", T.yn[:], T.yns[:], [], "sto", r=span("yns", 0, F))
    finish([("sent", sent[0])])
